import numpy as np, ml_dtypes
CORES = [23,119,17,113]
N = 4
BF = ml_dtypes.bfloat16
def gentries(a):
    return np.ascontiguousarray(a.reshape(8, 16, -1).transpose(0, 2, 1)).reshape(8, -1)
def gtable(e):
    e = np.asarray(e); return np.ascontiguousarray(e.reshape(8, -1, 16).transpose(0, 2, 1)).reshape(128, -1).astype(np.int32)
V, H, K, P, D, ST, E, TH, CL = 768, 128, 4, 3, 4, 6, 3, 9, 2
M = V + 2 * H
KV = K * V
def parts(rng):
    src = np.argsort(rng.random((N, 8, KV)), axis=-1); snd = np.argsort(rng.random((N, 8, V)), axis=-1)[..., :2 * H]
    dl = rng.integers(1, D + 1, (N, 8, KV)); wi = rng.integers(0, 65, (N, 8, 16, KV))
    dr = np.clip(rng.integers(-32, 81, (N, 8, 1, V)) + rng.integers(-32, 33, (N, 8, 16, V)), -128, 128)
    lo = 0.125 + 0.875 * rng.random((N, 8, 16, V))
    return wi, dr, lo, src, dl, np.ascontiguousarray(snd)
def pack(wi, dr, lo, src, dl, snd):
    return {"w": (wi * 0.015625).reshape(N, 128, KV).astype(BF), "src": np.stack([gtable(a) for a in src]), "dly": np.stack([gtable(a) for a in dl]),
            "snd": np.stack([gtable(a) for a in snd]), "drive": (dr * 0.015625).reshape(N, 128, V).astype(BF), "loss": lo.reshape(N, 128, V).astype(BF)}
def put(row, slots, ports):
    for s, p in zip(slots, ports):
        a = int(np.flatnonzero(row == p)[0]); row[a], row[s] = row[s], row[a]
def setup_inputs(rng):
    return pack(*parts(rng))
def setup_inputs_spread(rng):
    wi, dr, lo, src, dl, snd = parts(rng)
    wi = np.rint(wi * np.exp2(-1.0 * rng.integers(0, 3, (N, 8, 1, KV)))).astype(np.int64)
    dr = np.clip(rng.integers(-64, 113, (N, 8, 1, V)) + rng.integers(-24, 25, (N, 8, 16, V)), -128, 128)
    lo = (0.25 + 0.75 * rng.random(lo.shape)) * np.exp2(1.0 * rng.integers(-1, 2, (N, 8, 1, V)))
    return pack(wi, dr, lo, src, dl, snd)
def setup_inputs_ends(rng):
    wi, dr, lo, src, dl, snd = parts(rng)
    kind = rng.integers(0, 8, (N, 8, V)); kind[..., :4] = 0; kind[..., V - 4:] = 0; kind[..., V // 2] = 2
    kk = kind[:, :, None, :]; wk = np.tile(kk, (1, 1, 1, K)); pm = np.where(rng.random(wi.shape) < 0.5, 0, 64)
    wi = np.where((wk < 2) | (wk == 5), 64, np.where(wk == 2, 0, np.where(wk < 5, pm, wi)))
    dr = np.where((kk < 2) | (kk == 3) | (kk == 4), 128, np.where((kk == 2) | (kk == 5), -128, dr))
    lo = np.where(rng.random(lo.shape) < 0.85, np.where(rng.random(lo.shape) < 0.4, 2.0, 0.125), lo)
    dl = np.where(rng.random(dl.shape) < 0.5, 1, D)
    low = np.concatenate([np.arange(H), np.arange(V - H, V)]); snd = low[np.argsort(rng.random(snd.shape), axis=-1)]
    on = [0, V - 1, 1, V - 2][:K]; last = [k * V + V - 1 for k in range(K)]; mid = [k * V + V // 2 for k in range(K)]
    on2 = [2, V - 3, 3, V - 4][:K]; near = [k * V + V // 4 for k in range(K)]
    for q in range(N):
        for g in range(8):
            put(src[q, g], last, on); put(src[q, g], mid, [c + M for c in on]); dl[q, g, last] = 1; dl[q, g, mid] = 1
            put(src[q, g], near, on2); dl[q, g, near] = 1
            dd = np.where(rng.random(16) < 0.5, -128, rng.integers(-127, -64, 16)); dd[15] = -128; dr[q, g, :, V // 4] = dd
            for k in range(K): wi[q, g, :, near[k]] = (63 - dd + k) // K
    return pack(wi, dr, lo, src, dl, snd)
def setup_inputs_corners(rng):
    wi, dr, lo, src, dl, snd = parts(rng)
    for q in range(N):
        for g in range(8):
            c = (g + q) % 8
            if c == 0: src[q, g] = np.arange(KV); dr[q, g, :, 0] = 128; dr[q, g, :, V - 1] = 128
            if c == 1: src[q, g] = np.arange(KV)[::-1]; dl[q, g] = np.where(np.arange(KV) % 2 == 0, 1, D)
            if c == 2: dl[q, g] = 1
            if c == 3: dl[q, g] = D
            if c == 4: wi[q, g] = 0; dr[q, g] = rng.choice(np.array([32, 36, 40, 44, 48, 64, 80]), (16, V))
            if c == 5: dr[q, g] = 128
            if c == 6:
                half = rng.random((1, V)) < 0.5; dr[q, g] = np.where(half, -128, np.minimum(dr[q, g] + 48, 128)); wi[q, g] = np.minimum(wi[q, g], np.where(np.tile(half, (1, K)), 32, 16))
            if c == 7:
                place = rng.permutation(16)[:, None]; m = np.where(rng.random((1, V)) < 0.5, TH, TH - 1)
                dr[q, g] = np.where(place < m, 128, -64); wi[q, g] = np.minimum(wi[q, g], 16); src[q, g] = np.roll(np.arange(KV), 1)
                snd[q, g] = np.arange(2 * H) if q % 2 == 0 else V - 1 - np.arange(2 * H)
    return pack(wi, dr, lo, src, dl, snd)
def setup_inputs_calm(rng):
    wi, dr, lo, src, dl, snd = parts(rng)
    place = rng.permutation(16)[:, None]; wi = np.rint(wi * 0.25).astype(np.int64)
    m = rng.choice(np.array([7, 8, 8, 9, 9, 10, 16]), (N, 8, 1, V)); m[:, 1::2] = rng.choice(np.array([0, 1, 2, 3, 16, 16]), (N, 4, 1, V))
    for q, g in ((0, 0), (N - 1, 7)):
        a, b, c = (q - 1) % N, (g - 1) % 8, (q + 1) % N
        m[q, g] = 16; m[a, b, 0, snd[a, b, :H]] = 16; m[c, g, 0, snd[c, g, H:]] = 16
    lo = np.where(rng.random(lo.shape) < 0.125, 0.125, 0.125 + 0.125 * rng.random(lo.shape))
    return pack(wi, np.where(place < m, 128, -64), lo, src, dl, snd)
def check_ranges(d):
    bad = []
    for k, lo, hi in (("w", 0, 1), ("drive", -2, 2), ("loss", 0.125, 2), ("src", 0, KV - 1), ("dly", 1, D), ("snd", 0, V - 1)):
        a = np.asarray(d[k], np.float64)
        if not (np.min(a) >= lo and np.max(a) <= hi): bad.append("range of " + k)
    for k in ("w", "drive"):
        a = np.asarray(d[k], np.float64) * 64
        if not np.all(a == np.rint(a)): bad.append("steps of " + k)
    if any(np.any(np.sort(gentries(a), axis=1) != np.arange(KV)) for a in d["src"]): bad.append("src is no permutation")
    if any(np.any(np.diff(np.sort(gentries(a), axis=1), axis=1) == 0) for a in d["snd"]): bad.append("snd repeats a neuron")
    return bad
def turned(a, n):
    return np.ascontiguousarray(np.asarray(a, np.float64).reshape(N, 8, 16, n).transpose(0, 1, 3, 2))
def rows(a, n):
    return np.ascontiguousarray(a.transpose(0, 1, 3, 2)).reshape(N, 128, n).astype(np.float32)
def reference(w, src, dly, snd, drive, loss):
    wt = turned(w, KV); dr = turned(drive, V); ls = turned(loss, V)
    port = np.stack([gentries(a) for a in src]).astype(np.int64); dl = np.stack([gentries(a) for a in dly]).astype(np.int64); sn = np.stack([gentries(a) for a in snd]).astype(np.int64)
    units = [(q, g) for q in range(N) for g in range(8)]; slot = np.arange(KV)
    gam = np.zeros((N, 8, KV, 16)); cnt = np.zeros((N, 8, V, 16))
    for e in range(E):
        ix = (D - dl) * M + port % M
        inv = np.argsort(port, axis=-1)
        jx = np.take_along_axis((dl - 1) * V + slot % V, inv, axis=-1)
        wp = np.take_along_axis(wt, inv[..., None], axis=2)
        spk = np.zeros((N, 8, ST + D, M, 16), np.float32)
        slope = np.zeros((N, 8, ST, V, 16), np.float32); u = np.zeros((N, 8, V, 16)); gain = np.zeros((N, 8, KV, 16), np.float32)
        for t in range(ST):
            for q, g in units:
                x = spk[q, g, t:t + D].reshape(D * M, 16)[ix[q, g]]
                cur = dr[q, g] + np.add.reduce((wt[q, g] * x).reshape(K, V, 16), axis=0)
                v = 0.5 * u[q, g] + cur; s = (v >= 1).astype(np.float32)
                u[q, g] = np.where(v >= 1, 0.0, v); spk[q, g, t + D, :V] = s; cnt[q, g] += s
                slope[q, g, t] = np.where(cur < 0.75, 2.0, np.where(cur < 1.25, 1.0, 0.5))
                gain[q, g] += (x.reshape(K, V, 16) * (2 * s - 1)).reshape(KV, 16)
            for q, g in units:
                spk[(q + 1) % N, (g + 1) % 8, t + D, V:V + H] = spk[q, g, t + D, sn[q, g, :H]]
                spk[(q - 1) % N, g, t + D, V + H:] = spk[q, g, t + D, sn[q, g, H:]]
        lam = np.zeros((N, 8, ST + D, V, 16)); part = np.zeros((N, 8, M, 16))
        for t in range(ST - 1, -1, -1):
            for q, g in units:
                z = wp[q, g] * lam[q, g, t + 1:t + 1 + D].reshape(D * V, 16)[jx[q, g]]
                part[q, g] = np.add.reduce(z.reshape(P, M, 16), axis=0)
            for q, g in units:
                j = part[q, g, :V] + ls[q, g]
                j[sn[q, g, :H]] += part[(q + 1) % N, (g + 1) % 8, V:V + H]; j[sn[q, g, H:]] += part[(q - 1) % N, g, V + H:]
                s = spk[q, g, t + D, :V]
                y = np.minimum((1 - s) * (0.5 * lam[q, g, t + 1]) + s * (slope[q, g, t] * j), CL); lam[q, g, t] = y
                x = spk[q, g, t:t + D].reshape(D * M, 16)[ix[q, g]]
                gam[q, g] += (x.reshape(K, V, 16) * y).reshape(KV, 16)
        if e < E - 1:
            eager = np.add.reduce((gain > 0).astype(np.int64), axis=3) >= TH
            mate = slot ^ (1 << e)
            port = np.where(eager & eager[..., mate], port[..., mate], port)
    return {"lam": rows(lam[:, :, 0], V), "gam": rows(gam, KV), "cnt": rows(cnt, V)}

def check_inputs(d):
    bad = list(check_ranges(d))
    if not bad:
        for name, y in reference(**d).items():
            for q in range(N):
                v = np.abs(np.asarray(y[q], np.float64)); s = np.sqrt(np.mean(v * v))
                if v.max() > 13 * s or s < 2.0 ** -5: bad.append('%s of rank %d is uneven or too small' % (name, q))
    return bad

@@ -1,0 +1,658 @@
+import math
+import numpy as np
+from concourse.bass import DstId, RemoteDMATransfer
+from concourse.mybir import AluOpType as A, ActivationFunctionType as F
+
+V, H, K, M, KV, L = 768, 128, 4, 1024, 3072, 192
+E = 3
+TINY = 2.0 ** -30
+NWX = 6
+ES = True
+ZP = False
+f32, bf, i32, u16 = "float32", "bfloat16", "int32", "uint16"
+
+SCRATCH = {
+    "wq": ("sbuf", [128, KV], bf),
+    "wx": ("sbuf", [128, NWX * KV], bf),
+    "mlog": ("sbuf", [128, 5 * KV + 8], f32),
+    "z": ("sbuf", [128, KV], f32),
+    "retg": ("sbuf", [128, V], f32),
+    "acc": ("sbuf", [128, KV], f32),
+    "log0": ("sbuf", [128, 8 * M + V], bf),
+    "log1": ("sbuf", [128, 8 * M + V], bf),
+    "fa": ("sbuf", [128, NWX * V], bf),
+    "f0": ("sbuf", [128, V], bf),
+    "xw": ("sbuf", [128, 4 * M], f32),
+    "pint": ("sbuf", [128, 5 * L], i32),
+    "pv": ("sbuf", [128, 2 * V], f32),
+    "zz": ("sbuf", [128, V], f32),
+    "hz0": ("sbuf", [128, V], bf),
+    "rr": ("sbuf", [128, V], bf),
+    "cap": ("sbuf", [128, V], f32),
+    "dm": ("sbuf", [128, V], bf),
+    "ls": ("sbuf", [128, V], bf),
+    "ones": ("sbuf", [128, V], bf),
+    "cn": ("sbuf", [128, V], bf),
+    "ret": ("sbuf", [128, 2 * 264], f32),
+    "sf": ("sbuf", [128, 2 * 384], bf),
+    "sb": ("sbuf", [128, 2 * 256], f32),
+    "id2": ("sbuf", [128, 256], bf),
+    "id2f": ("sbuf", [128, 256], f32),
+    "pw": ("sbuf", [128, 7 * 128], bf),
+    "xm": ("sbuf", [128, 4 * 128], f32),
+    "fm": ("sbuf", [128, 144], bf),
+    "bg": ("sbuf", [128, 16], bf),
+    "sndi": ("sbuf", [128, 16], i32),
+    "pcol": ("sbuf", [128, 8], i32),
+    "pcf": ("sbuf", [128, 4], f32),
+    "cf": ("sbuf", [128, L], f32),
+    "ixf": ("sbuf", [128, L], f32),
+    "val": ("sbuf", [128, 4 * L], f32),
+    "tf": ("sbuf", [128, 2 * L], f32),
+    "eag": ("sbuf", [128, L], f32),
+    "both": ("sbuf", [128, 2 * L], f32),
+    "tmp": ("sbuf", [128, L], f32),
+    "ix": ("sbuf", [128, L], u16),
+    "rho": ("sbuf", [128, L], u16),
+    "linv": ("sbuf", [128, L], u16),
+    "jx": ("sbuf", [128, 5 * L], u16),
+    "snu": ("sbuf", [128, 16], u16),
+    "snp": ("sbuf", [128, 16], u16),
+    "inu": ("sbuf", [128, 48], u16),
+    "psN": ("psum", [128, 1024], f32),
+    "psW": ("psum", [128, 1024], f32),
+    "psP": ("psum", [128, 1024], f32),
+    "psL": ("psum", [128, 1024], f32),
+}
+SEMAPHORES = (["cv", "cs", "cp", "cg"] + ["arr%d" % i for i in range(27)] + ["snt%d" % i for i in range(27)]
+              + ["dq%d" % i for i in range(48)])
+
+ALIAS = {"ti": ("pint", 0, 3 * L), "srci": ("pint", 3 * L, L), "dlyi": ("pint", 4 * L, L), "hz": ("zz", 0, V),
+         "dr": ("dm", 0, V)}
+CH = [(0, 512), (512, V)]
+CY = 0.83e-3 * 1.25
+GA, SC, PE = 1.55, 3.5, 0.42e-3 * 1.25
+COMM = 4.5
+
+
+def plan(T, topo, core):
+    ops = []
+    rank = T.rank_of(core)
+    n = len(T.cores)
+    nxt, prv = T.cores[(rank + 1) % n], T.cores[(rank - 1) % n]
+    en, ep = topo.engines(core, nxt), topo.engines(core, prv)
+    en, ep = en[:len(en) // 2], ep[len(ep) // 2:]
+    mn, mp = sum(1 << e for e in en), sum(1 << e for e in ep)
+    nsig = len(en) + len(ep)
+    dn, dp = DstId(rid=topo.addr(nxt)[0], pnc=topo.addr(nxt)[1]), DstId(rid=topo.addr(prv)[0], pnc=topo.addr(prv)[1])
+    cnts = {"msg": 0, "dq": 0, "tag": "S", "fn": []}
+
+    def R(name, a=None, b=None, step=None):
+        name, off, w = ALIAS.get(name) or (name, 0, T[name].shape[1])
+        t = T[name]
+        a = off + (0 if a is None else a)
+        b = off + (w if b is None else b)
+        ap = t[:, a:b] if step is None else t[:, a:b:step]
+        if name.startswith("ps"):
+            return ap, [(name, k, k + 1, True) for k in range(a // 512, (b - 1) // 512 + 1)], True, b - a
+        return ap, [(name, a, b, False)], False, (b - a if step is None else (b - a + step - 1) // step)
+
+    def add(engs, cost, reads, writes, emit, kind="c", lat=0.0, sem=None, after=()):
+        rd = [r for x in reads for r in x[1]]
+        wr = [r for x in writes for r in x[1]]
+        ops.append({"ex": [r for r in rd if r[3] and r not in wr], "engs": engs, "cost": cost, "rd": rd, "wr": wr,
+                    "emit": emit, "kind": kind, "lat": lat, "sem": sem, "after": list(after), "tag": cnts["tag"]})
+        return len(ops) - 1
+
+    def two(*xs):
+        return all(x[0].dtype != T.acc.dtype and x[0].dtype != T.pint.dtype for x in xs)
+
+    def ts(o, i, s1, s2, op0, op1=None, extra=()):
+        c = 0.06 + max(64, i[3] * (0.5 if two(o, i) else 1)) * CY
+        if op1 is None:
+            return add("v", c, [i] + list(extra), [o], lambda g, e: g.vector.tensor_scalar(o[0], i[0], s1, None, op0))
+        return add("v", c, [i] + list(extra), [o], lambda g, e: g.vector.tensor_scalar(o[0], i[0], s1, s2, op0, op1))
+
+    def tt(o, a, b, op):
+        c = 0.06 + max(64, a[3] * (1 if (a[2] or b[2]) else 2) * (0.5 if two(o, a, b) else 1)) * CY
+        return add("v", c, [a, b], [o], lambda g, e: g.vector.tensor_tensor(o[0], a[0], b[0], op))
+
+    def cp(o, i):
+        c = 0.06 + max(64, i[3] * (0.5 if two(o, i) else 1)) * CY
+        return add("v", c, [i], [o], lambda g, e: g.vector.tensor_copy(o[0], i[0]))
+
+    def act(o, i, func=F.Identity, scale=1.0, bias=0.0):
+        return add("s", 0.07 + max(64, i[3]) * CY, [i], [o],
+                   lambda g, e: g.scalar.activation(o[0], i[0], func, bias=bias, scale=scale))
+
+    def mov(o, i, scale=1.0, engs="sv"):
+        def emit(g, e):
+            if e == "s":
+                return g.scalar.activation(o[0], i[0], F.Identity, bias=0.0, scale=scale)
+            return g.vector.tensor_scalar(o[0], i[0], scale, None, A.mult)
+        return add(engs, 0.07 + max(64, i[3]) * CY, [i], [o], emit)
+
+    def gat(o, win, lst, engs="s"):
+        def emit(g, e):
+            if e == "s":
+                return g.scalar.activation(o[0], win[0].indirect(lst[0]), F.Identity)
+            return g.vector.tensor_copy(o[0], win[0].indirect(lst[0]))
+        return add(engs, 0.07 + o[3] * GA * CY, [win, lst], [o], emit)
+
+    def gmul(o, win, lst, b):
+        return add("v", 0.06 + o[3] * GA * CY, [win, lst, b], [o],
+                   lambda g, e: g.vector.tensor_tensor(o[0], win[0].indirect(lst[0]), b[0], A.mult))
+
+    def scat(win, lst, i):
+        return add("v", 0.06 + i[3] * SC * CY, [lst, i], [win],
+                   lambda g, e: g.vector.tensor_copy(win[0].indirect(lst[0]), i[0]))
+
+    def mset(o, c):
+        return add("v", 0.06 + max(64, o[3] * (0.5 if two(o) else 1)) * CY, [], [o], lambda g, e: g.vector.memset(o[0], c))
+
+    def mm(ps, o0, n, terms, start=True, stop=True):
+        a = o0
+        while a < o0 + n:
+            b = min(o0 + n, (a // 512 + 1) * 512)
+            rd, c, rhs = [], 0.03, []
+            for t in terms:
+                st = t[3] if len(t) > 3 else 1
+                lo = t[2] + (a - o0) * st
+                r = R(t[1], lo, lo + (b - a - 1) * st + 1, None if st == 1 else st)
+                rd += [t[0], r]; rhs.append(r[0])
+                c += (max(64, b - a) * (1 if two(t[0]) else 4) + 16) * PE
+
+            def emit(g, e, a=a, b=b, rhs=rhs):
+                ins = None
+                for j, t in enumerate(terms):
+                    ins = g.tensor.matmul(T[ps][:, a:b], t[0][0], rhs[j], start and j == 0, stop and j == len(terms) - 1)
+                return ins
+            add("p", c, rd, [R(ps, a, b)], emit)
+            a = b
+
+    def dma(q, o, i, reads, writes, nbytes, **kw):
+        s = "dq%d" % cnts["dq"]; cnts["dq"] += 1
+        def emit(g, e):
+            if e == "g":
+                return g.dma_start(o, i, **kw)
+            return (g.sync if e == "y" else g.scalar).dma_start(o, i)
+        f = 2.0 if kw.get("accum_op") is not None else 1.0
+        return add(q, 1.0 if q == "g" else 0.1, reads, writes, emit, "d", 2.0 + f * nbytes / 4700.0, s)
+
+    def send(to_next, land_next, to_prev, land_prev, guard):
+        k = cnts["msg"]; cnts["msg"] += 1
+        def emit(g, e):
+            g.remote_dma_fused([
+                RemoteDMATransfer(dst_ids=[dn], dma_engine_mask=mn, remote_sem=T.sem["arr%d" % k], src=to_next[0], dst=land_next[0]),
+                RemoteDMATransfer(dst_ids=[dp], dma_engine_mask=mp, remote_sem=T.sem["arr%d" % k], src=to_prev[0], dst=land_prev[0]),
+            ], local_sem=T.sem["snt%d" % k])
+            return None
+        s = add("g", 0.5, [to_next, to_prev], [], emit, "r", COMM - 1.0, ("snt%d" % k, nsig))
+        ops[s]["guard"] = [r for x in guard for r in x[1]]
+        add("", 0.0, [], [land_next, land_prev], None, "a", 0.5, ("arr%d" % k, nsig), after=[s])
+
+    def gop(cost, reads, writes, emit):
+        return add("g", cost, reads, writes, emit)
+
+    ID, IDF = R("id2", 0, 128), R("id2f", 0, 128)
+    SHF, SHB = R("id2", 112, 240), R("id2f", 16, 144)
+    PW = [ID] + [R("pw", j * 128, (j + 1) * 128) for j in range(4)]
+    EIGHT, HALF, NEGH = R("pw", 512, 640), R("pw", 640, 768), R("pw", 768, 896)
+    XM = [R("xm", 0, 128), R("xm", 128, 256)]
+    DM = [R("xm", 256, 384), R("xm", 384, 512)]
+    logn = lambda e: "log%d" % (e % 2)
+    blk = lambda t: (t + 3) * M
+
+    def fland(e, t):
+        return R(logn(e), blk(t) + V, blk(t) + V + H), R(logn(e), blk(t) + V + H, blk(t) + M)
+
+    def rland(k):
+        return R("ret", (k % 2) * 264, (k % 2) * 264 + H), R("ret", (k % 2) * 264 + H, (k % 2) * 264 + 2 * H)
+
+    fmsg, bmsg = [0], [0]
+
+    def wires(e, t):
+        o = (fmsg[0] % 2) * 384; fmsg[0] += 1
+        gat(R("sf", o, o + 256), R(logn(e), blk(t), blk(t) + V), R("snu"), "s" if t else "sv")
+        mm("psW", V, H, [(SHF, "sf", o)])
+        mov(R("sf", o + 256, o + 384), R("psW", V, V + H))
+        a, b = fland(e, t)
+        ne, nt = (e, t + 1) if t < 4 else (e + 1, 1)
+        send(R("sf", o + 256, o + 384), a, R("sf", o + H, o + 256), b, list(fland(ne, nt)) if ne < E else [])
+
+    dma("y", T.dm[:], T.drive[:], [], [R("dr")], 1536)
+    dma("a", T.sndi[:], T.snd[:], [], [R("sndi")], 64)
+    dma("y", R("srci")[0], T.src[:], [], [R("srci")], 768)
+    dma("a", R("dlyi")[0], T.dly[:], [], [R("dlyi")], 768)
+    dma("y", T.wq[:], T.w[:], [], [R("wq")], 6144)
+    dma("y", T.ls[:], T.loss[:], [], [R("ls")], 1536)
+    mset(R("ones"), 1.0)
+    gop(0.45, [R("ones")], [ID], lambda g, e: g.affine_select(ID[0], T.ones[:, 0:128], [[-1, 128]], A.is_equal, 0.0, 0, 1))
+    cp(R("id2", 128, 256), ID)
+    cp(R("snu"), R("sndi"))
+    ts(R("log0", blk(0), blk(0) + V), R("dr"), 1.0, None, A.is_ge)
+    wires(0, 0)
+    mset(R("log0", 0, 3 * M), 0.0)
+    ts(R("wq"), R("wq"), TINY, None, A.max)
+    ts(R("ti", 0, L), R("srci"), 1023, None, A.bitwise_and)
+    cp(R("cf"), R("ti", 0, L))
+    ts(R("tmp"), R("dlyi"), -1024.0, 4096.0, A.mult, A.add)
+    tt(R("ixf"), R("tmp"), R("cf"), A.add)
+    cp(R("ix"), R("ixf"))
+    act(R("rr"), R("dr"), F.Identity, -0.5, 0.5)
+    act(R("cn"), R("log0", blk(0), blk(0) + V), F.Identity, 0.5, 0.0)
+    tt(R("hz0"), R("rr"), R("cn"), A.max)
+    act(R("f0"), R("dr"), F.Identity, -2.0, 195.0 - 1.0 / 64)
+    act(R("dm"), R("dr"), F.Identity, 1.0, -0.5)
+    ts(R("f0"), R("f0"), 192.0, 0.5, A.subtract, A.max)
+    act(R("cn"), R("log0", blk(0), blk(0) + V), F.Identity, -8.0, 8.0)
+    tt(R("f0"), R("f0"), R("cn"), A.max)
+    mov(R("id2f"), R("id2"))
+    for j in range(4):
+        mov(PW[j + 1], ID, 16.0 ** (j + 1))
+    NEG = EIGHT
+    mov(EIGHT, ID, 8.0 if ZP else -1.0); mov(HALF, ID, 0.5); mov(NEGH, ID, -0.5)
+    for e in range(2):
+        b = 1 << e
+        for r in range(2 * b):
+            cp(R("xm", e * 128 + r, (e + 1) * 128, 2 * b), R("id2f", r ^ b, 128, 2 * b))
+        tt(DM[e], XM[e], IDF, A.subtract)
+    gop(0.2, [R("ones")], [R("bg", 0, 8)], lambda g, e: g.affine_select(T.bg[:, 0:8], T.ones[:, 0:8], [[-16, 8]], A.is_ge, 0.0, 0, 1))
+    gop(0.2, [R("bg", 0, 8)], [R("bg", 8, 16)], lambda g, e: g.affine_select(T.bg[:, 8:16], T.bg[:, 0:8], [[16, 8]], A.is_ge, 0.0, 15, -1))
+    mset(R("fm"), 0.0)
+    cp(R("fm", 16, 144, 16), R("bg", 8, 16))
+    mset(R("log1", 0, 3 * M), 0.0)
+    mov(R("log1", blk(0), blk(1)), R("log0", blk(0), blk(1)))
+    mset(R("mlog", 5 * KV, 5 * KV + 8), 0.0)
+    mset(R("ret", 256, 264), 0.0); mset(R("ret", 520, 528), 0.0)
+    cnts["tag"] = "I"
+    ts(R("ti", 0, L), R("srci"), 4, 15, A.arith_shift_right, A.bitwise_and)
+    ts(R("ti", L, 2 * L), R("srci"), 15, None, A.bitwise_and)
+    ts(R("ti", 2 * L, 3 * L), R("srci"), 8, None, A.arith_shift_right)
+    ts(R("tmp"), R("ti", 0, L), 192.0, None, A.mult)
+    ts(R("eag"), R("ti", L, 2 * L), 12.0, None, A.mult)
+    tt(R("tmp"), R("tmp"), R("eag"), A.add)
+    tt(R("tmp"), R("tmp"), R("ti", 2 * L, 3 * L), A.add)
+    cp(R("rho"), R("tmp"))
+    gop(0.13 + 2 * KV * CY, [], [R("mlog", KV, 2 * KV)],
+        lambda g, e: g.iota(T.mlog[:, KV:2 * KV], [[1, L], [L, 16]], 0, 0, allow_small_or_imprecise_dtypes=True))
+    for j in range(12):
+        scat(R("mlog", 0, KV), R("rho", j * 16, j * 16 + 16), R("mlog", KV + j * 256, KV + j * 256 + 256))
+    dma("y", T.tf[:, 0:L], T.mlog[0:128:16, 0:KV], [R("mlog", 0, KV)], [R("tf", 0, L)], 6000)
+    cp(R("linv"), R("tf", 0, L))
+    gop(0.2, [], [R("pcol", 0, 1)], lambda g, e: g.iota(T.pcol[:, 0:1], [[1, 1]], 0, 1))
+    ts(R("pcol", 4, 5), R("pcol", 0, 1), 15, None, A.bitwise_and)
+    cp(R("pcf", 0, 1), R("pcol", 4, 5))
+    gop(0.55, [], [R("val", L, 2 * L)],
+        lambda g, e: g.iota(T.val[:, L:2 * L], [[16, L]], -KV, 0, allow_small_or_imprecise_dtypes=True))
+    ts(R("tmp"), R("dlyi"), float(KV), T.pcf[:, 0:1], A.mult, A.add, extra=[R("pcf", 0, 1)])
+    tt(R("val", 0, L), R("tmp"), R("val", L, 2 * L), A.add)
+
+    def tables(s, e):
+        cnts["tag"] = "T%d" % e
+        dma("y", T.mlog[0:128:16, 0:KV], s[0], [s], [R("mlog", 0, KV)], 6000)
+        for j in range(4):
+            gat(R("mlog", KV + j * V, KV + (j + 1) * V), R("mlog", 0, KV), R("linv", j * 48, j * 48 + 48))
+        o = R("tf", e % 2 * L, (e % 2 + 1) * L)
+        dma("y", o[0], T.mlog[0:128:16, KV:2 * KV], [R("mlog", KV, 2 * KV)], [o], 6000)
+    tables(R("val", 0, L), 0)
+    cnts["tag"] = "J"
+    ts(R("ti", 0, 16), R("sndi"), 15, None, A.bitwise_and)
+    ts(R("ti", 16, 32), R("sndi"), 4, None, A.arith_shift_right)
+    ts(R("tmp", 0, 16), R("ti", 0, 16), 48.0, None, A.mult)
+    tt(R("tmp", 0, 16), R("tmp", 0, 16), R("ti", 16, 32), A.add)
+    cp(R("snp"), R("tmp", 0, 16))
+    gop(0.7, [], [R("retg", 0, 256)],
+        lambda g, e: g.iota(T.retg[:, 0:256], [[1, 256]], 0, 0, allow_small_or_imprecise_dtypes=True))
+    mset(R("cap"), 256.0)
+    scat(R("cap"), R("snp"), R("retg", 0, 256))
+    dma("y", T.tmp[:, 0:48], T.cap[0:128:16, :], [R("cap")], [R("tmp", 0, 48)], 1500)
+    cp(R("inu"), R("tmp", 0, 48))
+
+    free = list(range(NWX))
+    slot = {}
+
+    def xpart(e, d):
+        mm("psW", 0, M, [(PW[u], logn(e), blk(u)) for u in range(6 - d)])
+        act(R("xw", (4 - d) * M, (5 - d) * M), R("psW"), F.Identity, 16.0 ** d, 0.5)
+
+    def fstep(e, t):
+        s = free.pop(0); slot[e, t] = s
+        cnts["tag"] = "F%d%d" % (e, t)
+        lg = logn(e)
+        if e < E - 1 and t == 5:
+            xpart(e, 1)
+        win = R(lg, blk(t - 4), blk(t))
+        for k in range(K):
+            for a, b in ([(0, V)] if k < K - 1 else CH):
+                o = k * V
+                gmul(R("wx", s * KV + o + a, s * KV + o + b), win, R("ix", (o + a) // 16, (o + b) // 16), R("wq", o + a, o + b))
+                if k == 0:
+                    mm("psN", 0, V, [(ID, "dm", 0)] + ([(NEGH, lg, blk(t - 1))] if t > 1 and ZP else []), True, False)
+                mm("psN", a, b - a, [(ID, "wx", s * KV + o + a)], False, k == K - 1)
+        hz = "hz0" if t == 1 else "hz"
+        for a, b in CH:
+            if t < 5:
+                tt(R("psW", a, b), R(hz, a, b), R("psN", a, b), A.subtract)
+                i = act(R(lg, blk(t) + a, blk(t) + b), R("psW", a, b), F.Sigmoid, -2.0 ** 20, 256.0)
+                cnts["fn"] = cnts["fn"][-1:] + [i]
+            else:
+                tt(R(lg, blk(t) + a, blk(t) + b), R(hz, a, b), R("psN", a, b), A.is_le)
+        if t < 5:
+            wires(e, t)
+            if ZP:
+                act(R("hz"), R("psW", 0, V), F.Relu, 0.5, 0.0)
+            else:
+                tt(R("zz"), R("psW", 0, V), R(lg, blk(t), blk(t) + V), A.max)
+                mov(R("hz"), R("zz"), 0.5, "s")
+        if ZP:
+            mm("psN", 0, V, [(ID, "dm", 0)] + [(ID, "wx", s * KV + k * V) for k in range(K)] + [(EIGHT, lg, blk(t))])
+        act(R("rr"), R("psN", 0, V), F.Identity, -2.0, (210.0 if ZP else 194.0) - 1.0 / 64)
+        fa = R("fa", s * V, (s + 1) * V)
+        if ES and e > 0:
+            act(R("rr"), R("rr"), F.Relu, 1.0, -192.5)
+            act(fa, R("rr"), F.Identity, 1.0, 0.5)
+        else:
+            ts(fa, R("rr"), 192.0, 0.5, A.subtract, A.max)
+        if e < E - 1 and 2 <= t < 5:
+            xpart(e, 6 - t)
+
+    def count(e):
+        lg = logn(e)
+        mm("psN", 0, V, [(ID, lg, blk(u)) for u in range(6)] + ([(ID, "cn", 0)] if e else []))
+        if e < E - 1:
+            mov(R("cn"), R("psN", 0, V))
+        else:
+            mov(R("zz"), R("psN", 0, V))
+            dma("y", T.cnt[:], T.zz[:], [R("zz")], [], 3072)
+
+    def swap(o, a, both, e):
+        mm("psW", 512, L, [(DM[e], a[0], a[1])])
+        tt(R("tmp"), R("psW", 512, 512 + L), both, A.mult)
+        tt(R(o[0], o[1], o[1] + L), R(a[0], a[1], a[1] + L), R("tmp"), A.add)
+
+    def votes(e):
+        lg = logn(e); s = free[0]
+        cnts["tag"] = "V%d" % e
+        mm("psW", 0, V, [(PW[5 - u], lg, blk(u)) for u in range(1, 5)], True, False)
+        mm("psW", 0, V, [(PW[0], lg, blk(5))], False, True)
+        act(R("zz"), R("psW", 0, V), F.Identity, -2.0 * 16.0 ** -5, sum(16.0 ** -u for u in range(6)))
+        for j in range(6):
+            p = R("pv", (j % 3) * 512, (j % 3 + 1) * 512)
+            a = j * 512
+            while a < (j + 1) * 512:
+                b = min((j + 1) * 512, (a // V + 1) * V)
+                o = (j % 3 - j) * 512
+                gmul(R("pv", a + o, b + o), R("xw"), R("ix", a // 16, b // 16), R("zz", a % V, (b - 1) % V + 1))
+                a = b
+            q = R("psN", (j % 2) * 512, (j % 2 + 1) * 512)
+            act(q, p, F.Identity, 1.0, 1.5 * 2.0 ** 27)
+            act(q, q, F.Identity, 1.0, -1.5 * 2.0 ** 27)
+            tt(R("wx", s * KV + j * 512, s * KV + (j + 1) * 512), q, p, A.is_gt)
+            if j in (2, 5):
+                c0 = (j - 2) * 32
+                mm("psW", c0, 96, [(R("fm", 16 - i, 144 - i), "wx", s * KV + c0 * 16 + i, 16) for i in range(16)])
+        mm("psW", 768, L, [(DM[e], "cf", 0)])
+        ts(R("eag"), R("psW", 0, L), 9.0, None, A.is_ge)
+        mm("psW", 512, L, [(XM[e], "eag", 0)])
+        both = R("both", e * L, (e + 1) * L)
+        tt(both, R("psW", 512, 512 + L), R("eag"), A.mult)
+        tt(R("tmp"), R("psW", 768, 768 + L), both, A.mult)
+        tt(R("ixf"), R("ixf"), R("tmp"), A.add)
+        cp(R("ix"), R("ixf"))
+        if e == 0:
+            tt(R("cf"), R("cf"), R("tmp"), A.add)
+            swap(("val", L), ("val", 0), both, 0)
+        else:
+            swap(("val", 2 * L), ("val", 0), both, 1)
+            swap(("val", 3 * L), ("val", 2 * L), R("both", 0, L), 0)
+
+    def lists(e):
+        j = e % 2
+        for tau in range(4, -1 if e == E - 1 else 0, -1):
+            ts(R("jx", tau * L, (tau + 1) * L), R("tf", j * L, (j + 1) * L), float((5 - tau) * KV), None, A.min)
+
+    nacc = [0]
+
+    def bstep(e, t):
+        lg = logn(e)
+        S = R(lg, blk(t), blk(t) + V)
+        head = ([] if ZP or t in (0, 5) else [(ID, "ones", 0), (NEG, lg, blk(t))]) + [(HALF, "ls", 0)]
+        alt = "sv" if e == E - 1 else "s"
+        cnts["tag"] = "B%d%d" % (e, t)
+        if t == 5:
+            mm("psP", 0, V, head)
+            cap = S
+        else:
+            k = bmsg[0]; bmsg[0] += 1
+            win = R("mlog", t * KV, 5 * KV + 8)
+            for a in range(3):
+                gat(R("z", a * M + V, (a + 1) * M), win, R("jx", t * L + a * 64 + 48, t * L + (a + 1) * 64), alt)
+                mm("psP", V, H, [(SHB, "z", a * M + V)], a == 0, a == 2)
+                mm("psL", V, H, [(IDF, "z", a * M + V + H)], a == 0, a == 2)
+            o = (k % 2) * 256
+            mov(R("sb", o, o + H), R("psP", V, V + H))
+            mov(R("sb", o + H, o + 256), R("psL", V, V + H))
+            a0, a1 = rland(k)
+            send(R("sb", o + H, o + 256), a1, R("sb", o, o + H), a0, list(rland(k + 1)))
+            mov(R("psL", 0, V), R("psL", 0, V), 0.5, "s")
+            tt(R("cap"), R("psL", 0, V), S, A.max)
+            cap = R("cap")
+            mm("psP", 0, V, head, True, False)
+            for a in range(3):
+                gat(R("z", a * M, a * M + V), win, R("jx", t * L + a * 64, t * L + a * 64 + 48), alt)
+                mm("psP", 0, V, [(IDF, "z", a * M)], False, False)
+            for a, b in CH[::-1]:
+                gat(R("retg", a, b), R("ret", (k % 2) * 264, (k % 2) * 264 + 264), R("inu", a // 16, b // 16), alt)
+                mm("psP", a, b - a, [(IDF, "retg", a)], False, True)
+                if a == 0:
+                    ops[-1]["after"].append(len(ops) - 3)
+                    if alt == "s":
+                        ops[-2]["after"].append(len(ops) - 4)
+        fn, fo = ("f0", 0) if t == 0 else ("fa", slot[e, t] * V)
+        cn, co = (lg, blk(t)) if t == 5 else ("cap", 0)
+        for a, b in CH[::-1]:
+            tt(R("psP", a, b), R("psP", a, b), R(fn, fo + a, fo + b), A.mult)
+            tt(R("psL", a, b), R("psP", a, b), R(cn, co + a, co + b), A.min)
+            for k in range(K if t else 0):
+                o = k * V
+                tt(R("mlog", (t - 1) * KV + o + a, (t - 1) * KV + o + b), R("psL", a, b),
+                   R("wx", slot[e, t] * KV + o + a, slot[e, t] * KV + o + b), A.mult)
+        if t == 0:
+            mov(R("cap"), R("psL", 0, V), 2.0)
+            dma("y", T.lam[:], T.cap[:], [R("cap")], [], 3072)
+            return
+        s = slot[e, t]
+        free.append(s)
+        mb = R("mlog", (t - 1) * KV, t * KV)
+        if e == E - 1 and t == 1:
+            for j in range(6):
+                c = ("psN", "psW")[j % 2]; o = (j // 2 % 2) * 512
+                tt(R(c, o, o + 512), R("acc", j * 512, j * 512 + 512), R("mlog", j * 512, j * 512 + 512), A.add)
+                tt(R("acc", j * 512, j * 512 + 512), R(c, o, o + 512), R("xw", j * 512, j * 512 + 512), A.mult)
+                if j % 2:
+                    dma("y", T.gam[:, (j - 1) * 512:(j + 1) * 512], T.acc[:, (j - 1) * 512:(j + 1) * 512],
+                        [R("acc", (j - 1) * 512, (j + 1) * 512)], [], 4096)
+        elif nacc[0] == 0:
+            dma("y", T.acc[:], mb[0], [mb], [R("acc")], 12288)
+        else:
+            dma("g", T.acc[:], mb[0], [mb, R("acc")], [R("acc")], 12288, accum_op=A.add, max_dma_last_dim=6144)
+        nacc[0] += 1
+
+    for t in range(1, 6):
+        fstep(0, t)
+    for e in range(E):
+        cnts["tag"] = "C%d" % e
+        count(e)
+        if e < E - 1:
+            votes(e)
+        cnts["tag"] = "R%d" % e
+        if e == E - 1:
+            for fn in (F.Ln, F.Exp):
+                last = cnts["fn"]
+                for j in range(6):
+                    x, w = R("xw", j * 512, j * 512 + 512), R("wq", j * 512, j * 512 + 512)
+                    p = R(("psN", "psW")[j % 2], (j // 2 % 2) * 512, (j // 2 % 2) * 512 + 512)
+                    i = act(x, w, fn) if fn == F.Ln else act(p, x, fn, -1.0, math.log(2.0))
+                    ops[i]["after"] += last
+                    ops[i]["cost"] += 0.0 if j else 1.9
+                    cnts["fn"] = cnts["fn"] + [i]
+                    last = [i] + last
+                    if fn == F.Exp:
+                        tt(x, p, w, A.mult)
+                        act(x, x, F.Identity, -0.5, 2.0)
+                        tt(x, p, x, A.mult)
+        lists(e)
+        if e < E - 1:
+            tables(R("val", (2 * e + 1) * L, (2 * e + 2) * L), e + 1)
+        for t in range(5, 0, -1):
+            if e < E - 1:
+                fstep(e + 1, 6 - t)
+            bstep(e, t)
+    bstep(E - 1, 0)
+    return ops
+
+
+KEPT = {}
+SEED, ROUNDS = 1, 2000
+
+
+def order(ops):
+    n = len(ops)
+    deps = [set(o["after"]) for o in ops]
+    raw = [set(o["after"]) for o in ops]
+    hist = {}
+    for i, o in enumerate(ops):
+        for nm, a, b, x in o["rd"]:
+            for j, c, d, w in hist.get(nm, ()):
+                if w and c < b and a < d:
+                    deps[i].add(j); raw[i].add(j)
+        for nm, a, b, x in o["wr"] + o.get("guard", []):
+            for j, c, d, w in hist.get(nm, ()):
+                if c < b and a < d:
+                    deps[i].add(j); raw[i].add(j)
+        for nm, a, b, x in o["ex"]:
+            for j, c, d, w in hist.get(nm, ()):
+                if c < b and a < d:
+                    deps[i].add(j)
+        for nm, a, b, x in o["ex"]:
+            hist[nm] = [h for h in hist.get(nm, []) if not (a <= h[1] and h[2] <= b)] + [(i, a, b, False)]
+        for nm, a, b, x in o["wr"]:
+            hist[nm] = [h for h in hist.get(nm, []) if not (a <= h[1] and h[2] <= b)] + [(i, a, b, True)]
+        for nm, a, b, x in o["rd"]:
+            if not x:
+                hist.setdefault(nm, []).append((i, a, b, False))
+        deps[i].discard(i); raw[i].discard(i)
+    succ = [[] for _ in ops]
+    for i in range(n):
+        for j in deps[i]:
+            succ[j].append(i)
+    HOP = 0.12
+    prio = [0.0] * n
+    for i in range(n - 1, -1, -1):
+        prio[i] = ops[i]["cost"] + ops[i]["lat"] + HOP + max([prio[j] for j in succ[i]], default=0.0)
+    qof = {"v": "v", "s": "s", "p": "p", "g": "g", "y": "y", "a": "s"}
+
+    hop = lambda i, j: HOP if i in raw[j] and not ops[i]["engs"] == ops[j]["engs"] == "p" else 0.0
+    fw = [[(j, hop(i, j)) for j in succ[i]] for i in range(n)]
+    bw = [[(j, hop(j, i)) for j in sorted(deps[i])] for i in range(n)]
+
+    def place(key, back=False):
+        nxt = bw if back else fw
+        left = [len(d) for d in (fw if back else bw)]
+        ready_at = [0.0] * n
+        ready = [i for i in range(n) if left[i] == 0]
+        line = {q: [] for q in "vspgy"}
+        eng, fin, st = [None] * n, [0.0] * n, [0.0] * n
+        while ready:
+            i = max(ready, key=lambda x: key[x])
+            ready.remove(i)
+            best, c = None, ops[i]["cost"]
+            for q in (ops[i]["engs"] or "-"):
+                t0, k = ready_at[i] + (ops[i]["lat"] if back else 0.0), 0
+                if q != "-":
+                    ln = line[qof[q]]
+                    k = len(ln)
+                    while k > 0 and ln[k - 1][1] > t0:
+                        k -= 1
+                    while k < len(ln) and ln[k][0] < t0 + c:
+                        t0 = max(t0, ln[k][1]); k += 1
+                if best is None or t0 < best[0] - 1e-9:
+                    best = (t0, q, k)
+            t0, q, k = best
+            if q != "-":
+                line[qof[q]].insert(k, (t0, t0 + c))
+            eng[i], st[i], fin[i] = q, t0, t0 + c + (0.0 if back else ops[i]["lat"])
+            for j, h in nxt[i]:
+                left[j] -= 1
+                if ready_at[j] < fin[i] + h:
+                    ready_at[j] = fin[i] + h
+                if left[j] == 0:
+                    ready.append(j)
+        return eng, st, fin
+
+    if "best" not in KEPT:
+        rng = np.random.RandomState(SEED)
+        tags = sorted(set(o["tag"] for o in ops))
+        best = place(prio)
+        for it in range(ROUNDS):
+            shift = {t: 0.0 for t in tags}
+            for t in rng.randint(0, len(tags), 3):
+                shift[tags[t]] = float(rng.normal(0, 4.0))
+            noise = rng.normal(0, 0.3, n) * (it % 2)
+            r = place([best[2][i] + shift[ops[i]["tag"]] + float(noise[i]) for i in range(n)], True)
+            c = place(r[2])
+            if max(c[2]) <= max(best[2]):
+                best = c
+        KEPT["best"] = best
+    eng, st, fin = KEPT["best"]
+    seq = sorted(range(n), key=lambda i: (st[i], i))
+    return seq, eng, deps, raw, st, fin
+
+
+def rank_program(g, core, T, topo):
+    if T.rank_of(core) is None:
+        return
+    ops = plan(T, topo, core)
+    seq, eng, deps, raw, st, fin = order(ops)
+    queue = {"v": g.vector, "s": g.scalar, "p": g.tensor, "g": g, "y": g.sync, "a": g.scalar}
+    same = {"v": "v", "s": "s", "p": "p", "g": "g", "y": "y", "a": "s"}
+    csem = {"v": "cv", "s": "cs", "p": "cp", "g": "cg"}
+    known = {q: {} for q in "vspgy"}
+    count = {q: 0 for q in csem}
+    token, clock, total = {}, {}, {}
+    for i in seq:
+        o, q = ops[i], eng[i]
+        if o["kind"] == "a":
+            token[i] = o["sem"]; clock[i] = {}; total[o["sem"][0]] = o["sem"][1]
+            continue
+        kn = known[same[q]]
+        need = {}
+        for j in deps[i]:
+            if ops[j]["kind"] == "c" and eng[j] == q and o["kind"] == "c" and (q == "p" or j not in raw[i]):
+                continue
+            s, v = token[j]
+            if v > need.get(s, (0, None))[0]:
+                need[s] = (v, j)
+        for s, (v, j) in sorted(need.items(), key=lambda x: -fin[x[1][1]]):
+            if kn.get(s, 0) < v:
+                queue[q].wait_ge(T.sem[s], v)
+                kn[s] = v
+                for s2, v2 in clock[j].items():
+                    if kn.get(s2, 0) < v2:
+                        kn[s2] = v2
+        clock[i] = dict(kn)
+        ins = o["emit"](g, q)
+        if o["kind"] == "c":
+            count[q] += 1
+            ins.then_inc(T.sem[csem[q]], 1)
+            token[i] = (csem[q], count[q])
+        elif o["kind"] == "d":
+            ins.then_inc(T.sem[o["sem"]], 16)
+            token[i] = (o["sem"], 16)
+        else:
+            token[i] = o["sem"]
+        total[token[i][0]] = token[i][1]
+    for s, v in total.items():
+        if known["g"].get(s, 0) < v:
+            g.wait_ge(T.sem[s], v)

@@ -7,8 +7,14 @@ V, H, K, M, KV, L = 768, 128, 4, 1024, 3072, 192
 E = 3
 TINY = 2.0 ** -30
 NWX = 6
-ES = True
+ES = False
 ZP = False
+XS = [2, 0, 0]
+PG, GADD, ZD, FIN = True, 0, True, 4
+UC = [False, False, False]
+CP = [False, False, False]
+ALT = "sv"
+YW = True
 f32, bf, i32, u16 = "float32", "bfloat16", "int32", "uint16"
 
 SCRATCH = {
@@ -65,17 +71,17 @@ SCRATCH = {
     "psL": ("psum", [128, 1024], f32),
 }
 SEMAPHORES = (["cv", "cs", "cp", "cg"] + ["arr%d" % i for i in range(27)] + ["snt%d" % i for i in range(27)]
-              + ["dq%d" % i for i in range(48)])
+              + ["dq%d" % i for i in range(56)])
 
 ALIAS = {"ti": ("pint", 0, 3 * L), "srci": ("pint", 3 * L, L), "dlyi": ("pint", 4 * L, L), "hz": ("zz", 0, V),
          "dr": ("dm", 0, V)}
 CH = [(0, 512), (512, V)]
-CY = 0.83e-3 * 1.25
-GA, SC, PE = 1.55, 3.5, 0.42e-3 * 1.25
-COMM = 4.5
+PARS = [(1.25, 1.55, 3.5, 4.5), (1.0, 1.4, 3.0, 4.3), (1.5, 2.05, 5.0, 4.5)]
+WEIGHTS = [1 / 331.0, 1 / 285.0, 1 / 420.0]
 
 
-def plan(T, topo, core):
+def plan(T, topo, core, par=PARS[0]):
+    CY, GA, SC, PE, COMM = 0.83e-3 * par[0], par[1], par[2], 0.42e-3 * par[0], par[3]
     ops = []
     rank = T.rank_of(core)
     n = len(T.cores)
@@ -139,9 +145,9 @@ def plan(T, topo, core):
             return g.vector.tensor_copy(o[0], win[0].indirect(lst[0]))
         return add(engs, 0.07 + o[3] * GA * CY, [win, lst], [o], emit)
 
-    def gmul(o, win, lst, b):
+    def gmul(o, win, lst, b, op=A.mult):
         return add("v", 0.06 + o[3] * GA * CY, [win, lst, b], [o],
-                   lambda g, e: g.vector.tensor_tensor(o[0], win[0].indirect(lst[0]), b[0], A.mult))
+                   lambda g, e: g.vector.tensor_tensor(o[0], win[0].indirect(lst[0]), b[0], op))
 
     def scat(win, lst, i):
         return add("v", 0.06 + i[3] * SC * CY, [lst, i], [win],
@@ -233,7 +239,8 @@ def plan(T, topo, core):
     ts(R("log0", blk(0), blk(0) + V), R("dr"), 1.0, None, A.is_ge)
     wires(0, 0)
     mset(R("log0", 0, 3 * M), 0.0)
-    ts(R("wq"), R("wq"), TINY, None, A.max)
+    ts(R("wq", 0, 2 * V), R("wq", 0, 2 * V), TINY, None, A.max)
+    act(R("wq", 2 * V, KV), R("wq", 2 * V, KV), F.Identity, 1.0, TINY)
     ts(R("ti", 0, L), R("srci"), 1023, None, A.bitwise_and)
     cp(R("cf"), R("ti", 0, L))
     ts(R("tmp"), R("dlyi"), -1024.0, 4096.0, A.mult, A.add)
@@ -326,7 +333,12 @@ def plan(T, topo, core):
         for k in range(K):
             for a, b in ([(0, V)] if k < K - 1 else CH):
                 o = k * V
-                gmul(R("wx", s * KV + o + a, s * KV + o + b), win, R("ix", (o + a) // 16, (o + b) // 16), R("wq", o + a, o + b))
+                wx, ix = R("wx", s * KV + o + a, s * KV + o + b), R("ix", (o + a) // 16, (o + b) // 16)
+                if k >= K - XS[e]:
+                    gat(wx, win, ix)
+                    tt(wx, wx, R("wq", o + a, o + b), A.mult)
+                else:
+                    gmul(wx, win, ix, R("wq", o + a, o + b))
                 if k == 0:
                     mm("psN", 0, V, [(ID, "dm", 0)] + ([(NEGH, lg, blk(t - 1))] if t > 1 and ZP else []), True, False)
                 mm("psN", a, b - a, [(ID, "wx", s * KV + o + a)], False, k == K - 1)
@@ -342,6 +354,11 @@ def plan(T, topo, core):
             wires(e, t)
             if ZP:
                 act(R("hz"), R("psW", 0, V), F.Relu, 0.5, 0.0)
+            elif ZD and e > 0:
+                act(R("zz"), R("psW", 0, V), F.Relu)
+                S = R(lg, blk(t), blk(t) + V)
+                dma("g", T.zz[:], S[0], [S, R("zz")], [R("zz")], 3072, accum_op=A.add)
+                mov(R("hz"), R("zz"), 0.5, "s")
             else:
                 tt(R("zz"), R("psW", 0, V), R(lg, blk(t), blk(t) + V), A.max)
                 mov(R("hz"), R("zz"), 0.5, "s")
@@ -376,11 +393,17 @@ def plan(T, topo, core):
         cnts["tag"] = "V%d" % e
         mm("psW", 0, V, [(PW[5 - u], lg, blk(u)) for u in range(1, 5)], True, False)
         mm("psW", 0, V, [(PW[0], lg, blk(5))], False, True)
-        act(R("zz"), R("psW", 0, V), F.Identity, -2.0 * 16.0 ** -5, sum(16.0 ** -u for u in range(6)))
+        act(R("psW", 0, V) if PG else R("zz"), R("psW", 0, V), F.Identity, -2.0 * 16.0 ** -5, sum(16.0 ** -u for u in range(6)))
+        for k in range(K if PG else 0):
+            p = R("mlog", 2 * KV + k * V, 2 * KV + (k + 1) * V)
+            gat(p, R("xw"), R("ix", k * 48, k * 48 + 48))
+            tt(p, R("psW", 0, V), p, A.mult)
         for j in range(6):
             p = R("pv", (j % 3) * 512, (j % 3 + 1) * 512)
             a = j * 512
-            while a < (j + 1) * 512:
+            if PG:
+                p = R("mlog", 2 * KV + a, 2 * KV + a + 512)
+            while a < (j + 1) * 512 and not PG:
                 b = min((j + 1) * 512, (a // V + 1) * V)
                 o = (j % 3 - j) * 512
                 gmul(R("pv", a + o, b + o), R("xw"), R("ix", a // 16, b // 16), R("zz", a % V, (b - 1) % V + 1))
@@ -413,12 +436,13 @@ def plan(T, topo, core):
             ts(R("jx", tau * L, (tau + 1) * L), R("tf", j * L, (j + 1) * L), float((5 - tau) * KV), None, A.min)
 
     nacc = [0]
+    REC = [R("pv", 0, V), R("pv", V, 2 * V), R("val"), R("zz")]
 
     def bstep(e, t):
         lg = logn(e)
         S = R(lg, blk(t), blk(t) + V)
         head = ([] if ZP or t in (0, 5) else [(ID, "ones", 0), (NEG, lg, blk(t))]) + [(HALF, "ls", 0)]
-        alt = "sv" if e == E - 1 else "s"
+        alt = ALT if e == E - 1 else "s"
         cnts["tag"] = "B%d%d" % (e, t)
         if t == 5:
             mm("psP", 0, V, head)
@@ -427,7 +451,16 @@ def plan(T, topo, core):
             k = bmsg[0]; bmsg[0] += 1
             win = R("mlog", t * KV, 5 * KV + 8)
             for a in range(3):
-                gat(R("z", a * M + V, (a + 1) * M), win, R("jx", t * L + a * 64 + 48, t * L + (a + 1) * 64), alt)
+                zw, jw = R("z", a * M + V, (a + 1) * M), R("jx", t * L + a * 64 + 48, t * L + (a + 1) * 64)
+                if e < E - 1 or not YW:
+                    gat(zw, win, jw, alt)
+                else:
+                    lx, yw = ("rho", "linv", "ix")[t % 3], R(("rr", "hz0")[t % 2], a * 256, a * 256 + 256)
+                    if a == 0:
+                        ts(R(lx), R("eag"), float((5 - t) * V), None, A.min)
+                    assert slot[e, 5] == 4
+                    gat(yw, R("wx", t * KV, 5 * KV + 16), jw)
+                    gmul(zw, R("xw", t * V, 5 * V + 8), R(lx, a * 64 + 48, (a + 1) * 64), yw)
                 mm("psP", V, H, [(SHB, "z", a * M + V)], a == 0, a == 2)
                 mm("psL", V, H, [(IDF, "z", a * M + V + H)], a == 0, a == 2)
             o = (k % 2) * 256
@@ -435,13 +468,24 @@ def plan(T, topo, core):
             mov(R("sb", o + H, o + 256), R("psL", V, V + H))
             a0, a1 = rland(k)
             send(R("sb", o + H, o + 256), a1, R("sb", o, o + H), a0, list(rland(k + 1)))
-            mov(R("psL", 0, V), R("psL", 0, V), 0.5, "s")
-            tt(R("cap"), R("psL", 0, V), S, A.max)
+            if CP[e]:
+                mov(R("cap"), R("psL", 0, V), 0.5, "s")
+                mm("psL", 0, V, [(ID, lg, blk(t)), (IDF, "cap", 0)])
+                act(R("cap"), R("psL", 0, V), F.Relu, -1.0, 1.0)
+                act(R("cap"), R("cap"), F.Identity, -1.0, 1.0)
+            else:
+                mov(R("psL", 0, V), R("psL", 0, V), 0.5, "s")
+                tt(R("cap"), R("psL", 0, V), S, A.max)
             cap = R("cap")
             mm("psP", 0, V, head, True, False)
             for a in range(3):
-                gat(R("z", a * M, a * M + V), win, R("jx", t * L + a * 64, t * L + a * 64 + 48), alt)
-                mm("psP", 0, V, [(IDF, "z", a * M)], False, False)
+                zo, jo = R("z", a * M, a * M + V), R("jx", t * L + a * 64, t * L + a * 64 + 48)
+                if e >= GADD and a == 2:
+                    gmul(zo, win, jo, R("z", M, M + V), A.add)
+                else:
+                    gat(zo, win, jo, alt)
+                if not (e >= GADD and a == 1):
+                    mm("psP", 0, V, [(IDF, "z", a * M)], False, False)
             for a, b in CH[::-1]:
                 gat(R("retg", a, b), R("ret", (k % 2) * 264, (k % 2) * 264 + 264), R("inu", a // 16, b // 16), alt)
                 mm("psP", a, b - a, [(IDF, "retg", a)], False, True)
@@ -454,6 +498,12 @@ def plan(T, topo, core):
         for a, b in CH[::-1]:
             tt(R("psP", a, b), R("psP", a, b), R(fn, fo + a, fo + b), A.mult)
             tt(R("psL", a, b), R("psP", a, b), R(cn, co + a, co + b), A.min)
+            if e == E - 1 and t and YW:
+                mov(R("xw", (t - 1) * V + a, (t - 1) * V + b), R("psL", a, b), 1.0, "s")
+            if UC[e] and a:
+                continue
+            if UC[e]:
+                b = V
             for k in range(K if t else 0):
                 o = k * V
                 tt(R("mlog", (t - 1) * KV + o + a, (t - 1) * KV + o + b), R("psL", a, b),
@@ -466,13 +516,17 @@ def plan(T, topo, core):
         free.append(s)
         mb = R("mlog", (t - 1) * KV, t * KV)
         if e == E - 1 and t == 1:
-            for j in range(6):
-                c = ("psN", "psW")[j % 2]; o = (j // 2 % 2) * 512
-                tt(R(c, o, o + 512), R("acc", j * 512, j * 512 + 512), R("mlog", j * 512, j * 512 + 512), A.add)
-                tt(R("acc", j * 512, j * 512 + 512), R(c, o, o + 512), R("xw", j * 512, j * 512 + 512), A.mult)
-                if j % 2:
-                    dma("y", T.gam[:, (j - 1) * 512:(j + 1) * 512], T.acc[:, (j - 1) * 512:(j + 1) * 512],
-                        [R("acc", (j - 1) * 512, (j + 1) * 512)], [], 4096)
+            for j in range(K):
+                p, ac = R(("psN", "psW")[j % 2], 0, V), R("acc", j * V, (j + 1) * V)
+                mj = R("mlog", j * V, (j + 1) * V)
+                if j < FIN:
+                    dma("g", ac[0], mj[0], [mj, ac], [ac], 3072, accum_op=A.add)
+                    mov(p, REC[j], 1.0, "s")
+                    tt(ac, p, ac, A.mult)
+                else:
+                    tt(p, ac, mj, A.add)
+                    tt(ac, p, REC[j], A.mult)
+                dma("y", T.gam[:, j * V:(j + 1) * V], ac[0], [ac], [], 3072)
         elif nacc[0] == 0:
             dma("y", T.acc[:], mb[0], [mb], [R("acc")], 12288)
         else:
@@ -490,9 +544,8 @@ def plan(T, topo, core):
         if e == E - 1:
             for fn in (F.Ln, F.Exp):
                 last = cnts["fn"]
-                for j in range(6):
-                    x, w = R("xw", j * 512, j * 512 + 512), R("wq", j * 512, j * 512 + 512)
-                    p = R(("psN", "psW")[j % 2], (j // 2 % 2) * 512, (j // 2 % 2) * 512 + 512)
+                for j in range(K):
+                    x, w, p = REC[j], R("wq", j * V, (j + 1) * V), R(("psN", "psW")[j % 2], 0, V)
                     i = act(x, w, fn) if fn == F.Ln else act(p, x, fn, -1.0, math.log(2.0))
                     ops[i]["after"] += last
                     ops[i]["cost"] += 0.0 if j else 1.9
@@ -502,6 +555,17 @@ def plan(T, topo, core):
                         tt(x, p, w, A.mult)
                         act(x, x, F.Identity, -0.5, 2.0)
                         tt(x, p, x, A.mult)
+            cnts["tag"] = "L"
+            t2, q = R("tf", 0, L), R("ti", 0, L)
+            ts(q, t2, 1.0 / KV, -0.4998, A.mult, A.add)
+            ts(R("cf"), q, -float(KV), None, A.mult)
+            ts(R("ixf"), q, float(V), None, A.mult)
+            tt(R("cf"), R("cf"), t2, A.add)
+            ts(q, R("cf"), 1.0 / V, -0.4993, A.mult, A.add)
+            tt(R("cf"), R("cf"), R("ixf"), A.add)
+            ts(R("ixf"), q, -float(V), None, A.mult)
+            tt(R("eag"), R("cf"), R("ixf"), A.add)
+            mset(R("xw", 5 * V, 5 * V + 8), 0.0)
         lists(e)
         if e < E - 1:
             tables(R("val", (2 * e + 1) * L, (2 * e + 2) * L), e + 1)
@@ -514,10 +578,10 @@ def plan(T, topo, core):
 
 
 KEPT = {}
-SEED, ROUNDS = 1, 2000
+SEED, ROUNDS = 2, 3000
 
 
-def order(ops):
+def order(ops, others=()):
     n = len(ops)
     deps = [set(o["after"]) for o in ops]
     raw = [set(o["after"]) for o in ops]
@@ -594,7 +658,26 @@ def order(ops):
     if "best" not in KEPT:
         rng = np.random.RandomState(SEED)
         tags = sorted(set(o["tag"] for o in ops))
+        alts = [([o["cost"] for o in a], [o["lat"] for o in a]) for a in others]
+
+        def score(c):
+            tot = max(c[2]) * WEIGHTS[0]
+            sq = sorted(range(n), key=lambda i: (c[1][i], i))
+            for (cost, lat), w in zip(alts, WEIGHTS[1:]):
+                busy, end = {}, [0.0] * n
+                for i in sq:
+                    t = 0.0
+                    for j, h in bw[i]:
+                        if end[j] + h > t:
+                            t = end[j] + h
+                    q = qof.get(c[0][i])
+                    if q:
+                        t = max(t, busy.get(q, 0.0)); busy[q] = t + cost[i]
+                    end[i] = t + cost[i] + lat[i]
+                tot += max(end) * w
+            return tot
         best = place(prio)
+        top = score(best)
         for it in range(ROUNDS):
             shift = {t: 0.0 for t in tags}
             for t in rng.randint(0, len(tags), 3):
@@ -602,8 +685,10 @@ def order(ops):
             noise = rng.normal(0, 0.3, n) * (it % 2)
             r = place([best[2][i] + shift[ops[i]["tag"]] + float(noise[i]) for i in range(n)], True)
             c = place(r[2])
-            if max(c[2]) <= max(best[2]):
-                best = c
+            if max(c[2]) <= max(best[2]) * 1.02:
+                v = score(c)
+                if v <= top:
+                    best, top = c, v
         KEPT["best"] = best
     eng, st, fin = KEPT["best"]
     seq = sorted(range(n), key=lambda i: (st[i], i))
@@ -614,7 +699,7 @@ def rank_program(g, core, T, topo):
     if T.rank_of(core) is None:
         return
     ops = plan(T, topo, core)
-    seq, eng, deps, raw, st, fin = order(ops)
+    seq, eng, deps, raw, st, fin = order(ops, [plan(T, topo, core, p) for p in PARS[1:]])
     queue = {"v": g.vector, "s": g.scalar, "p": g.tensor, "g": g, "y": g.sync, "a": g.scalar}
     same = {"v": "v", "s": "s", "p": "p", "g": "g", "y": "y", "a": "s"}
     csem = {"v": "cv", "s": "cs", "p": "cp", "g": "cg"}

@@ -8,11 +8,20 @@ E = 3
 TINY = 2.0 ** -30
 NWX = 6
 ES = False
-ZP = False
-XS = [2, 0, 0]
-PG, GADD, ZD, FIN = True, 0, True, 4
+XS = [2, 2, 2]
+GADD, FIN = 0, 4
 UC = [False, False, False]
-CP = [False, False, False]
+SP = "s"
+ZD = [True, True, True]
+VR = ()
+NA = 1
+MMS = 2
+XD = True
+FOLD = False
+ZP = [1, 1, 2]
+DS = [0, 0, 0]
+XK = [(), (3,), (2, 3), (1, 2, 3)]
+ZA = [True, True, False]
 ALT = "sv"
 YW = True
 f32, bf, i32, u16 = "float32", "bfloat16", "int32", "uint16"
@@ -21,16 +30,16 @@ SCRATCH = {
     "wq": ("sbuf", [128, KV], bf),
     "wx": ("sbuf", [128, NWX * KV], bf),
     "mlog": ("sbuf", [128, 5 * KV + 8], f32),
-    "z": ("sbuf", [128, KV], f32),
+    "z": ("sbuf", [128, 2 * V], f32),
     "retg": ("sbuf", [128, V], f32),
     "acc": ("sbuf", [128, KV], f32),
-    "log0": ("sbuf", [128, 8 * M + V], bf),
-    "log1": ("sbuf", [128, 8 * M + V], bf),
+    "log": ("sbuf", [128, 15 * M], bf),
+    "dpt": ("sbuf", [128, L], f32),
     "fa": ("sbuf", [128, NWX * V], bf),
     "f0": ("sbuf", [128, V], bf),
     "xw": ("sbuf", [128, 4 * M], f32),
     "pint": ("sbuf", [128, 5 * L], i32),
-    "pv": ("sbuf", [128, 2 * V], f32),
+    "hl": ("sbuf", [128, KV + 8], f32),
     "zz": ("sbuf", [128, V], f32),
     "hz0": ("sbuf", [128, V], bf),
     "rr": ("sbuf", [128, V], bf),
@@ -40,11 +49,15 @@ SCRATCH = {
     "ones": ("sbuf", [128, V], bf),
     "cn": ("sbuf", [128, V], bf),
     "ret": ("sbuf", [128, 2 * 264], f32),
-    "sf": ("sbuf", [128, 2 * 384], bf),
-    "sb": ("sbuf", [128, 2 * 256], f32),
+    "sf": ("sbuf", [128, 384], bf),
+    "sb": ("sbuf", [128, 256], f32),
     "id2": ("sbuf", [128, 256], bf),
-    "id2f": ("sbuf", [128, 256], f32),
-    "pw": ("sbuf", [128, 7 * 128], bf),
+    "id2f": ("sbuf", [128, 272], f32),
+    "zw": ("sbuf", [128, V], f32),
+    "wpw": ("sbuf", [128, V], bf),
+    "lt": ("sbuf", [128, 96], f32),
+    "lw": ("sbuf", [128, 288], u16),
+    "pw": ("sbuf", [128, 10 * 128], bf),
     "xm": ("sbuf", [128, 4 * 128], f32),
     "fm": ("sbuf", [128, 144], bf),
     "bg": ("sbuf", [128, 16], bf),
@@ -61,7 +74,7 @@ SCRATCH = {
     "ix": ("sbuf", [128, L], u16),
     "rho": ("sbuf", [128, L], u16),
     "linv": ("sbuf", [128, L], u16),
-    "jx": ("sbuf", [128, 5 * L], u16),
+    "jx": ("sbuf", [128, 5 * 144], u16),
     "snu": ("sbuf", [128, 16], u16),
     "snp": ("sbuf", [128, 16], u16),
     "inu": ("sbuf", [128, 48], u16),
@@ -71,17 +84,17 @@ SCRATCH = {
     "psL": ("psum", [128, 1024], f32),
 }
 SEMAPHORES = (["cv", "cs", "cp", "cg"] + ["arr%d" % i for i in range(27)] + ["snt%d" % i for i in range(27)]
-              + ["dq%d" % i for i in range(56)])
+              + ["dq%d" % i for i in range(80)])
 
-ALIAS = {"ti": ("pint", 0, 3 * L), "srci": ("pint", 3 * L, L), "dlyi": ("pint", 4 * L, L), "hz": ("zz", 0, V),
+ALIAS = {"ti": ("pint", 0, 3 * L), "srci": ("pint", 3 * L, L), "dlyi": ("pint", 4 * L, L),
          "dr": ("dm", 0, V)}
 CH = [(0, 512), (512, V)]
-PARS = [(1.25, 1.55, 3.5, 4.5), (1.0, 1.4, 3.0, 4.3), (1.5, 2.05, 5.0, 4.5)]
-WEIGHTS = [1 / 331.0, 1 / 285.0, 1 / 420.0]
+PARS = [(1.2, 1.55, 3.5, 4.0, 0.5), (1.0, 1.4, 3.0, 3.6, 0.42), (1.45, 1.9, 5.0, 4.5, 0.6), (1.2, 1.4, 3.5, 4.0, 0.85)]
+WEIGHTS = [1 / 300.0, 1 / 250.0, 1 / 380.0, 2 / 380.0]
 
 
 def plan(T, topo, core, par=PARS[0]):
-    CY, GA, SC, PE, COMM = 0.83e-3 * par[0], par[1], par[2], 0.42e-3 * par[0], par[3]
+    CY, GA, SC, PE, COMM = 0.83e-3 * par[0], par[1], par[2], 1e-3 * par[4], par[3]
     ops = []
     rank = T.rank_of(core)
     n = len(T.cores)
@@ -107,7 +120,7 @@ def plan(T, topo, core, par=PARS[0]):
         rd = [r for x in reads for r in x[1]]
         wr = [r for x in writes for r in x[1]]
         ops.append({"ex": [r for r in rd if r[3] and r not in wr], "engs": engs, "cost": cost, "rd": rd, "wr": wr,
-                    "emit": emit, "kind": kind, "lat": lat, "sem": sem, "after": list(after), "tag": cnts["tag"]})
+                    "emit": emit, "kind": kind, "lat": lat, "sem": sem, "after": list(after), "tag": cnts["tag"], "occ": 0.0})
         return len(ops) - 1
 
     def two(*xs):
@@ -115,6 +128,8 @@ def plan(T, topo, core, par=PARS[0]):
 
     def ts(o, i, s1, s2, op0, op1=None, extra=()):
         c = 0.06 + max(64, i[3] * (0.5 if two(o, i) else 1)) * CY
+        if op0 == A.mult and op1 in (None, A.add) and not extra and all(x[0].dtype == T.acc.dtype for x in (o, i)):
+            return mov(o, i, s1, "sv", s2 or 0.0)
         if op1 is None:
             return add("v", c, [i] + list(extra), [o], lambda g, e: g.vector.tensor_scalar(o[0], i[0], s1, None, op0))
         return add("v", c, [i] + list(extra), [o], lambda g, e: g.vector.tensor_scalar(o[0], i[0], s1, s2, op0, op1))
@@ -131,17 +146,19 @@ def plan(T, topo, core, par=PARS[0]):
         return add("s", 0.07 + max(64, i[3]) * CY, [i], [o],
                    lambda g, e: g.scalar.activation(o[0], i[0], func, bias=bias, scale=scale))
 
-    def mov(o, i, scale=1.0, engs="sv"):
+    def mov(o, i, scale=1.0, engs="sv", bias=0.0):
         def emit(g, e):
             if e == "s":
-                return g.scalar.activation(o[0], i[0], F.Identity, bias=0.0, scale=scale)
-            return g.vector.tensor_scalar(o[0], i[0], scale, None, A.mult)
+                return g.scalar.activation(o[0], i[0], F.Identity, bias=bias, scale=scale)
+            return g.vector.tensor_scalar(o[0], i[0], scale, bias, A.mult, A.add)
         return add(engs, 0.07 + max(64, i[3]) * CY, [i], [o], emit)
 
-    def gat(o, win, lst, engs="s"):
+    def gat(o, win, lst, engs="s", plus=0.0):
         def emit(g, e):
             if e == "s":
-                return g.scalar.activation(o[0], win[0].indirect(lst[0]), F.Identity)
+                return g.scalar.activation(o[0], win[0].indirect(lst[0]), F.Identity, bias=plus)
+            if plus:
+                return g.vector.tensor_scalar(o[0], win[0].indirect(lst[0]), plus, None, A.add)
             return g.vector.tensor_copy(o[0], win[0].indirect(lst[0]))
         return add(engs, 0.07 + o[3] * GA * CY, [win, lst], [o], emit)
 
@@ -157,6 +174,10 @@ def plan(T, topo, core, par=PARS[0]):
         return add("v", 0.06 + max(64, o[3] * (0.5 if two(o) else 1)) * CY, [], [o], lambda g, e: g.vector.memset(o[0], c))
 
     def mm(ps, o0, n, terms, start=True, stop=True):
+        if n > 256 and len(terms) > MMS:
+            for j in range(0, len(terms), MMS):
+                mm(ps, o0, n, terms[j:j + MMS], start and j == 0, stop and j + MMS >= len(terms))
+            return
         a = o0
         while a < o0 + n:
             b = min(o0 + n, (a // 512 + 1) * 512)
@@ -183,17 +204,20 @@ def plan(T, topo, core, par=PARS[0]):
                 return g.dma_start(o, i, **kw)
             return (g.sync if e == "y" else g.scalar).dma_start(o, i)
         f = 2.0 if kw.get("accum_op") is not None else 1.0
-        return add(q, 1.0 if q == "g" else 0.1, reads, writes, emit, "d", 2.0 + f * nbytes / 4700.0, s)
+        add(q, 1.0 if q == "g" else 0.1, reads, writes, emit, "d", 2.0, s)
+        ops[-1]["occ"] = f * nbytes / 4700.0
 
     def send(to_next, land_next, to_prev, land_prev, guard):
         k = cnts["msg"]; cnts["msg"] += 1
         def emit(g, e):
             g.remote_dma_fused([
-                RemoteDMATransfer(dst_ids=[dn], dma_engine_mask=mn, remote_sem=T.sem["arr%d" % k], src=to_next[0], dst=land_next[0]),
-                RemoteDMATransfer(dst_ids=[dp], dma_engine_mask=mp, remote_sem=T.sem["arr%d" % k], src=to_prev[0], dst=land_prev[0]),
+                RemoteDMATransfer(dst_ids=[dn], dma_engine_mask=mn, remote_sem=T.sem["arr%d" % k], srcs=[x[0] for x in to_next],
+                                  dsts=[land_next[0]], alu_op=int(len(to_next) > 1)),
+                RemoteDMATransfer(dst_ids=[dp], dma_engine_mask=mp, remote_sem=T.sem["arr%d" % k], srcs=[to_prev[0]], dsts=[land_prev[0]]),
             ], local_sem=T.sem["snt%d" % k])
             return None
-        s = add("g", 0.5, [to_next, to_prev], [], emit, "r", COMM - 1.0, ("snt%d" % k, nsig))
+        s = add("g", 0.5, to_next + [to_prev], [], emit, "r", COMM - 2.0 + 0.25 * (len(to_next) - 1), ("snt%d" % k, nsig))
+        ops[s]["occ"] = 1.0
         ops[s]["guard"] = [r for x in guard for r in x[1]]
         add("", 0.0, [], [land_next, land_prev], None, "a", 0.5, ("arr%d" % k, nsig), after=[s])
 
@@ -201,16 +225,18 @@ def plan(T, topo, core, par=PARS[0]):
         return add("g", cost, reads, writes, emit)
 
     ID, IDF = R("id2", 0, 128), R("id2f", 0, 128)
-    SHF, SHB = R("id2", 112, 240), R("id2f", 16, 144)
+    SHF, SHB, TWOF = R("id2", 112, 240), R("id2f", 16, 144), R("id2f", 144, 272)
     PW = [ID] + [R("pw", j * 128, (j + 1) * 128) for j in range(4)]
-    EIGHT, HALF, NEGH = R("pw", 512, 640), R("pw", 640, 768), R("pw", 768, 896)
+    TWO, HALF, NEG, Y0, NEG2, THREE = [R("pw", j * 128, (j + 1) * 128) for j in range(4, 10)]
+    MAGIC = 1.5 * 2.0 ** 26
     XM = [R("xm", 0, 128), R("xm", 128, 256)]
     DM = [R("xm", 256, 384), R("xm", 384, 512)]
-    logn = lambda e: "log%d" % (e % 2)
-    blk = lambda t: (t + 3) * M
+    lg = "log"
+    blk = lambda e, t: (5 - t if e % 2 else 9 + t) * M
+    place = lambda e, d: d - 1 if e % 2 else 4 - d
 
     def fland(e, t):
-        return R(logn(e), blk(t) + V, blk(t) + V + H), R(logn(e), blk(t) + V + H, blk(t) + M)
+        return R(lg, blk(e, t) + V, blk(e, t) + V + H), R(lg, blk(e, t) + V + H, blk(e, t) + M)
 
     def rland(k):
         return R("ret", (k % 2) * 264, (k % 2) * 264 + H), R("ret", (k % 2) * 264 + H, (k % 2) * 264 + 2 * H)
@@ -218,47 +244,51 @@ def plan(T, topo, core, par=PARS[0]):
     fmsg, bmsg = [0], [0]
 
     def wires(e, t):
-        o = (fmsg[0] % 2) * 384; fmsg[0] += 1
-        gat(R("sf", o, o + 256), R(logn(e), blk(t), blk(t) + V), R("snu"), "s" if t else "sv")
-        mm("psW", V, H, [(SHF, "sf", o)])
-        mov(R("sf", o + 256, o + 384), R("psW", V, V + H))
+        o = 0
+        gat(R("sf", o, o + 256), R(lg, blk(e, t), blk(e, t) + V), R("snu"), SP)
+        ps = "psN" if ZP[e] else "psW"
+        mm(ps, V, H, [(SHF, "sf", o)])
+        mov(R("sf", o + 256, o + 384), R(ps, V, V + H))
         a, b = fland(e, t)
         ne, nt = (e, t + 1) if t < 4 else (e + 1, 1)
-        send(R("sf", o + 256, o + 384), a, R("sf", o + H, o + 256), b, list(fland(ne, nt)) if ne < E else [])
+        send([R("sf", o + 256, o + 384)], a, R("sf", o + H, o + 256), b, list(fland(ne, nt)) if ne < E else [])
 
     dma("y", T.dm[:], T.drive[:], [], [R("dr")], 1536)
     dma("a", T.sndi[:], T.snd[:], [], [R("sndi")], 64)
     dma("y", R("srci")[0], T.src[:], [], [R("srci")], 768)
     dma("a", R("dlyi")[0], T.dly[:], [], [R("dlyi")], 768)
     dma("y", T.wq[:], T.w[:], [], [R("wq")], 6144)
-    dma("y", T.ls[:], T.loss[:], [], [R("ls")], 1536)
+    dma("y", T.ls[:, 0:V], T.loss[:], [], [R("ls", 0, V)], 1536)
+    S0 = R(lg, blk(0, 0), blk(0, 0) + V)
     mset(R("ones"), 1.0)
     gop(0.45, [R("ones")], [ID], lambda g, e: g.affine_select(ID[0], T.ones[:, 0:128], [[-1, 128]], A.is_equal, 0.0, 0, 1))
     cp(R("id2", 128, 256), ID)
     cp(R("snu"), R("sndi"))
-    ts(R("log0", blk(0), blk(0) + V), R("dr"), 1.0, None, A.is_ge)
+    ts(S0, R("dr"), 1.0, None, A.is_ge)
     wires(0, 0)
-    mset(R("log0", 0, 3 * M), 0.0)
+    mset(R(lg, 6 * M, 9 * M), 0.0)
     ts(R("wq", 0, 2 * V), R("wq", 0, 2 * V), TINY, None, A.max)
     act(R("wq", 2 * V, KV), R("wq", 2 * V, KV), F.Identity, 1.0, TINY)
     ts(R("ti", 0, L), R("srci"), 1023, None, A.bitwise_and)
     cp(R("cf"), R("ti", 0, L))
-    ts(R("tmp"), R("dlyi"), -1024.0, 4096.0, A.mult, A.add)
-    tt(R("ixf"), R("tmp"), R("cf"), A.add)
+    ts(R("dpt"), R("dlyi"), -1024.0, 4096.0, A.mult, A.add)
+    tt(R("ixf"), R("dpt"), R("cf"), A.add)
     cp(R("ix"), R("ixf"))
-    act(R("rr"), R("dr"), F.Identity, -0.5, 0.5)
-    act(R("cn"), R("log0", blk(0), blk(0) + V), F.Identity, 0.5, 0.0)
-    tt(R("hz0"), R("rr"), R("cn"), A.max)
+    act(R("rr"), R("dr"), F.Identity, -1.0, 1.0)
+    tt(R("hz0"), R("rr"), S0, A.max)
     act(R("f0"), R("dr"), F.Identity, -2.0, 195.0 - 1.0 / 64)
     act(R("dm"), R("dr"), F.Identity, 1.0, -0.5)
     ts(R("f0"), R("f0"), 192.0, 0.5, A.subtract, A.max)
-    act(R("cn"), R("log0", blk(0), blk(0) + V), F.Identity, -8.0, 8.0)
+    act(R("cn"), S0, F.Identity, -8.0, 8.0)
     tt(R("f0"), R("f0"), R("cn"), A.max)
-    mov(R("id2f"), R("id2"))
+    mov(R("id2f", 0, 144), R("id2", 0, 144))
     for j in range(4):
         mov(PW[j + 1], ID, 16.0 ** (j + 1))
-    NEG = EIGHT
-    mov(EIGHT, ID, 8.0 if ZP else -1.0); mov(HALF, ID, 0.5); mov(NEGH, ID, -0.5)
+    for x, c in ((TWO, 2.0), (THREE, 3.0), (NEG2, -2.0), (NEG, -1.0), (HALF, 0.5), (Y0, -8.5 * 16 ** 4)):
+        mov(x, ID, c)
+    for j, c in ((1, -8.5 * 16 ** 2), (2, -8.5)):
+        mov(R("rr", 0, 128), R("id2", j, 128 + j), c)
+        tt(Y0, Y0, R("rr", 0, 128), A.add)
     for e in range(2):
         b = 1 << e
         for r in range(2 * b):
@@ -268,11 +298,19 @@ def plan(T, topo, core, par=PARS[0]):
     gop(0.2, [R("bg", 0, 8)], [R("bg", 8, 16)], lambda g, e: g.affine_select(T.bg[:, 8:16], T.bg[:, 0:8], [[16, 8]], A.is_ge, 0.0, 15, -1))
     mset(R("fm"), 0.0)
     cp(R("fm", 16, 144, 16), R("bg", 8, 16))
-    mset(R("log1", 0, 3 * M), 0.0)
-    mov(R("log1", blk(0), blk(1)), R("log0", blk(0), blk(1)))
+    mov(R(lg, blk(1, 0), blk(1, 0) + M), R(lg, blk(0, 0), blk(0, 0) + M))
     mset(R("mlog", 5 * KV, 5 * KV + 8), 0.0)
+    mset(R("hl", KV, KV + 8), 0.0)
+    mov(TWOF, ID, 2.0)
     mset(R("ret", 256, 264), 0.0); mset(R("ret", 520, 528), 0.0)
     cnts["tag"] = "I"
+    ts(R("ti", 0, L), R("srci"), 10, None, A.arith_shift_right)
+    ts(R("tmp"), R("cf"), 768.0, None, A.is_ge)
+    ts(R("eag"), R("ti", 0, L), -512.0, -1536.0, A.mult, A.add)
+    tt(R("tmp"), R("tmp"), R("eag"), A.mult)
+    ts(R("eag"), R("ti", 0, L), 768.0, 768.0, A.mult, A.add)
+    tt(R("tmp"), R("tmp"), R("eag"), A.add)
+    tt(R("srci"), R("tmp"), R("cf"), A.add)
     ts(R("ti", 0, L), R("srci"), 4, 15, A.arith_shift_right, A.bitwise_and)
     ts(R("ti", L, 2 * L), R("srci"), 15, None, A.bitwise_and)
     ts(R("ti", 2 * L, 3 * L), R("srci"), 8, None, A.arith_shift_right)
@@ -281,8 +319,10 @@ def plan(T, topo, core, par=PARS[0]):
     tt(R("tmp"), R("tmp"), R("eag"), A.add)
     tt(R("tmp"), R("tmp"), R("ti", 2 * L, 3 * L), A.add)
     cp(R("rho"), R("tmp"))
-    gop(0.13 + 2 * KV * CY, [], [R("mlog", KV, 2 * KV)],
-        lambda g, e: g.iota(T.mlog[:, KV:2 * KV], [[1, L], [L, 16]], 0, 0, allow_small_or_imprecise_dtypes=True))
+    gop(0.13 + 2 * V * CY, [], [R("mlog", KV, KV + V)],
+        lambda g, e: g.iota(T.mlog[:, KV:KV + V], [[1, 48], [L, 16]], 0, 0, allow_small_or_imprecise_dtypes=True))
+    for j in range(1, K):
+        act(R("mlog", KV + j * V, KV + (j + 1) * V), R("mlog", KV, KV + V), F.Identity, 1.0, 48.0 * j)
     for j in range(12):
         scat(R("mlog", 0, KV), R("rho", j * 16, j * 16 + 16), R("mlog", KV + j * 256, KV + j * 256 + 256))
     dma("y", T.tf[:, 0:L], T.mlog[0:128:16, 0:KV], [R("mlog", 0, KV)], [R("tf", 0, L)], 6000)
@@ -320,51 +360,76 @@ def plan(T, topo, core, par=PARS[0]):
     slot = {}
 
     def xpart(e, d):
-        mm("psW", 0, M, [(PW[u], logn(e), blk(u)) for u in range(6 - d)])
-        act(R("xw", (4 - d) * M, (5 - d) * M), R("psW"), F.Identity, 16.0 ** d, 0.5)
+        C, o, s = 2.0 ** -21, place(e, d) * M, blk(e, 5 - d)
+        if not XD:
+            a, b, d = (0, M, d) if d > 1 else (0, V, 1) if d else (V, M, 1)
+            mm("psN", a, b - a, [(PW[u], lg, blk(e, u) + a) for u in range(6 - d)])
+            return act(R("xw", place(e, d) * M + a, place(e, d) * M + b), R("psN", a, b), F.Identity, 16.0 ** (d - 5), C)
+        if d == 4:
+            act(R("xw", o, o + M), R(lg, blk(e, 0), blk(e, 0) + M), F.Identity, 1.0 / 16, C)
+        elif d:
+            act(R("xw", o, o + M), R("xw", place(e, d + 1) * M, (place(e, d + 1) + 1) * M), F.Identity, 1.0 / 16, C * 15 / 16)
+        else:
+            o, s = place(e, 1) * M, blk(e, 4)
+            return tt(R("xw", o + V, o + M), R("xw", o + V, o + M), R(lg, s + V, s + M), A.add)
+        x, y = R("xw", o, o + (M if d > 1 else V)), R(lg, s, s + (M if d > 1 else V))
+        dma("g", x[0], y[0], [x, y], [x], 4096, accum_op=A.add)
+
+    def spike(o, i):
+        def emit(g, e):
+            if e == "s":
+                return g.scalar.activation(o[0], i[0], F.Sigmoid, bias=256.0, scale=-2.0 ** 20)
+            return g.vector.tensor_scalar(o[0], i[0], 2.0 ** -12, None, A.is_le)
+        return add(SP, 0.07 + i[3] * CY, [i], [o], emit)
 
     def fstep(e, t):
         s = free.pop(0); slot[e, t] = s
         cnts["tag"] = "F%d%d" % (e, t)
-        lg = logn(e)
         if e < E - 1 and t == 5:
-            xpart(e, 1)
-        win = R(lg, blk(t - 4), blk(t))
+            xpart(e, 0)
+        a = min(blk(e, t - 4), blk(e, t - 1))
+        win = R(lg, a, a + 4 * M)
+        zp = ZP[e] and (t < 5 or ZP[e] > 1)
+        ps, sg = ("psW", NEG2) if zp else ("psN", TWO)
+        if zp:
+            mm("psW", 0, V, ([(ID, "hz0", 0)] if t == 1 else [(IDF, "zz", 0), (ID, lg, blk(e, t - 1))]) + [(NEG2, "dm", 0)], True, False)
+        else:
+            mm("psN", 0, V, [(TWO, "dm", 0)], True, False)
         for k in range(K):
             for a, b in ([(0, V)] if k < K - 1 else CH):
                 o = k * V
                 wx, ix = R("wx", s * KV + o + a, s * KV + o + b), R("ix", (o + a) // 16, (o + b) // 16)
-                if k >= K - XS[e]:
+                if k in XK[XS[e] if t < 5 or e == E - 1 else 0]:
                     gat(wx, win, ix)
                     tt(wx, wx, R("wq", o + a, o + b), A.mult)
                 else:
                     gmul(wx, win, ix, R("wq", o + a, o + b))
-                if k == 0:
-                    mm("psN", 0, V, [(ID, "dm", 0)] + ([(NEGH, lg, blk(t - 1))] if t > 1 and ZP else []), True, False)
-                mm("psN", a, b - a, [(ID, "wx", s * KV + o + a)], False, k == K - 1)
-        hz = "hz0" if t == 1 else "hz"
+                mm(ps, a, b - a, [(sg, "wx", s * KV + o + a)], False, k == K - 1)
         for a, b in CH:
-            if t < 5:
-                tt(R("psW", a, b), R(hz, a, b), R("psN", a, b), A.subtract)
-                i = act(R(lg, blk(t) + a, blk(t) + b), R("psW", a, b), F.Sigmoid, -2.0 ** 20, 256.0)
-                cnts["fn"] = cnts["fn"][-1:] + [i]
-            else:
-                tt(R(lg, blk(t) + a, blk(t) + b), R(hz, a, b), R("psN", a, b), A.is_le)
+            S, hz = R(lg, blk(e, t) + a, blk(e, t) + b), R("hz0" if t == 1 else "zz", a, b)
+            if not zp and (t == 5 or DS[e]):
+                tt(S, hz, R("psN", a, b), A.is_le)
+                continue
+            if not zp:
+                tt(R("psW", a, b), hz, R("psN", a, b), A.subtract)
+            cnts["fn"] = cnts["fn"][-1:] + [spike(S, R("psW", a, b))]
         if t < 5:
             wires(e, t)
-            if ZP:
-                act(R("hz"), R("psW", 0, V), F.Relu, 0.5, 0.0)
-            elif ZD and e > 0:
-                act(R("zz"), R("psW", 0, V), F.Relu)
-                S = R(lg, blk(t), blk(t) + V)
+        if DS[e] and not zp and t < 5:
+            tt(R("psW", 0, V), R("hz0" if t == 1 else "zz"), R("psN", 0, V), A.subtract)
+        if zp:
+            mm("psN", 0, V, [(TWO, "dm", 0)] + [(TWO, "wx", s * KV + k * V) for k in range(K)])
+        if t < 5:
+            S = R(lg, blk(e, t), blk(e, t) + V)
+            if ZP[e] and (t < 4 or ZP[e] > 1):
+                act(R("zz"), R("psW", 0, V), F.Relu, 0.5, 0.0)
+            elif ZD[e]:
+                act(R("zz"), R("psW", 0, V), F.Relu, 0.5, 0.0)
                 dma("g", T.zz[:], S[0], [S, R("zz")], [R("zz")], 3072, accum_op=A.add)
-                mov(R("hz"), R("zz"), 0.5, "s")
             else:
-                tt(R("zz"), R("psW", 0, V), R(lg, blk(t), blk(t) + V), A.max)
-                mov(R("hz"), R("zz"), 0.5, "s")
-        if ZP:
-            mm("psN", 0, V, [(ID, "dm", 0)] + [(ID, "wx", s * KV + k * V) for k in range(K)] + [(EIGHT, lg, blk(t))])
-        act(R("rr"), R("psN", 0, V), F.Identity, -2.0, (210.0 if ZP else 194.0) - 1.0 / 64)
+                act(R("psW", 0, V), R("psW", 0, V), F.Relu, 0.5, 0.0)
+                tt(R("zz"), R("psW", 0, V), S, A.add)
+        act(R("rr"), R("psN", 0, V), F.Identity, -1.0, 194.0 - 1.0 / 64)
         fa = R("fa", s * V, (s + 1) * V)
         if ES and e > 0:
             act(R("rr"), R("rr"), F.Relu, 1.0, -192.5)
@@ -373,13 +438,16 @@ def plan(T, topo, core, par=PARS[0]):
             ts(fa, R("rr"), 192.0, 0.5, A.subtract, A.max)
         if e < E - 1 and 2 <= t < 5:
             xpart(e, 6 - t)
+            if t == 4:
+                xpart(e, 1)
 
     def count(e):
-        lg = logn(e)
-        mm("psN", 0, V, [(ID, lg, blk(u)) for u in range(6)] + ([(ID, "cn", 0)] if e else []))
-        if e < E - 1:
+        if e == 0:
+            mm("psN", 0, V, [(ID, lg, blk(e, u)) for u in range(1, 6)] + [(THREE, lg, blk(e, 0))])
             mov(R("cn"), R("psN", 0, V))
-        else:
+        elif e == E - 1:
+            mm("psN", 0, V, [(ID, lg, blk(1, u)) for u in range(1, 6)], True, False)
+            mm("psN", 0, V, [(ID, lg, blk(e, u)) for u in range(1, 6)] + [(ID, "cn", 0)], False, True)
             mov(R("zz"), R("psN", 0, V))
             dma("y", T.cnt[:], T.zz[:], [R("zz")], [], 3072)
 
@@ -389,40 +457,39 @@ def plan(T, topo, core, par=PARS[0]):
         tt(R(o[0], o[1], o[1] + L), R(a[0], a[1], a[1] + L), R("tmp"), A.add)
 
     def votes(e):
-        lg = logn(e); s = free[0]
+        s = free[0]
         cnts["tag"] = "V%d" % e
-        mm("psW", 0, V, [(PW[5 - u], lg, blk(u)) for u in range(1, 5)], True, False)
-        mm("psW", 0, V, [(PW[0], lg, blk(5))], False, True)
-        act(R("psW", 0, V) if PG else R("zz"), R("psW", 0, V), F.Identity, -2.0 * 16.0 ** -5, sum(16.0 ** -u for u in range(6)))
-        for k in range(K if PG else 0):
-            p = R("mlog", 2 * KV + k * V, 2 * KV + (k + 1) * V)
-            gat(p, R("xw"), R("ix", k * 48, k * 48 + 48))
+        ts(R("dpt"), R("dpt"), -1.0, 3072.0, A.mult, A.add)
+        tt(R("ixf"), R("dpt"), R("cf"), A.add)
+        mm("psW", 0, V, [(Y0, "ones", 0)] + [(PW[5 - u], lg, blk(e, u)) for u in range(1, 5)], True, False)
+        mm("psW", 0, V, [(PW[0], lg, blk(e, 5))], False, True)
+        P0 = 2 * KV
+        for k in range(K):
+            gat(R("mlog", P0 + k * V, P0 + (k + 1) * V), R("xw"), R("ix", k * 48, k * 48 + 48))
+        for k in range(K):
+            p = R("mlog", P0 + k * V, P0 + (k + 1) * V)
             tt(p, R("psW", 0, V), p, A.mult)
         for j in range(6):
-            p = R("pv", (j % 3) * 512, (j % 3 + 1) * 512)
-            a = j * 512
-            if PG:
-                p = R("mlog", 2 * KV + a, 2 * KV + a + 512)
-            while a < (j + 1) * 512 and not PG:
-                b = min((j + 1) * 512, (a // V + 1) * V)
-                o = (j % 3 - j) * 512
-                gmul(R("pv", a + o, b + o), R("xw"), R("ix", a // 16, b // 16), R("zz", a % V, (b - 1) % V + 1))
-                a = b
-            q = R("psN", (j % 2) * 512, (j % 2 + 1) * 512)
-            act(q, p, F.Identity, 1.0, 1.5 * 2.0 ** 27)
-            act(q, q, F.Identity, 1.0, -1.5 * 2.0 ** 27)
-            tt(R("wx", s * KV + j * 512, s * KV + (j + 1) * 512), q, p, A.is_gt)
+            p, q = R("mlog", P0 + j * 512, P0 + (j + 1) * 512), R("psN", (j % 2) * 512, (j % 2 + 1) * 512)
+            if j in VR:
+                ts(q, p, MAGIC, -MAGIC, A.add, A.add)
+            else:
+                act(q, p, F.Identity, 1.0, MAGIC)
+                act(q, q, F.Identity, 1.0, -MAGIC)
+            tt(R("wx", s * KV + j * 512, s * KV + (j + 1) * 512), q, p, A.is_lt)
             if j in (2, 5):
                 c0 = (j - 2) * 32
-                mm("psW", c0, 96, [(R("fm", 16 - i, 144 - i), "wx", s * KV + c0 * 16 + i, 16) for i in range(16)])
-        mm("psW", 768, L, [(DM[e], "cf", 0)])
-        ts(R("eag"), R("psW", 0, L), 9.0, None, A.is_ge)
+                mm("psW", V + c0, 96, [(R("fm", 16 - i, 144 - i), "wx", s * KV + c0 * 16 + i, 16) for i in range(16)])
+            if j == 2:
+                mm("psW", 0, L, [(DM[e], "cf", 0)])
+        ts(R("eag"), R("psW", V, V + L), 9.0, None, A.is_ge)
         mm("psW", 512, L, [(XM[e], "eag", 0)])
-        both = R("both", e * L, (e + 1) * L)
-        tt(both, R("psW", 512, 512 + L), R("eag"), A.mult)
-        tt(R("tmp"), R("psW", 768, 768 + L), both, A.mult)
+        tt(R("tmp"), R("psW", 0, L), R("eag"), A.mult)
+        tt(R("tmp"), R("psW", 512, 512 + L), R("tmp"), A.mult)
         tt(R("ixf"), R("ixf"), R("tmp"), A.add)
         cp(R("ix"), R("ixf"))
+        both = R("both", e * L, (e + 1) * L)
+        tt(both, R("psW", 512, 512 + L), R("eag"), A.mult)
         if e == 0:
             tt(R("cf"), R("cf"), R("tmp"), A.add)
             swap(("val", L), ("val", 0), both, 0)
@@ -431,75 +498,77 @@ def plan(T, topo, core, par=PARS[0]):
             swap(("val", 3 * L), ("val", 2 * L), R("both", 0, L), 0)
 
     def lists(e):
-        j = e % 2
+        j = e % 2 * L
+        x, q, a, b = R("tf", j, j + 48), R("ti", 0, 48), R("lt", 0, 48), R("lt", 48, 96)
+        ts(q, x, 1.0 / KV, -0.4998, A.mult, A.add)
+        ts(a, q, -float(KV), None, A.mult)
+        ts(b, q, float(V), None, A.mult)
+        tt(a, a, x, A.add)
+        cp(R("lw", 240, 288), a)
+        gat(R("wpw"), R("wq"), R("lw", 240, 288))
+        ts(q, a, 1.0 / V, -0.4993, A.mult, A.add)
+        tt(a, a, b, A.add)
+        ts(b, q, -float(V), None, A.mult)
+        tt(a, a, b, A.add)
         for tau in range(4, -1 if e == E - 1 else 0, -1):
-            ts(R("jx", tau * L, (tau + 1) * L), R("tf", j * L, (j + 1) * L), float((5 - tau) * KV), None, A.min)
+            ts(R("lw", tau * 48, tau * 48 + 48), a, float((5 - tau) * V), None, A.min)
+            ts(R("jx", tau * 144, (tau + 1) * 144), R("tf", j + 48, j + L), float((5 - tau) * KV), None, A.min)
 
     nacc = [0]
-    REC = [R("pv", 0, V), R("pv", V, 2 * V), R("val"), R("zz")]
+    REC = [R("hl", j * V, (j + 1) * V) for j in range(K)]
 
     def bstep(e, t):
-        lg = logn(e)
-        S = R(lg, blk(t), blk(t) + V)
-        head = ([] if ZP or t in (0, 5) else [(ID, "ones", 0), (NEG, lg, blk(t))]) + [(HALF, "ls", 0)]
+        head = [(HALF, "ls", 0)] + ([] if t in (0, 5) else [(NEG, lg, blk(e, t))])
         alt = ALT if e == E - 1 else "s"
+        hl = lambda t, a, b: R("xw", (t - 1) * V + a, (t - 1) * V + b) if e == E - 1 else R("hl", (t - 2) * V + a, (t - 2) * V + b)
         cnts["tag"] = "B%d%d" % (e, t)
         if t == 5:
             mm("psP", 0, V, head)
-            cap = S
         else:
             k = bmsg[0]; bmsg[0] += 1
             win = R("mlog", t * KV, 5 * KV + 8)
             for a in range(3):
-                zw, jw = R("z", a * M + V, (a + 1) * M), R("jx", t * L + a * 64 + 48, t * L + (a + 1) * 64)
-                if e < E - 1 or not YW:
-                    gat(zw, win, jw, alt)
-                else:
-                    lx, yw = ("rho", "linv", "ix")[t % 3], R(("rr", "hz0")[t % 2], a * 256, a * 256 + 256)
-                    if a == 0:
-                        ts(R(lx), R("eag"), float((5 - t) * V), None, A.min)
-                    assert slot[e, 5] == 4
-                    gat(yw, R("wx", t * KV, 5 * KV + 16), jw)
-                    gmul(zw, R("xw", t * V, 5 * V + 8), R(lx, a * 64 + 48, (a + 1) * 64), yw)
-                mm("psP", V, H, [(SHB, "z", a * M + V)], a == 0, a == 2)
-                mm("psL", V, H, [(IDF, "z", a * M + V + H)], a == 0, a == 2)
-            o = (k % 2) * 256
-            mov(R("sb", o, o + H), R("psP", V, V + H))
-            mov(R("sb", o + H, o + 256), R("psL", V, V + H))
+                o = a * 256
+                gmul(R("zw", o, o + 256), hl(t + 1, 0, (5 - t) * V + 8), R("lw", t * 48 + a * 16, t * 48 + a * 16 + 16),
+                     R("wpw", o, o + 256))
+                mm("psP", V, H, [(SHB, "zw", o)], a == 0, a == 2)
+                if not FOLD:
+                    mm("psL", V, H, [(IDF, "zw", o + H)], a == 0, a == 2)
+            mov(R("sb", 0, H), R("psP", V, V + H))
+            if not FOLD:
+                mov(R("sb", H, 256), R("psL", V, V + H))
             a0, a1 = rland(k)
-            send(R("sb", o + H, o + 256), a1, R("sb", o, o + H), a0, list(rland(k + 1)))
-            if CP[e]:
-                mov(R("cap"), R("psL", 0, V), 0.5, "s")
-                mm("psL", 0, V, [(ID, lg, blk(t)), (IDF, "cap", 0)])
-                act(R("cap"), R("psL", 0, V), F.Relu, -1.0, 1.0)
-                act(R("cap"), R("cap"), F.Identity, -1.0, 1.0)
-            else:
-                mov(R("psL", 0, V), R("psL", 0, V), 0.5, "s")
-                tt(R("cap"), R("psL", 0, V), S, A.max)
-            cap = R("cap")
+            send([R("zw", o + H, o + 256) for o in (0, 256, 512)] if FOLD else [R("sb", H, 256)], a1, R("sb", 0, H), a0,
+                 list(rland(k + 1)))
+            tt(R("cap"), R("psL", 0, V), R(lg, blk(e, t), blk(e, t) + V), A.max)
             mm("psP", 0, V, head, True, False)
             for a in range(3):
-                zo, jo = R("z", a * M, a * M + V), R("jx", t * L + a * 64, t * L + a * 64 + 48)
+                o = (a % 2) * V if e < GADD else min(a, 1) * V
+                zo, jo = R("z", o, o + V), R("jx", t * 144 + a * 48, t * 144 + a * 48 + 48)
                 if e >= GADD and a == 2:
-                    gmul(zo, win, jo, R("z", M, M + V), A.add)
+                    gmul(zo, win, jo, zo, A.add)
                 else:
                     gat(zo, win, jo, alt)
                 if not (e >= GADD and a == 1):
-                    mm("psP", 0, V, [(IDF, "z", a * M)], False, False)
+                    mm("psP", 0, V, [(TWOF, "z", o)], False, False)
             for a, b in CH[::-1]:
-                gat(R("retg", a, b), R("ret", (k % 2) * 264, (k % 2) * 264 + 264), R("inu", a // 16, b // 16), alt)
+                gat(R("retg", a, b), R("ret", (k % 2) * 264, (k % 2) * 264 + 264), R("inu", a // 16, b // 16), alt,
+                    1.0 if t else 0.0)
                 mm("psP", a, b - a, [(IDF, "retg", a)], False, True)
                 if a == 0:
                     ops[-1]["after"].append(len(ops) - 3)
                     if alt == "s":
                         ops[-2]["after"].append(len(ops) - 4)
         fn, fo = ("f0", 0) if t == 0 else ("fa", slot[e, t] * V)
-        cn, co = (lg, blk(t)) if t == 5 else ("cap", 0)
+        cn, co = (lg, blk(e, t)) if t == 5 else ("cap", 0)
         for a, b in CH[::-1]:
             tt(R("psP", a, b), R("psP", a, b), R(fn, fo + a, fo + b), A.mult)
-            tt(R("psL", a, b), R("psP", a, b), R(cn, co + a, co + b), A.min)
-            if e == E - 1 and t and YW:
-                mov(R("xw", (t - 1) * V + a, (t - 1) * V + b), R("psL", a, b), 1.0, "s")
+            if t:
+                h = hl(t, a, b) if t > 1 or e == E - 1 else R("cap", a, b)
+                tt(h, R("psP", a, b), R(cn, co + a, co + b), A.min)
+                mov(R("psL", a, b), h, 0.5, "s")
+            else:
+                tt(R("psL", a, b), R("psP", a, b), R(cn, co + a, co + b), A.min)
             if UC[e] and a:
                 continue
             if UC[e]:
@@ -527,45 +596,40 @@ def plan(T, topo, core, par=PARS[0]):
                     tt(p, ac, mj, A.add)
                     tt(ac, p, REC[j], A.mult)
                 dma("y", T.gam[:, j * V:(j + 1) * V], ac[0], [ac], [], 3072)
-        elif nacc[0] == 0:
-            dma("y", T.acc[:], mb[0], [mb], [R("acc")], 12288)
         else:
-            dma("g", T.acc[:], mb[0], [mb, R("acc")], [R("acc")], 12288, accum_op=A.add, max_dma_last_dim=6144)
+            cnts["tag"] = "A%d%d" % (e, t)
+            for a in range(0, KV, KV // NA):
+                x, y = R("acc", a, a + KV // NA), R("mlog", (t - 1) * KV + a, (t - 1) * KV + a + KV // NA)
+                if nacc[0] == 0:
+                    dma("y", x[0], y[0], [y], [x], 12288 // NA)
+                else:
+                    dma("g", x[0], y[0], [x, y], [x], 12288 // NA, accum_op=A.add, max_dma_last_dim=6144)
         nacc[0] += 1
 
     for t in range(1, 6):
         fstep(0, t)
     for e in range(E):
-        cnts["tag"] = "C%d" % e
-        count(e)
         if e < E - 1:
             votes(e)
+        cnts["tag"] = "C%d" % e
+        count(e)
         cnts["tag"] = "R%d" % e
         if e == E - 1:
             for fn in (F.Ln, F.Exp):
                 last = cnts["fn"]
                 for j in range(K):
                     x, w, p = REC[j], R("wq", j * V, (j + 1) * V), R(("psN", "psW")[j % 2], 0, V)
-                    i = act(x, w, fn) if fn == F.Ln else act(p, x, fn, -1.0, math.log(2.0))
+                    i = act(x, w, fn) if fn == F.Ln else act(p, x, fn, -1.0, math.log(4.0))
                     ops[i]["after"] += last
                     ops[i]["cost"] += 0.0 if j else 1.9
                     cnts["fn"] = cnts["fn"] + [i]
                     last = [i] + last
                     if fn == F.Exp:
                         tt(x, p, w, A.mult)
-                        act(x, x, F.Identity, -0.5, 2.0)
+                        act(x, x, F.Identity, -0.25, 2.0)
                         tt(x, p, x, A.mult)
-            cnts["tag"] = "L"
-            t2, q = R("tf", 0, L), R("ti", 0, L)
-            ts(q, t2, 1.0 / KV, -0.4998, A.mult, A.add)
-            ts(R("cf"), q, -float(KV), None, A.mult)
-            ts(R("ixf"), q, float(V), None, A.mult)
-            tt(R("cf"), R("cf"), t2, A.add)
-            ts(q, R("cf"), 1.0 / V, -0.4993, A.mult, A.add)
-            tt(R("cf"), R("cf"), R("ixf"), A.add)
-            ts(R("ixf"), q, -float(V), None, A.mult)
-            tt(R("eag"), R("cf"), R("ixf"), A.add)
             mset(R("xw", 5 * V, 5 * V + 8), 0.0)
+        cnts["tag"] = "L%d" % e
         lists(e)
         if e < E - 1:
             tables(R("val", (2 * e + 1) * L, (2 * e + 2) * L), e + 1)
@@ -614,46 +678,73 @@ def order(ops, others=()):
     HOP = 0.12
     prio = [0.0] * n
     for i in range(n - 1, -1, -1):
-        prio[i] = ops[i]["cost"] + ops[i]["lat"] + HOP + max([prio[j] for j in succ[i]], default=0.0)
+        prio[i] = ops[i]["cost"] + ops[i]["lat"] + ops[i]["occ"] + HOP + max([prio[j] for j in succ[i]], default=0.0)
     qof = {"v": "v", "s": "s", "p": "p", "g": "g", "y": "y", "a": "s"}
 
     hop = lambda i, j: HOP if i in raw[j] and not ops[i]["engs"] == ops[j]["engs"] == "p" else 0.0
     fw = [[(j, hop(i, j)) for j in succ[i]] for i in range(n)]
     bw = [[(j, hop(j, i)) for j in sorted(deps[i])] for i in range(n)]
 
-    def place(key, back=False):
-        nxt = bw if back else fw
+    engs, cost, lat, zero = [o["engs"] for o in ops], [o["cost"] for o in ops], [o["lat"] for o in ops], [0.0] * n
+    occ = [o["occ"] for o in ops]
+    both = [a + b for a, b in zip(lat, occ)]
+
+    def place(key, back=False, look=0.5, margin=2.0, bias=0.3):
+        nxt, pre, post = (bw, both, zero) if back else (fw, zero, lat)
+        dma = 0.0
         left = [len(d) for d in (fw if back else bw)]
-        ready_at = [0.0] * n
-        ready = [i for i in range(n) if left[i] == 0]
-        line = {q: [] for q in "vspgy"}
-        eng, fin, st = [None] * n, [0.0] * n, [0.0] * n
-        while ready:
-            i = max(ready, key=lambda x: key[x])
-            ready.remove(i)
-            best, c = None, ops[i]["cost"]
-            for q in (ops[i]["engs"] or "-"):
-                t0, k = ready_at[i] + (ops[i]["lat"] if back else 0.0), 0
-                if q != "-":
-                    ln = line[qof[q]]
-                    k = len(ln)
-                    while k > 0 and ln[k - 1][1] > t0:
-                        k -= 1
-                    while k < len(ln) and ln[k][0] < t0 + c:
-                        t0 = max(t0, ln[k][1]); k += 1
-                if best is None or t0 < best[0] - 1e-9:
-                    best = (t0, q, k)
-            t0, q, k = best
-            if q != "-":
-                line[qof[q]].insert(k, (t0, t0 + c))
-            eng[i], st[i], fin[i] = q, t0, t0 + c + (0.0 if back else ops[i]["lat"])
-            for j, h in nxt[i]:
-                left[j] -= 1
-                if ready_at[j] < fin[i] + h:
-                    ready_at[j] = fin[i] + h
-                if left[j] == 0:
-                    ready.append(j)
-        return eng, st, fin
+        at = [0.0] * n
+        cand, free = {q: [] for q in "vspgy"}, {q: 0.0 for q in "vspgy"}
+        eng, st, fin = [None] * n, [0.0] * n, [0.0] * n
+        done = []
+
+        def ready(j):
+            at[j] += pre[j]
+            for q in engs[j]:
+                cand[qof[q]].append(j)
+            if not engs[j]:
+                eng[j], st[j], fin[j] = "-", at[j], at[j] + post[j]
+                done.append(j)
+        for i in range(n):
+            if left[i] == 0:
+                ready(i)
+        while True:
+            while done:
+                i = done.pop()
+                for j, h in nxt[i]:
+                    left[j] -= 1
+                    if at[j] < fin[i] + h:
+                        at[j] = fin[i] + h
+                    if left[j] == 0:
+                        ready(j)
+            bq, bt = None, 1e18
+            for q, c in cand.items():
+                if c:
+                    t = max(min([at[i] for i in c]), free[q])
+                    if t < bt:
+                        bq, bt = q, t
+            if bq is None:
+                return eng, st, fin
+            now = [i for i in cand[bq] if at[i] <= bt + 1e-9]
+            i = max(now, key=lambda x: key[x])
+            c = cost[i] + occ[i]
+            soon = [j for j in cand[bq] if bt + 1e-9 < at[j] < bt + min(c, look * c + 0.15) and key[j] > key[i] + margin]
+            if soon:
+                j = max(soon, key=lambda x: key[x])
+                fit = [x for x in now if bt + cost[x] <= at[j] + 0.05]
+                i = max(fit, key=lambda x: key[x]) if fit else j
+            if len(engs[i]) > 1 and bq == "v" and free["s"] <= max(bt, at[i]) + bias:
+                if max([x for x in cand["s"] if at[x] <= max(free["s"], at[i]) + 1e-9], key=lambda x: key[x]) == i:
+                    bq = "s"
+            t0 = max(free[bq], at[i])
+            for q in engs[i]:
+                cand[qof[q]].remove(i)
+            eng[i], st[i], fin[i] = (bq if bq in engs[i] else engs[i]), t0, t0 + cost[i] + post[i]
+            free[bq] = t0 + cost[i]
+            if occ[i] and not back:
+                dma = max(dma, free[bq]) + occ[i]
+                fin[i] = dma + lat[i]
+            done.append(i)
 
     if "best" not in KEPT:
         rng = np.random.RandomState(SEED)
@@ -674,19 +765,25 @@ def order(ops, others=()):
                     if q:
                         t = max(t, busy.get(q, 0.0)); busy[q] = t + cost[i]
                     end[i] = t + cost[i] + lat[i]
+                    if occ[i]:
+                        busy["d"] = max(busy.get("d", 0.0), t + cost[i]) + occ[i]
+                        end[i] = busy["d"] + lat[i]
                 tot += max(end) * w
             return tot
-        best = place(prio)
-        top = score(best)
+        best = cur = place(prio)
+        top = now = score(best)
         for it in range(ROUNDS):
             shift = {t: 0.0 for t in tags}
             for t in rng.randint(0, len(tags), 3):
-                shift[tags[t]] = float(rng.normal(0, 4.0))
+                shift[tags[t]] = float(rng.normal(0, 3.0))
             noise = rng.normal(0, 0.3, n) * (it % 2)
-            r = place([best[2][i] + shift[ops[i]["tag"]] + float(noise[i]) for i in range(n)], True)
-            c = place(r[2])
-            if max(c[2]) <= max(best[2]) * 1.02:
+            how = (0.0, 0.5, 1.0)[rng.randint(3)], (0.5, 2.0)[rng.randint(2)], (0.0, 0.3, 1.0)[rng.randint(3)]
+            r = place([cur[2][i] + shift[ops[i]["tag"]] + float(noise[i]) for i in range(n)], True, *how)
+            c = place(r[2], False, *how)
+            if max(c[2]) <= max(cur[2]) * 1.02:
                 v = score(c)
+                if v <= now + 0.01 * (1 - it / ROUNDS):
+                    cur, now = c, v
                 if v <= top:
                     best, top = c, v
         KEPT["best"] = best

@@ -5,33 +5,49 @@ from concourse.mybir import AluOpType as A, ActivationFunctionType as F
 
 V, H, K, M, KV, L = 768, 128, 4, 1024, 3072, 192
 E = 3
+LX = L + 16
 TINY = 2.0 ** -30
 NWX = 6
-ES = False
 XS = [2, 2, 2]
-GADD, FIN = 0, 4
-UC = [False, False, False]
+X5 = [2, 2, 2]
+XK = [(), (3,), (2, 3), (1, 2, 3), (0, 1, 2, 3)]
 SP = "s"
-ZD = [True, True, True]
-VR = ()
-NA = 1
+NA = [1, 1, 4]
 MMS = 2
-XD = True
-FOLD = False
-ZP = [1, 1, 2]
-DS = [0, 0, 0]
-XK = [(), (3,), (2, 3), (1, 2, 3)]
-ZA = [True, True, False]
-ALT = "sv"
-YW = True
+WM = ["l", "l", "l"]
+GF = [1, 1, 1]
+CUT = [True, True, True]
+ALT = ["s", "s", "s"]
+VP = True
+MCUT = [True, True, True]
+GCUT = [True, True, True]
+WCUT = [True, True, True]
+FM = [False, False, False]
+M1 = False
+DEF = True
+CD = True
+TP = 1
+VF = (0, 9)
+TL = True
+FD = True
+PM = [0, 0, 0]
+PCAP = [False, False, False]
+WA = [False, False, True]
+SP2 = ["sv", "sv", "sv"]
+SW = ["sv", "sv", "sv"]
+GB = [-1, -1, 0]
+RET = "ccc"
+X0 = False
+VS = ()
 f32, bf, i32, u16 = "float32", "bfloat16", "int32", "uint16"
 
 SCRATCH = {
     "wq": ("sbuf", [128, KV], bf),
     "wx": ("sbuf", [128, NWX * KV], bf),
-    "mlog": ("sbuf", [128, 5 * KV + 8], f32),
+    "mlp": ("sbuf", [128, 256 + 4 * KV + 264], f32),
+    "hg": ("sbuf", [128, KV + 8], f32),
     "z": ("sbuf", [128, 2 * V], f32),
-    "retg": ("sbuf", [128, V], f32),
+    "inv": ("sbuf", [128, 96], f32),
     "acc": ("sbuf", [128, KV], f32),
     "log": ("sbuf", [128, 15 * M], bf),
     "dpt": ("sbuf", [128, L], f32),
@@ -39,45 +55,45 @@ SCRATCH = {
     "f0": ("sbuf", [128, V], bf),
     "xw": ("sbuf", [128, 4 * M], f32),
     "pint": ("sbuf", [128, 5 * L], i32),
-    "hl": ("sbuf", [128, KV + 8], f32),
+    "hl": ("sbuf", [128, KV], f32),
     "zz": ("sbuf", [128, V], f32),
     "hz0": ("sbuf", [128, V], bf),
-    "rr": ("sbuf", [128, V], bf),
     "cap": ("sbuf", [128, V], f32),
     "dm": ("sbuf", [128, V], bf),
     "ls": ("sbuf", [128, V], bf),
     "ones": ("sbuf", [128, V], bf),
     "cn": ("sbuf", [128, V], bf),
     "ret": ("sbuf", [128, 2 * 264], f32),
+    "inu": ("sbuf", [128, 48], u16),
     "sf": ("sbuf", [128, 384], bf),
     "sb": ("sbuf", [128, 256], f32),
     "id2": ("sbuf", [128, 256], bf),
-    "id2f": ("sbuf", [128, 272], f32),
+    "id2f": ("sbuf", [128, 528], f32),
     "zw": ("sbuf", [128, V], f32),
     "wpw": ("sbuf", [128, V], bf),
     "lt": ("sbuf", [128, 96], f32),
     "lw": ("sbuf", [128, 288], u16),
-    "pw": ("sbuf", [128, 10 * 128], bf),
+    "pw": ("sbuf", [128, 13 * 128], bf),
     "xm": ("sbuf", [128, 4 * 128], f32),
     "fm": ("sbuf", [128, 144], bf),
     "bg": ("sbuf", [128, 16], bf),
     "sndi": ("sbuf", [128, 16], i32),
+    "sns": ("sbuf", [128, 8], i32),
     "pcol": ("sbuf", [128, 8], i32),
     "pcf": ("sbuf", [128, 4], f32),
     "cf": ("sbuf", [128, L], f32),
     "ixf": ("sbuf", [128, L], f32),
     "val": ("sbuf", [128, 4 * L], f32),
-    "tf": ("sbuf", [128, 2 * L], f32),
+    "tf": ("sbuf", [128, 2 * LX], f32),
     "eag": ("sbuf", [128, L], f32),
     "both": ("sbuf", [128, 2 * L], f32),
     "tmp": ("sbuf", [128, L], f32),
     "ix": ("sbuf", [128, L], u16),
     "rho": ("sbuf", [128, L], u16),
-    "linv": ("sbuf", [128, L], u16),
-    "jx": ("sbuf", [128, 5 * 144], u16),
+    "linv": ("sbuf", [128, LX], u16),
+    "jx": ("sbuf", [128, 5 * LX], u16),
     "snu": ("sbuf", [128, 16], u16),
     "snp": ("sbuf", [128, 16], u16),
-    "inu": ("sbuf", [128, 48], u16),
     "psN": ("psum", [128, 1024], f32),
     "psW": ("psum", [128, 1024], f32),
     "psP": ("psum", [128, 1024], f32),
@@ -87,10 +103,11 @@ SEMAPHORES = (["cv", "cs", "cp", "cg"] + ["arr%d" % i for i in range(27)] + ["sn
               + ["dq%d" % i for i in range(80)])
 
 ALIAS = {"ti": ("pint", 0, 3 * L), "srci": ("pint", 3 * L, L), "dlyi": ("pint", 4 * L, L),
-         "dr": ("dm", 0, V)}
-CH = [(0, 512), (512, V)]
-PARS = [(1.2, 1.55, 3.5, 4.0, 0.5), (1.0, 1.4, 3.0, 3.6, 0.42), (1.45, 1.9, 5.0, 4.5, 0.6), (1.2, 1.4, 3.5, 4.0, 0.85)]
-WEIGHTS = [1 / 300.0, 1 / 250.0, 1 / 380.0, 2 / 380.0]
+         "dr": ("dm", 0, V), "rr": ("fa", 5 * V, V), "mlog": ("mlp", 256, 4 * KV + 264)}
+OFF = 128
+CH = [(0, 512 - OFF), (512 - OFF, V)]
+PARS = [(1.25, 1.6, 3.8, 4.0, 0.55, 0.04), (1.0, 1.56, 3.8, 3.4, 0.42, 0.05), (1.0, 1.15, 2.5, 3.8, 0.45, 0.05)]
+WEIGHTS = [0.3 / 285, 0.35 / 230, 0.35 / 222]
 
 
 def plan(T, topo, core, par=PARS[0]):
@@ -106,7 +123,13 @@ def plan(T, topo, core, par=PARS[0]):
     dn, dp = DstId(rid=topo.addr(nxt)[0], pnc=topo.addr(nxt)[1]), DstId(rid=topo.addr(prv)[0], pnc=topo.addr(prv)[1])
     cnts = {"msg": 0, "dq": 0, "tag": "S", "fn": []}
 
+    def bank(name, a):
+        return "ps" + name[2:], (a + OFF) % 1024 if name[1] == "s" else a
+
     def R(name, a=None, b=None, step=None):
+        if name[:2] in ("ps", "pr"):
+            name, c = bank(name, a)
+            a, b = c, c + b - a
         name, off, w = ALIAS.get(name) or (name, 0, T[name].shape[1])
         t = T[name]
         a = off + (0 if a is None else a)
@@ -116,7 +139,12 @@ def plan(T, topo, core, par=PARS[0]):
             return ap, [(name, k, k + 1, True) for k in range(a // 512, (b - 1) // 512 + 1)], True, b - a
         return ap, [(name, a, b, False)], False, (b - a if step is None else (b - a + step - 1) // step)
 
+    def rows(name, a, b):
+        name, off, w = ALIAS.get(name) or (name, 0, 0)
+        return T[name][0:128:16, off + a:off + b]
+
     def add(engs, cost, reads, writes, emit, kind="c", lat=0.0, sem=None, after=()):
+        cost -= par[5] if engs in ("v", "s", "sv") else 0.0
         rd = [r for x in reads for r in x[1]]
         wr = [r for x in writes for r in x[1]]
         ops.append({"ex": [r for r in rd if r[3] and r not in wr], "engs": engs, "cost": cost, "rd": rd, "wr": wr,
@@ -160,14 +188,14 @@ def plan(T, topo, core, par=PARS[0]):
             if plus:
                 return g.vector.tensor_scalar(o[0], win[0].indirect(lst[0]), plus, None, A.add)
             return g.vector.tensor_copy(o[0], win[0].indirect(lst[0]))
-        return add(engs, 0.07 + o[3] * GA * CY, [win, lst], [o], emit)
+        return add(engs, 0.065 + par[5] + o[3] * GA * CY, [win, lst], [o], emit)
 
     def gmul(o, win, lst, b, op=A.mult):
-        return add("v", 0.06 + o[3] * GA * CY, [win, lst, b], [o],
+        return add("v", 0.05 + par[5] + o[3] * GA * CY, [win, lst, b], [o],
                    lambda g, e: g.vector.tensor_tensor(o[0], win[0].indirect(lst[0]), b[0], op))
 
     def scat(win, lst, i):
-        return add("v", 0.06 + i[3] * SC * CY, [lst, i], [win],
+        return add("v", 0.05 + par[5] + i[3] * SC * CY, [lst, i], [win],
                    lambda g, e: g.vector.tensor_copy(win[0].indirect(lst[0]), i[0]))
 
     def mset(o, c):
@@ -178,6 +206,7 @@ def plan(T, topo, core, par=PARS[0]):
             for j in range(0, len(terms), MMS):
                 mm(ps, o0, n, terms[j:j + MMS], start and j == 0, stop and j + MMS >= len(terms))
             return
+        ps, o0 = bank(ps, o0)
         a = o0
         while a < o0 + n:
             b = min(o0 + n, (a // 512 + 1) * 512)
@@ -194,7 +223,7 @@ def plan(T, topo, core, par=PARS[0]):
                 for j, t in enumerate(terms):
                     ins = g.tensor.matmul(T[ps][:, a:b], t[0][0], rhs[j], start and j == 0, stop and j == len(terms) - 1)
                 return ins
-            add("p", c, rd, [R(ps, a, b)], emit)
+            add("p", c, rd, [R("pr" + ps[2:], a, b)], emit)
             a = b
 
     def dma(q, o, i, reads, writes, nbytes, **kw):
@@ -226,8 +255,9 @@ def plan(T, topo, core, par=PARS[0]):
 
     ID, IDF = R("id2", 0, 128), R("id2f", 0, 128)
     SHF, SHB, TWOF = R("id2", 112, 240), R("id2f", 16, 144), R("id2f", 144, 272)
+    NEGF, HALFF = R("id2f", 272, 400), R("id2f", 400, 528)
     PW = [ID] + [R("pw", j * 128, (j + 1) * 128) for j in range(4)]
-    TWO, HALF, NEG, Y0, NEG2, THREE = [R("pw", j * 128, (j + 1) * 128) for j in range(4, 10)]
+    TWO, HALF, NEG, Y0, NEG2, THREE, NMAG, BIG, NBIG = [R("pw", j * 128, (j + 1) * 128) for j in range(4, 13)]
     MAGIC = 1.5 * 2.0 ** 26
     XM = [R("xm", 0, 128), R("xm", 128, 256)]
     DM = [R("xm", 256, 384), R("xm", 384, 512)]
@@ -243,10 +273,13 @@ def plan(T, topo, core, par=PARS[0]):
 
     fmsg, bmsg = [0], [0]
 
-    def wires(e, t):
+    def wires(e, t, ps="psW"):
         o = 0
-        gat(R("sf", o, o + 256), R(lg, blk(e, t), blk(e, t) + V), R("snu"), SP)
-        ps = "psN" if ZP[e] else "psW"
+        if SW[e] == "s":
+            gat(R("sf", o, o + 256), R(lg, blk(e, t), blk(e, t) + V), R("snu"), SP)
+        else:
+            gat(R("sf", 0, H), R(lg, blk(e, t), blk(e, t) + V), R("snu", 0, 8), "s")
+            gat(R("sf", H, 256), R(lg, blk(e, t), blk(e, t) + V), R("snu", 8, 16), SW[e])
         mm(ps, V, H, [(SHF, "sf", o)])
         mov(R("sf", o + 256, o + 384), R(ps, V, V + H))
         a, b = fland(e, t)
@@ -255,6 +288,10 @@ def plan(T, topo, core, par=PARS[0]):
 
     dma("y", T.dm[:], T.drive[:], [], [R("dr")], 1536)
     dma("a", T.sndi[:], T.snd[:], [], [R("sndi")], 64)
+    if FD:
+        for q, (a, b, c) in zip("ya", ((16, 128, 0), (0, 16, 112))):
+            dma(q, T.fa[a:b, 4 * V:5 * V], T.drive[c:c + b - a, :], [], [R("fa", 4 * V + a, 4 * V + b)], 1536)
+            dma(q, T.sns[a:b, :], T.snd[c:c + b - a, 0:8], [], [R("sns", a // 16, a // 16 + 1)], 32)
     dma("y", R("srci")[0], T.src[:], [], [R("srci")], 768)
     dma("a", R("dlyi")[0], T.dly[:], [], [R("dlyi")], 768)
     dma("y", T.wq[:], T.w[:], [], [R("wq")], 6144)
@@ -264,8 +301,15 @@ def plan(T, topo, core, par=PARS[0]):
     gop(0.45, [R("ones")], [ID], lambda g, e: g.affine_select(ID[0], T.ones[:, 0:128], [[-1, 128]], A.is_equal, 0.0, 0, 1))
     cp(R("id2", 128, 256), ID)
     cp(R("snu"), R("sndi"))
+    if FD:
+        cp(R("snp", 0, 8), R("sns"))
+        for x, y, z in ((R("sf", 256, 384), R("fa", 4 * V, 5 * V), R("snp", 0, 8)), (R("sf", H, 256), R("dr"), R("snu", 8, 16))):
+            add("v", 0.05 + par[5] + H * GA * CY, [y, z], [x],
+                lambda g, e, x=x, y=y, z=z: g.vector.tensor_scalar(x[0], y[0].indirect(z[0]), 1.0, None, A.is_ge))
+        send([R("sf", 256, 384)], fland(0, 0)[0], R("sf", H, 256), fland(0, 0)[1], list(fland(0, 1)))
     ts(S0, R("dr"), 1.0, None, A.is_ge)
-    wires(0, 0)
+    if not FD:
+        wires(0, 0)
     mset(R(lg, 6 * M, 9 * M), 0.0)
     ts(R("wq", 0, 2 * V), R("wq", 0, 2 * V), TINY, None, A.max)
     act(R("wq", 2 * V, KV), R("wq", 2 * V, KV), F.Identity, 1.0, TINY)
@@ -281,10 +325,12 @@ def plan(T, topo, core, par=PARS[0]):
     ts(R("f0"), R("f0"), 192.0, 0.5, A.subtract, A.max)
     act(R("cn"), S0, F.Identity, -8.0, 8.0)
     tt(R("f0"), R("f0"), R("cn"), A.max)
+    act(R("f0"), R("f0"), F.Identity, 2.0)
     mov(R("id2f", 0, 144), R("id2", 0, 144))
     for j in range(4):
         mov(PW[j + 1], ID, 16.0 ** (j + 1))
-    for x, c in ((TWO, 2.0), (THREE, 3.0), (NEG2, -2.0), (NEG, -1.0), (HALF, 0.5), (Y0, -8.5 * 16 ** 4)):
+    for x, c in ((TWO, 2.0), (THREE, 3.0), (NEG2, -2.0), (NEG, -1.0), (HALF, 0.5), (Y0, -8.5 * 16 ** 4),
+                 (NMAG, -MAGIC)) + (((BIG, 2.0 ** 24), (NBIG, -2.0 ** 24)) if any(PCAP) else ()):
         mov(x, ID, c)
     for j, c in ((1, -8.5 * 16 ** 2), (2, -8.5)):
         mov(R("rr", 0, 128), R("id2", j, 128 + j), c)
@@ -299,10 +345,13 @@ def plan(T, topo, core, par=PARS[0]):
     mset(R("fm"), 0.0)
     cp(R("fm", 16, 144, 16), R("bg", 8, 16))
     mov(R(lg, blk(1, 0), blk(1, 0) + M), R(lg, blk(0, 0), blk(0, 0) + M))
-    mset(R("mlog", 5 * KV, 5 * KV + 8), 0.0)
-    mset(R("hl", KV, KV + 8), 0.0)
+    mset(R("mlog", 4 * KV, 4 * KV + 264), 0.0)
+    mset(R("hg", KV, KV + 8), 0.0)
     mov(TWOF, ID, 2.0)
-    mset(R("ret", 256, 264), 0.0); mset(R("ret", 520, 528), 0.0)
+    if VS:
+        mov(NEGF, ID, -1.0)
+    if any(PM):
+        mov(HALFF, ID, 0.5)
     cnts["tag"] = "I"
     ts(R("ti", 0, L), R("srci"), 10, None, A.arith_shift_right)
     ts(R("tmp"), R("cf"), 768.0, None, A.is_ge)
@@ -311,22 +360,26 @@ def plan(T, topo, core, par=PARS[0]):
     ts(R("eag"), R("ti", 0, L), 768.0, 768.0, A.mult, A.add)
     tt(R("tmp"), R("tmp"), R("eag"), A.add)
     tt(R("srci"), R("tmp"), R("cf"), A.add)
-    ts(R("ti", 0, L), R("srci"), 4, 15, A.arith_shift_right, A.bitwise_and)
-    ts(R("ti", L, 2 * L), R("srci"), 15, None, A.bitwise_and)
-    ts(R("ti", 2 * L, 3 * L), R("srci"), 8, None, A.arith_shift_right)
-    ts(R("tmp"), R("ti", 0, L), 192.0, None, A.mult)
-    ts(R("eag"), R("ti", L, 2 * L), 12.0, None, A.mult)
+    ts(R("ti", 0, L), R("srci"), 8, None, A.arith_shift_right)
+    ts(R("tmp"), R("ti", 0, L), -3071.0, None, A.mult)
+    ts(R("eag"), R("srci"), 12.0, None, A.mult)
     tt(R("tmp"), R("tmp"), R("eag"), A.add)
-    tt(R("tmp"), R("tmp"), R("ti", 2 * L, 3 * L), A.add)
     cp(R("rho"), R("tmp"))
     gop(0.13 + 2 * V * CY, [], [R("mlog", KV, KV + V)],
-        lambda g, e: g.iota(T.mlog[:, KV:KV + V], [[1, 48], [L, 16]], 0, 0, allow_small_or_imprecise_dtypes=True))
+        lambda g, e: g.iota(R("mlog", KV, KV + V)[0], [[1, 48], [L, 16]], 0, 0, allow_small_or_imprecise_dtypes=True))
     for j in range(1, K):
         act(R("mlog", KV + j * V, KV + (j + 1) * V), R("mlog", KV, KV + V), F.Identity, 1.0, 48.0 * j)
     for j in range(12):
         scat(R("mlog", 0, KV), R("rho", j * 16, j * 16 + 16), R("mlog", KV + j * 256, KV + j * 256 + 256))
-    dma("y", T.tf[:, 0:L], T.mlog[0:128:16, 0:KV], [R("mlog", 0, KV)], [R("tf", 0, L)], 6000)
-    cp(R("linv"), R("tf", 0, L))
+    ts(R("ti", L, L + 16), R("sndi"), 8, None, A.arith_shift_right)
+    ts(R("lt", 0, 16), R("ti", L, L + 16), -3071.0, 9.0, A.mult, A.add)
+    ts(R("lt", 16, 32), R("sndi"), 12.0, None, A.mult)
+    tt(R("lt", 0, 16), R("lt", 0, 16), R("lt", 16, 32), A.add)
+    cp(R("lw", 0, 16), R("lt", 0, 16))
+    gat(R("zz", 0, 256), R("mlog", 0, KV), R("lw", 0, 16))
+    dma("y", T.tf[:, 0:L], rows("mlog", 0, KV), [R("mlog", 0, KV)], [R("tf", 0, L)], 6000)
+    dma("a", T.tf[:, L:LX], rows("zz", 0, 256), [R("zz", 0, 256)], [R("tf", L, LX)], 600)
+    cp(R("linv"), R("tf", 0, LX))
     gop(0.2, [], [R("pcol", 0, 1)], lambda g, e: g.iota(T.pcol[:, 0:1], [[1, 1]], 0, 1))
     ts(R("pcol", 4, 5), R("pcol", 0, 1), 15, None, A.bitwise_and)
     cp(R("pcf", 0, 1), R("pcol", 4, 5))
@@ -337,11 +390,14 @@ def plan(T, topo, core, par=PARS[0]):
 
     def tables(s, e):
         cnts["tag"] = "T%d" % e
-        dma("y", T.mlog[0:128:16, 0:KV], s[0], [s], [R("mlog", 0, KV)], 6000)
+        a, b, c = (("mlog", "mlog", KV), ("hl", "mlog", 2 * KV) if TL else ("hl", "xw", 0), ("hl", "xw", 0))[e]
+        dma("y", rows(a, 0, KV), s[0], [s], [R(a, 0, KV)], 6000)
         for j in range(4):
-            gat(R("mlog", KV + j * V, KV + (j + 1) * V), R("mlog", 0, KV), R("linv", j * 48, j * 48 + 48))
-        o = R("tf", e % 2 * L, (e % 2 + 1) * L)
-        dma("y", o[0], T.mlog[0:128:16, KV:2 * KV], [R("mlog", KV, 2 * KV)], [o], 6000)
+            gat(R(b, c + j * V, c + (j + 1) * V), R(a, 0, KV), R("linv", j * 48, j * 48 + 48))
+        gat(R("zz", 0, 256), R(a, 0, KV), R("linv", L, LX))
+        j = e % 2 * LX
+        dma("y", T.tf[:, j:j + L], rows(b, c, c + KV), [R(b, c, c + KV)], [R("tf", j, j + L)], 6000)
+        dma("a", T.tf[:, j + L:j + LX], rows("zz", 0, 256), [R("zz", 0, 256)], [R("tf", j + L, j + LX)], 600)
     tables(R("val", 0, L), 0)
     cnts["tag"] = "J"
     ts(R("ti", 0, 16), R("sndi"), 15, None, A.bitwise_and)
@@ -349,33 +405,35 @@ def plan(T, topo, core, par=PARS[0]):
     ts(R("tmp", 0, 16), R("ti", 0, 16), 48.0, None, A.mult)
     tt(R("tmp", 0, 16), R("tmp", 0, 16), R("ti", 16, 32), A.add)
     cp(R("snp"), R("tmp", 0, 16))
-    gop(0.7, [], [R("retg", 0, 256)],
-        lambda g, e: g.iota(T.retg[:, 0:256], [[1, 256]], 0, 0, allow_small_or_imprecise_dtypes=True))
+    gop(0.7, [], [R("z", 0, 256)],
+        lambda g, e: g.iota(T.z[:, 0:256], [[1, 256]], 0, 0, allow_small_or_imprecise_dtypes=True))
     mset(R("cap"), 256.0)
-    scat(R("cap"), R("snp"), R("retg", 0, 256))
-    dma("y", T.tmp[:, 0:48], T.cap[0:128:16, :], [R("cap")], [R("tmp", 0, 48)], 1500)
-    cp(R("inu"), R("tmp", 0, 48))
+    scat(R("cap"), R("snp"), R("z", 0, 256))
+    dma("y", T.inv[:, 0:48], T.cap[0:128:16, :], [R("cap")], [R("inv", 0, 48)], 1500)
+    ts(R("inv", 48, 96), R("inv", 0, 48), 256.0, None, A.is_ge)
+    if "g" in RET:
+        cp(R("inu"), R("inv", 0, 48))
+        mset(R("ret", 256, 264), 0.0); mset(R("ret", 520, 528), 0.0)
 
     free = list(range(NWX))
     slot = {}
 
     def xpart(e, d):
         C, o, s = 2.0 ** -21, place(e, d) * M, blk(e, 5 - d)
-        if not XD:
-            a, b, d = (0, M, d) if d > 1 else (0, V, 1) if d else (V, M, 1)
-            mm("psN", a, b - a, [(PW[u], lg, blk(e, u) + a) for u in range(6 - d)])
-            return act(R("xw", place(e, d) * M + a, place(e, d) * M + b), R("psN", a, b), F.Identity, 16.0 ** (d - 5), C)
         if d == 4:
             act(R("xw", o, o + M), R(lg, blk(e, 0), blk(e, 0) + M), F.Identity, 1.0 / 16, C)
         elif d:
-            act(R("xw", o, o + M), R("xw", place(e, d + 1) * M, (place(e, d + 1) + 1) * M), F.Identity, 1.0 / 16, C * 15 / 16)
+            for a, b in ([(0, V), (V, M)] if d == 1 else [(0, M)]):
+                act(R("xw", o + a, o + b), R("xw", place(e, d + 1) * M + a, place(e, d + 1) * M + b), F.Identity, 1.0 / 16, C * 15 / 16)
         else:
             o, s = place(e, 1) * M, blk(e, 4)
-            return tt(R("xw", o + V, o + M), R("xw", o + V, o + M), R(lg, s + V, s + M), A.add)
-        x, y = R("xw", o, o + (M if d > 1 else V)), R(lg, s, s + (M if d > 1 else V))
-        dma("g", x[0], y[0], [x, y], [x], 4096, accum_op=A.add)
+            x, y = R("xw", o + V, o + M), R(lg, s + V, s + M)
+            return dma("g", x[0], y[0], [x, y], [x], 1024, accum_op=A.add) if X0 else tt(x, x, y, A.add)
+        for a, b in ([(0, M)] if d > 2 else [(0, V), (V, M)][:d]):
+            x, y = R("xw", o + a, o + b), R(lg, s + a, s + b)
+            dma("g", x[0], y[0], [x, y], [x], 4 * (b - a), accum_op=A.add)
 
-    def spike(o, i):
+    def spike(o, i, SP):
         def emit(g, e):
             if e == "s":
                 return g.scalar.activation(o[0], i[0], F.Sigmoid, bias=256.0, scale=-2.0 ** 20)
@@ -389,71 +447,72 @@ def plan(T, topo, core, par=PARS[0]):
             xpart(e, 0)
         a = min(blk(e, t - 4), blk(e, t - 1))
         win = R(lg, a, a + 4 * M)
-        zp = ZP[e] and (t < 5 or ZP[e] > 1)
-        ps, sg = ("psW", NEG2) if zp else ("psN", TWO)
+        zp = t < 5 or e == E - 1
+        pw, pn = ("psN", "psW") if t % 2 and zp else ("psW", "psN")
+        ps, sg = (pw, NEG2) if zp else (pn, TWO)
         if zp:
-            mm("psW", 0, V, ([(ID, "hz0", 0)] if t == 1 else [(IDF, "zz", 0), (ID, lg, blk(e, t - 1))]) + [(NEG2, "dm", 0)], True, False)
+            if t > 1:
+                mm(pw, 0, V, [(ID, "dm", 0)], True, False)
+                act(R(pw, 0, V), R(pn, 0, V), F.Relu, 0.5, 0.0)
+            mm(pw, 0, V, [(ID, "hz0", 0) if t == 1 else (ID, lg, blk(e, t - 1)), (NEG2, "dm", 0)], t == 1, False)
         else:
             mm("psN", 0, V, [(TWO, "dm", 0)], True, False)
+        xk = XK[XS[e] if t < 5 else X5[e]]
         for k in range(K):
             for a, b in ([(0, V)] if k < K - 1 else CH):
                 o = k * V
                 wx, ix = R("wx", s * KV + o + a, s * KV + o + b), R("ix", (o + a) // 16, (o + b) // 16)
-                if k in XK[XS[e] if t < 5 or e == E - 1 else 0]:
+                if k in xk:
                     gat(wx, win, ix)
                     tt(wx, wx, R("wq", o + a, o + b), A.mult)
+                elif FM[e] and k < 2 and 1 not in xk:
+                    if k == 0:
+                        gmul(R("wx", s * KV, s * KV + 2 * V), win, R("ix", 0, 96), R("wq", 0, 2 * V))
                 else:
                     gmul(wx, win, ix, R("wq", o + a, o + b))
                 mm(ps, a, b - a, [(sg, "wx", s * KV + o + a)], False, k == K - 1)
         for a, b in CH:
             S, hz = R(lg, blk(e, t) + a, blk(e, t) + b), R("hz0" if t == 1 else "zz", a, b)
-            if not zp and (t == 5 or DS[e]):
+            if not zp:
                 tt(S, hz, R("psN", a, b), A.is_le)
                 continue
-            if not zp:
-                tt(R("psW", a, b), hz, R("psN", a, b), A.subtract)
-            cnts["fn"] = cnts["fn"][-1:] + [spike(S, R("psW", a, b))]
+            cnts["fn"] = cnts["fn"][-1:] + [spike(S, R(pw, a, b), SP2[e] if a else "s")]
         if t < 5:
-            wires(e, t)
-        if DS[e] and not zp and t < 5:
-            tt(R("psW", 0, V), R("hz0" if t == 1 else "zz"), R("psN", 0, V), A.subtract)
+            wires(e, t, pw)
         if zp:
-            mm("psN", 0, V, [(TWO, "dm", 0)] + [(TWO, "wx", s * KV + k * V) for k in range(K)])
-        if t < 5:
+            mm(pn, 0, V, [(TWO, "dm", 0)] + [(TWO, "wx", s * KV + k * V) for k in range(K)])
+        if t == 4 and e < E - 1:
             S = R(lg, blk(e, t), blk(e, t) + V)
-            if ZP[e] and (t < 4 or ZP[e] > 1):
-                act(R("zz"), R("psW", 0, V), F.Relu, 0.5, 0.0)
-            elif ZD[e]:
-                act(R("zz"), R("psW", 0, V), F.Relu, 0.5, 0.0)
-                dma("g", T.zz[:], S[0], [S, R("zz")], [R("zz")], 3072, accum_op=A.add)
-            else:
-                act(R("psW", 0, V), R("psW", 0, V), F.Relu, 0.5, 0.0)
-                tt(R("zz"), R("psW", 0, V), S, A.add)
-        act(R("rr"), R("psN", 0, V), F.Identity, -1.0, 194.0 - 1.0 / 64)
+            act(R("zz"), R(pw, 0, V), F.Relu, 0.5, 0.0)
+            dma("g", T.zz[:], S[0], [S, R("zz")], [R("zz")], 3072, accum_op=A.add)
         fa = R("fa", s * V, (s + 1) * V)
-        if ES and e > 0:
-            act(R("rr"), R("rr"), F.Relu, 1.0, -192.5)
-            act(fa, R("rr"), F.Identity, 1.0, 0.5)
-        else:
-            ts(fa, R("rr"), 192.0, 0.5, A.subtract, A.max)
+        act(fa, R(pn, 0, V), F.Identity, -1.0, 194.0 - 1.0 / 64)
+        ts(fa, fa, 192.0, 0.5, A.subtract, A.max)
         if e < E - 1 and 2 <= t < 5:
             xpart(e, 6 - t)
             if t == 4:
                 xpart(e, 1)
 
     def count(e):
-        if e == 0:
-            mm("psN", 0, V, [(ID, lg, blk(e, u)) for u in range(1, 6)] + [(THREE, lg, blk(e, 0))])
+        if e == 0 and CD:
+            for u in range(1, 6):
+                x, y = R("cn"), R(lg, blk(e, u), blk(e, u) + V)
+                if u == 1:
+                    dma("y", x[0], y[0], [y], [x], 1536)
+                else:
+                    dma("g", x[0], y[0], [x, y], [x], 1536, accum_op=A.add)
+        elif e == 0:
+            mm("psN", 0, V, [(ID, lg, blk(e, u)) for u in range(1, 6)])
             mov(R("cn"), R("psN", 0, V))
         elif e == E - 1:
-            mm("psN", 0, V, [(ID, lg, blk(1, u)) for u in range(1, 6)], True, False)
+            mm("psN", 0, V, [(ID, lg, blk(1, u)) for u in range(1, 6)] + [(THREE, lg, blk(e, 0))], True, False)
             mm("psN", 0, V, [(ID, lg, blk(e, u)) for u in range(1, 6)] + [(ID, "cn", 0)], False, True)
-            mov(R("zz"), R("psN", 0, V))
+            mov(R("zz"), R("psN", 0, V), 1.0, "s")
             dma("y", T.cnt[:], T.zz[:], [R("zz")], [], 3072)
 
     def swap(o, a, both, e):
-        mm("psW", 512, L, [(DM[e], a[0], a[1])])
-        tt(R("tmp"), R("psW", 512, 512 + L), both, A.mult)
+        mm("prW", 512, L, [(DM[e], a[0], a[1])])
+        tt(R("tmp"), R("prW", 512, 512 + L), both, A.mult)
         tt(R(o[0], o[1], o[1] + L), R(a[0], a[1], a[1] + L), R("tmp"), A.add)
 
     def votes(e):
@@ -463,33 +522,41 @@ def plan(T, topo, core, par=PARS[0]):
         tt(R("ixf"), R("dpt"), R("cf"), A.add)
         mm("psW", 0, V, [(Y0, "ones", 0)] + [(PW[5 - u], lg, blk(e, u)) for u in range(1, 5)], True, False)
         mm("psW", 0, V, [(PW[0], lg, blk(e, 5))], False, True)
-        P0 = 2 * KV
         for k in range(K):
-            gat(R("mlog", P0 + k * V, P0 + (k + 1) * V), R("xw"), R("ix", k * 48, k * 48 + 48))
+            gat(R("hl", k * V, (k + 1) * V), R("xw"), R("ix", k * 48, k * 48 + 48))
         for k in range(K):
-            p = R("mlog", P0 + k * V, P0 + (k + 1) * V)
+            p = R("hl", k * V, (k + 1) * V)
             tt(p, R("psW", 0, V), p, A.mult)
         for j in range(6):
-            p, q = R("mlog", P0 + j * 512, P0 + (j + 1) * 512), R("psN", (j % 2) * 512, (j % 2 + 1) * 512)
-            if j in VR:
-                ts(q, p, MAGIC, -MAGIC, A.add, A.add)
+            a = j % 2 * 512
+            p, q, vote = R("hl", j * 512, (j + 1) * 512), R("prN", a, a + 512), R("wx", s * KV + j * 512, s * KV + (j + 1) * 512)
+            if VP:
+                mm("prN", a, 512, [(NMAG, "ones", 0)], True, False)
+            act(q, p, F.Identity, 1.0, MAGIC)
+            if j in VS:
+                mm("prN", a, 512, [(NMAG, "ones", 0), (NEGF, "hl", j * 512)], False, True)
+                act(vote, q, F.Sigmoid, -2.0 ** 20)
             else:
-                act(q, p, F.Identity, 1.0, MAGIC)
-                act(q, q, F.Identity, 1.0, -MAGIC)
-            tt(R("wx", s * KV + j * 512, s * KV + (j + 1) * 512), q, p, A.is_lt)
+                if VP:
+                    mm("prN", a, 512, [(NMAG, "ones", 0)], False, True)
+                else:
+                    act(q, q, F.Identity, 1.0, -MAGIC)
+                cnts["vote"] = [tt(vote, q, p, A.is_lt)]
             if j in (2, 5):
                 c0 = (j - 2) * 32
-                mm("psW", V + c0, 96, [(R("fm", 16 - i, 144 - i), "wx", s * KV + c0 * 16 + i, 16) for i in range(16)])
+                mm("prW", V + c0, 96, [(R("fm", 16 - i, 144 - i), "wx", s * KV + c0 * 16 + i, 16) for i in range(16)])
             if j == 2:
-                mm("psW", 0, L, [(DM[e], "cf", 0)])
-        ts(R("eag"), R("psW", V, V + L), 9.0, None, A.is_ge)
-        mm("psW", 512, L, [(XM[e], "eag", 0)])
-        tt(R("tmp"), R("psW", 0, L), R("eag"), A.mult)
-        tt(R("tmp"), R("psW", 512, 512 + L), R("tmp"), A.mult)
+                mm("prW", 0, L, [(DM[e], "cf", 0)])
+        x, y = R("eag"), R("prW", V, V + L)
+        add("sv", 0.07 + L * CY, [y], [x], lambda g, q: g.vector.tensor_scalar(x[0], y[0], 9.0, None, A.is_ge) if q == "v"
+            else g.scalar.activation(x[0], y[0], F.Sigmoid, bias=-8704.0, scale=1024.0))
+        mm("prW", 512, L, [(XM[e], "eag", 0)])
+        tt(R("tmp"), R("prW", 0, L), R("eag"), A.mult)
+        tt(R("tmp"), R("prW", 512, 512 + L), R("tmp"), A.mult)
         tt(R("ixf"), R("ixf"), R("tmp"), A.add)
-        cp(R("ix"), R("ixf"))
+        cnts["vote"].append(cp(R("ix"), R("ixf")))
         both = R("both", e * L, (e + 1) * L)
-        tt(both, R("psW", 512, 512 + L), R("eag"), A.mult)
+        tt(both, R("prW", 512, 512 + L), R("eag"), A.mult)
         if e == 0:
             tt(R("cf"), R("cf"), R("tmp"), A.add)
             swap(("val", L), ("val", 0), both, 0)
@@ -498,113 +565,183 @@ def plan(T, topo, core, par=PARS[0]):
             swap(("val", 3 * L), ("val", 2 * L), R("both", 0, L), 0)
 
     def lists(e):
-        j = e % 2 * L
+        j = e % 2 * LX
+        c = 48 if WM[e] == "l" else 0
+
+        def wired(x):
+            if RET[e] == "g":
+                return
+            tt(x, x, R("inv", 48, 96), A.mult)
+            tt(x, x, R("inv", 0, 48), A.add)
+        if e == E - 1:
+            y = R("tf", LX - j, 2 * LX - j)
+            ts(y, R("tf", j, j + LX), float(KV), float(4 * KV), A.is_lt, A.mult)
+            tt(y, y, R("tf", j, j + LX), A.add)
+            ts(y, y, -float(KV), None, A.add)
+            wired(R("tf", LX - j + 144, LX - j + L))
+            cp(R("jx", 0, LX), y)
+        wired(R("tf", j + 144, j + L))
+        for tau in range(4, 0, -1):
+            ts(R("jx", tau * LX + c, (tau + 1) * LX), R("tf", j + c, j + LX), float((5 - tau) * KV + 256), None, A.min)
+        if not c:
+            return
         x, q, a, b = R("tf", j, j + 48), R("ti", 0, 48), R("lt", 0, 48), R("lt", 48, 96)
         ts(q, x, 1.0 / KV, -0.4998, A.mult, A.add)
         ts(a, q, -float(KV), None, A.mult)
         ts(b, q, float(V), None, A.mult)
         tt(a, a, x, A.add)
         cp(R("lw", 240, 288), a)
-        gat(R("wpw"), R("wq"), R("lw", 240, 288))
+        x, y, z = R("wpw"), R("wq"), R("lw", 240, 288)
+        add("s", 0.065 + par[5] + V * GA * CY, [y, z], [x], lambda g, q: g.scalar.activation(x[0], y[0].indirect(z[0]), F.Identity, scale=0.5))
         ts(q, a, 1.0 / V, -0.4993, A.mult, A.add)
         tt(a, a, b, A.add)
         ts(b, q, -float(V), None, A.mult)
         tt(a, a, b, A.add)
         for tau in range(4, -1 if e == E - 1 else 0, -1):
             ts(R("lw", tau * 48, tau * 48 + 48), a, float((5 - tau) * V), None, A.min)
-            ts(R("jx", tau * 144, (tau + 1) * 144), R("tf", j + 48, j + L), float((5 - tau) * KV), None, A.min)
 
     nacc = [0]
     REC = [R("hl", j * V, (j + 1) * V) for j in range(K)]
 
     def bstep(e, t):
         head = [(HALF, "ls", 0)] + ([] if t in (0, 5) else [(NEG, lg, blk(e, t))])
-        alt = ALT if e == E - 1 else "s"
-        hl = lambda t, a, b: R("xw", (t - 1) * V + a, (t - 1) * V + b) if e == E - 1 else R("hl", (t - 2) * V + a, (t - 2) * V + b)
+        alt, one = ALT[e], TWOF
+        hl = lambda t, a, b: R("xw", (t - 1) * V + a, (t - 1) * V + b) if e == E - 1 else R("hg", (t - 2) * V + a, (t - 2) * V + b)
+        m0 = ((t - 2) % 4 if e == E - 1 else abs(t - 2)) * KV
         cnts["tag"] = "B%d%d" % (e, t)
         if t == 5:
             mm("psP", 0, V, head)
         else:
+            if t and PCAP[e]:
+                mm("psL", 0, V, [(ID, lg, blk(e, t))], True, False)
+                act(R("psL", 0, V), hl(t + 1, 0, V), F.Identity, 0.5)
+                mm("psL", 0, V, [(x, lg, blk(e, t)) for x in (BIG, NBIG, ID)], False, True)
+            elif t:
+                tt(R("cap"), R("psL", 0, V), R(lg, blk(e, t), blk(e, t) + V), A.max)
+            else:
+                act(R("hz0"), R(lg, blk(e, 0), blk(e, 0) + V), F.Identity, 2.0)
+                act(R("psP", 0, V), hl(1, 0, V))
+                tt(R("cap"), R("psP", 0, V), R("hz0"), A.max)
             k = bmsg[0]; bmsg[0] += 1
-            win = R("mlog", t * KV, 5 * KV + 8)
-            for a in range(3):
-                o = a * 256
-                gmul(R("zw", o, o + 256), hl(t + 1, 0, (5 - t) * V + 8), R("lw", t * 48 + a * 16, t * 48 + a * 16 + 16),
-                     R("wpw", o, o + 256))
-                mm("psP", V, H, [(SHB, "zw", o)], a == 0, a == 2)
-                if not FOLD:
-                    mm("psL", V, H, [(IDF, "zw", o + H)], a == 0, a == 2)
-            mov(R("sb", 0, H), R("psP", V, V + H))
-            if not FOLD:
-                mov(R("sb", H, 256), R("psL", V, V + H))
+            w0 = max(t - 1, 0) * KV
+            win = R("mlog", w0, 4 * KV + 264)
+            jw = lambda a, n: R("jx", t * LX + a * 16, t * LX + (a + n) * 16)
+            if WM[e] == "v":
+                zw = R("zw", 0, 256)
+                gat(zw, win, jw(0, 1), alt)
+                gmul(zw, win, jw(1, 1), zw, A.add)
+                gmul(zw, win, jw(2, 1), zw, A.add)
+                mm("psP", V, H, [(SHB, "zw", 0)])
+                mov(R("sb", 0, H), R("psP", V, V + H))
+                out = R("zw", H, 256)
+            else:
+                if WM[e] == "p":
+                    gat(R("zw"), win, jw(0, 3), alt)
+                for a in range(3):
+                    o = a * 256
+                    c = 1 if WCUT[e] else 3
+                    if WM[e] == "l" and a % c == 0:
+                        gmul(R("zw", o, o + 256 * c), hl(t + 1, 0, (5 - t) * V + 8),
+                             R("lw", t * 48 + a * 16, t * 48 + (a + c) * 16), R("wpw", o, o + 256 * c))
+                    mm("psP", V, H, [(SHB, "zw", o)], a == 0, (WA[e] or OFF > 0) and a == 2)
+                    if not WA[e]:
+                        mm("psP", V + H, H, [(IDF, "zw", o + H)], OFF > 0 and a == 0, a == 2)
+                    elif a:
+                        tt(R("sb", H, 256), R("zw", o + H, o + 256), R("zw" if a == 1 else "sb", H, 256), A.add)
+                c = H if WA[e] or OFF else 256
+                mov(R("sb", 0, c), R("psP", V, V + c))
+                if OFF and not WA[e]:
+                    mov(R("sb", H, 256), R("psP", V + H, V + 256))
+                out = R("sb", H, 256)
             a0, a1 = rland(k)
-            send([R("zw", o + H, o + 256) for o in (0, 256, 512)] if FOLD else [R("sb", H, 256)], a1, R("sb", 0, H), a0,
-                 list(rland(k + 1)))
-            tt(R("cap"), R("psL", 0, V), R(lg, blk(e, t), blk(e, t) + V), A.max)
+            send([out], a1, R("sb", 0, H), a0, list(rland(k + 1)))
             mm("psP", 0, V, head, True, False)
             for a in range(3):
-                o = (a % 2) * V if e < GADD else min(a, 1) * V
-                zo, jo = R("z", o, o + V), R("jx", t * 144 + a * 48, t * 144 + a * 48 + 48)
-                if e >= GADD and a == 2:
-                    gmul(zo, win, jo, zo, A.add)
-                else:
-                    gat(zo, win, jo, alt)
-                if not (e >= GADD and a == 1):
-                    mm("psP", 0, V, [(TWOF, "z", o)], False, False)
-            for a, b in CH[::-1]:
-                gat(R("retg", a, b), R("ret", (k % 2) * 264, (k % 2) * 264 + 264), R("inu", a // 16, b // 16), alt,
-                    1.0 if t else 0.0)
-                mm("psP", a, b - a, [(IDF, "retg", a)], False, True)
-                if a == 0:
-                    ops[-1]["after"].append(len(ops) - 3)
-                    if alt == "s":
-                        ops[-2]["after"].append(len(ops) - 4)
+                if a == 2 and RET[e] == "c":
+                    gmul(R("mlog", w0 - 256, w0), win, jw(12, 1), R("ret", k % 2 * 264, k % 2 * 264 + 256), A.add)
+                    win = R("mlog", w0 - 256, 4 * KV + 264)
+                for x, y in (CH[::-1] if GCUT[e] else [(0, V)]):
+                    gf = GF[e] + (GB[e] if x else 0)
+                    zb, o = ("zw", 0) if a == 2 and gf == 0 else ("z", min(a, 2 - gf) * V)
+                    zo, jo = R(zb, o + x, o + y), R("jx", t * LX + 48 + a * 48 + x // 16, t * LX + 48 + a * 48 + y // 16)
+                    if a > 2 - gf:
+                        gmul(zo, win, jo, zo, A.add)
+                    else:
+                        gat(zo, win, jo, alt, 0.5 if t and a == 0 else 0.0)
+                    if a == 2 or a < 2 - gf:
+                        mm("psP", x, y - x, [(one, zb, o + x)], False, a == 2 and RET[e] == "c")
+            for x, y in (CH[::-1] if RET[e] == "g" else []):
+                gat(R("hg", x, y), R("ret", k % 2 * 264, k % 2 * 264 + 264), R("inu", x // 16, y // 16), "sv")
+                mm("psP", x, y - x, [(one, "hg", x)], False, True)
         fn, fo = ("f0", 0) if t == 0 else ("fa", slot[e, t] * V)
-        cn, co = (lg, blk(e, t)) if t == 5 else ("cap", 0)
-        for a, b in CH[::-1]:
-            tt(R("psP", a, b), R("psP", a, b), R(fn, fo + a, fo + b), A.mult)
-            if t:
-                h = hl(t, a, b) if t > 1 or e == E - 1 else R("cap", a, b)
-                tt(h, R("psP", a, b), R(cn, co + a, co + b), A.min)
-                mov(R("psL", a, b), h, 0.5, "s")
-            else:
-                tt(R("psL", a, b), R("psP", a, b), R(cn, co + a, co + b), A.min)
-            if UC[e] and a:
+        for a, b in (CH[::-1] if CUT[e] else [(0, V)]):
+            pc = 0 < t < 5 and PCAP[e]
+            tt(R("cap" if pc else "psP", a, b), R("psP", a, b), R(fn, fo + a, fo + b), A.mult)
+            h = hl(t, a, b) if t > 1 or t and e == E - 1 else hl(3, a, b) if t else R("cap", a, b)
+            tt(h, R("psL" if pc else "psP", a, b), R(lg, blk(e, t) + a, blk(e, t) + b) if t == 5 else R("cap", a, b), A.min)
+            if t == 0:
+                dma("y", T.lam[:, a:b], T.cap[:, a:b], [R("cap", a, b)], [], 4 * (b - a))
                 continue
-            if UC[e]:
+            pl = "psW" if DEF and (e, t) == (E - 2, 1) else "psL"
+            if PM[e] and (a or PM[e] > 1):
+                i = mm(pl, a, b - a, [(HALFF, h[1][0][0], h[1][0][1])])
+            else:
+                i = mov(R(pl, a, b), h, 0.5, "s")
+            if e == E - 1 and t == 5:
+                cnts["fn"] = cnts["fn"] + [i]
+            if not MCUT[e] or t == 1 and not M1:
+                if a:
+                    continue
                 b = V
-            for k in range(K if t else 0):
+            for k in range(K):
                 o = k * V
-                tt(R("mlog", (t - 1) * KV + o + a, (t - 1) * KV + o + b), R("psL", a, b),
-                   R("wx", slot[e, t] * KV + o + a, slot[e, t] * KV + o + b), A.mult)
+                i = tt(R("mlog", m0 + o + a, m0 + o + b), R(pl, a, b),
+                       R("wx", slot[e, t] * KV + o + a, slot[e, t] * KV + o + b), A.mult)
+                if t == 5 and e < E - 1 and k >= VF[1]:
+                    ops[i]["after"].append(cnts["vote"][VF[0]])
         if t == 0:
-            mov(R("cap"), R("psL", 0, V), 2.0)
-            dma("y", T.lam[:], T.cap[:], [R("cap")], [], 3072)
             return
         s = slot[e, t]
         free.append(s)
-        mb = R("mlog", (t - 1) * KV, t * KV)
         if e == E - 1 and t == 1:
-            for j in range(K):
+            for j in (3, 2, 1, 0):
                 p, ac = R(("psN", "psW")[j % 2], 0, V), R("acc", j * V, (j + 1) * V)
-                mj = R("mlog", j * V, (j + 1) * V)
-                if j < FIN:
-                    dma("g", ac[0], mj[0], [mj, ac], [ac], 3072, accum_op=A.add)
-                    mov(p, REC[j], 1.0, "s")
-                    tt(ac, p, ac, A.mult)
+                mj = R("mlog", m0 + j * V, m0 + (j + 1) * V)
+                if j < TP:
+                    mm("psL", 0, V, [(IDF, "acc", j * V), (IDF, "mlog", m0 + j * V)])
+                    tt(ac, R("psL", 0, V), REC[j], A.mult)
                 else:
-                    tt(p, ac, mj, A.add)
-                    tt(ac, p, REC[j], A.mult)
+                    dma("g", ac[0], mj[0], [mj, ac], [ac], 3072, accum_op=A.add)
+                    if j < 2:
+                        mov(p, REC[j], 1.0, "s")
+                    tt(ac, p, ac, A.mult)
                 dma("y", T.gam[:, j * V:(j + 1) * V], ac[0], [ac], [], 3072)
         else:
             cnts["tag"] = "A%d%d" % (e, t)
-            for a in range(0, KV, KV // NA):
-                x, y = R("acc", a, a + KV // NA), R("mlog", (t - 1) * KV + a, (t - 1) * KV + a + KV // NA)
+            na = NA[e + (DEF and (e, t) == (E - 2, 1))]
+            for a in range(0, KV, KV // na):
+                x, y = R("acc", a, a + KV // na), R("mlog", m0 + a, m0 + a + KV // na)
                 if nacc[0] == 0:
-                    dma("y", x[0], y[0], [y], [x], 12288 // NA)
+                    dma("y", x[0], y[0], [y], [x], 12288 // na)
                 else:
-                    dma("g", x[0], y[0], [x, y], [x], 12288 // NA, accum_op=A.add, max_dma_last_dim=6144)
+                    dma("g", x[0], y[0], [x, y], [x], 12288 // na, accum_op=A.add, max_dma_last_dim=6144)
         nacc[0] += 1
+
+    def inverse():
+        cnts["tag"] = "R2"
+        for fn in (F.Ln, F.Exp):
+            last = cnts["fn"]
+            for j in range(K):
+                x, w, p = REC[j], R("wq", j * V, (j + 1) * V), R(("psN", "psW")[j % 2], 0, V)
+                i = act(x, w, fn) if fn == F.Ln else act(p, x, fn, -1.0, math.log(4.0))
+                ops[i]["after"] += last
+                ops[i]["cost"] += 0.0 if j else 1.6
+                cnts["fn"] = cnts["fn"] + [i]
+                last = [i] + last
+                if fn == F.Exp:
+                    tt(x, p, w, A.mult)
+                    act(x, x, F.Identity, -0.25, 2.0)
+                    tt(x if j < 2 else p, p, x, A.mult)
 
     for t in range(1, 6):
         fstep(0, t)
@@ -613,36 +750,27 @@ def plan(T, topo, core, par=PARS[0]):
             votes(e)
         cnts["tag"] = "C%d" % e
         count(e)
-        cnts["tag"] = "R%d" % e
         if e == E - 1:
-            for fn in (F.Ln, F.Exp):
-                last = cnts["fn"]
-                for j in range(K):
-                    x, w, p = REC[j], R("wq", j * V, (j + 1) * V), R(("psN", "psW")[j % 2], 0, V)
-                    i = act(x, w, fn) if fn == F.Ln else act(p, x, fn, -1.0, math.log(4.0))
-                    ops[i]["after"] += last
-                    ops[i]["cost"] += 0.0 if j else 1.9
-                    cnts["fn"] = cnts["fn"] + [i]
-                    last = [i] + last
-                    if fn == F.Exp:
-                        tt(x, p, w, A.mult)
-                        act(x, x, F.Identity, -0.25, 2.0)
-                        tt(x, p, x, A.mult)
             mset(R("xw", 5 * V, 5 * V + 8), 0.0)
         cnts["tag"] = "L%d" % e
         lists(e)
-        if e < E - 1:
+        if e < E - 1 and (e or not TL):
             tables(R("val", (2 * e + 1) * L, (2 * e + 2) * L), e + 1)
         for t in range(5, 0, -1):
             if e < E - 1:
                 fstep(e + 1, 6 - t)
             bstep(e, t)
+            if TL and (e, t) == (0, 1):
+                tables(R("val", L, 2 * L), 1)
+            if e == E - 1 and t == 5:
+                inverse()
     bstep(E - 1, 0)
     return ops
 
 
 KEPT = {}
-SEED, ROUNDS = 2, 3000
+AHEAD = 0.0
+SEED, ROUNDS, MOVES, HEAT, HOP = 5, 300, 48000, 2e-4, 0.1
 
 
 def order(ops, others=()):
@@ -675,7 +803,6 @@ def order(ops, others=()):
     for i in range(n):
         for j in deps[i]:
             succ[j].append(i)
-    HOP = 0.12
     prio = [0.0] * n
     for i in range(n - 1, -1, -1):
         prio[i] = ops[i]["cost"] + ops[i]["lat"] + ops[i]["occ"] + HOP + max([prio[j] for j in succ[i]], default=0.0)
@@ -770,7 +897,7 @@ def order(ops, others=()):
                         end[i] = busy["d"] + lat[i]
                 tot += max(end) * w
             return tot
-        best = cur = place(prio)
+        best = cur = place([prio[i] + (AHEAD if ops[i]["tag"][0] in "FV" else 0.0) for i in range(n)])
         top = now = score(best)
         for it in range(ROUNDS):
             shift = {t: 0.0 for t in tags}
@@ -786,17 +913,140 @@ def order(ops, others=()):
                     cur, now = c, v
                 if v <= top:
                     best, top = c, v
-        KEPT["best"] = best
-    eng, st, fin = KEPT["best"]
-    seq = sorted(range(n), key=lambda i: (st[i], i))
-    return seq, eng, deps, raw, st, fin
+        seq = sorted(range(n), key=lambda i: (best[1][i], i))
+        KEPT["best"] = polish([ops] + list(others), deps, raw, seq, best[0])
+    seq, eng, fin = KEPT["best"]
+    return seq, eng, deps, raw, fin
+
+
+def polish(plans, deps, raw, seq, eng):
+    ops = plans[0]
+    n, m = len(ops), len(plans)
+    num = {"v": 0, "s": 1, "p": 2, "g": 3, "y": 4, "a": 1, "-": -1}
+    anc, pre = [0] * n, []
+    for i in range(n):
+        a, keep = 0, []
+        for j in sorted(deps[i], reverse=True):
+            if not a >> j & 1:
+                keep.append(j)
+            a |= anc[j]
+        for j in deps[i]:
+            a |= 1 << j
+        anc[i] = a
+        pre.append([(j, HOP if j in raw[i] and not ops[i]["engs"] == ops[j]["engs"] == "p" else 0.0) for j in keep])
+    occ = [o["occ"] for o in ops]
+    costs, lats = [[o["cost"] for o in a] for a in plans], [[o["lat"] for o in a] for a in plans]
+    eng = list(eng)
+    q = [num[e] for e in eng]
+
+    def run(seq, p0, old, k0=0, room=1e9):
+        tot, out = 0.0, [None] * m
+        for k in [k0] + [k for k in range(m) if k != k0]:
+            end, rel, dm, cs, lt = old[k][0][:], old[k][1][:], old[k][2][:], costs[k], lats[k]
+            busy, seen, d, p = [0.0] * 5, 0, 0.0, p0 - 1
+            while p >= 0 and seen != 63:
+                i = seq[p]
+                x = q[i]
+                if x >= 0 and not seen >> x & 1:
+                    busy[x] = rel[i]; seen |= 1 << x
+                if occ[i] and not seen & 32:
+                    d = dm[i]; seen |= 32
+                p -= 1
+            for i in seq[p0:]:
+                t = 0.0
+                for j, h in pre[i]:
+                    u = end[j] + h
+                    if u > t:
+                        t = u
+                x = q[i]
+                if x >= 0:
+                    if busy[x] > t:
+                        t = busy[x]
+                    t += cs[i]; busy[x] = t; rel[i] = t
+                    if occ[i]:
+                        d = (d if d > t else t) + occ[i]; t = d; dm[i] = d
+                end[i] = t + lt[i]
+            t = max(end)
+            if k == k0 and (t - old[k][3]) * WEIGHTS[k] > room:
+                return 1e9, None
+            tot += t * WEIGHTS[k]
+            out[k] = (end, rel, dm, t)
+        return tot, out
+
+    def chain(seq, end, rel, dm):
+        prev, last, dprev, dl = [None] * n, [None] * 5, [None] * n, None
+        for i in seq:
+            if q[i] >= 0:
+                prev[i] = last[q[i]]; last[q[i]] = i
+                if occ[i]:
+                    dprev[i] = dl; dl = i
+        i, arcs, either, queued = end.index(max(end)), [], [], False
+        while i is not None:
+            if len(ops[i]["engs"]) > 1:
+                either.append(i)
+            if occ[i] and not queued and dprev[i] is not None and dm[dprev[i]] > rel[i] + 1e-9:
+                arcs.append((dprev[i], i)); i = dprev[i]
+                continue
+            b, t = None, 0.0
+            for j, h in pre[i]:
+                if end[j] + h > t:
+                    b, t = j, end[j] + h
+            queued = prev[i] is not None and rel[prev[i]] > t - 1e-9
+            if queued:
+                arcs.append((prev[i], i)); b = prev[i]
+            i = b
+        return arcs, either, prev
+
+    rng = np.random.RandomState(SEED)
+    now, state = run(seq, 0, [([0.0] * n,) * 3 + (0.0,)] * m)
+    best, arcs = (now, seq, eng[:], state[0][0]), None
+    for it in range(MOVES):
+        if arcs is None:
+            k0 = rng.randint(m)
+            arcs, either, prev = chain(seq, *state[k0][:3])
+            pos = [0] * n
+            for p, i in enumerate(seq):
+                pos[i] = p
+        r, flip = rng.rand(), None
+        if r < 0.08 and either:
+            flip = either[rng.randint(len(either))]
+            eng[flip] = "s" if eng[flip] == "v" else "v"
+            q[flip] = num[eng[flip]]
+            new, p0 = seq, pos[flip]
+        else:
+            a = rng.randint(len(arcs))
+            i, j = arcs[a]
+            for _ in range(rng.geometric((0.7, 0.2)[it % 2]) - 1):
+                if r < 0.55 and prev[i] is not None and not anc[j] >> prev[i] & 1:
+                    i = prev[i]
+                if r >= 0.55 and a > 0 and arcs[a - 1][0] == j and not anc[arcs[a - 1][1]] >> i & 1:
+                    a -= 1; j = arcs[a][1]
+            if anc[j] >> i & 1:
+                continue
+            p0, p1 = pos[i], pos[j]
+            if r < 0.55:
+                mid, b = seq[p0:p1], anc[j]
+                new = seq[:p0] + [x for x in mid if b >> x & 1] + [j] + [x for x in mid if not b >> x & 1] + seq[p1 + 1:]
+            else:
+                mid = seq[p0 + 1:p1 + 1]
+                new = seq[:p0] + [x for x in mid if not anc[x] >> i & 1] + [i] + [x for x in mid if anc[x] >> i & 1] + seq[p1 + 1:]
+        room = -math.log(1e-12 + rng.rand()) * (HEAT * (1 - it / MOVES) ** 2 + 1e-7)
+        v, st = run(new, p0, state, k0, room)
+        if v <= now + room:
+            now, state, seq, arcs = v, st, new, None
+            if v < best[0]:
+                best = (v, seq, eng[:], st[0][0])
+        elif flip is not None:
+            eng[flip] = "s" if eng[flip] == "v" else "v"
+            q[flip] = num[eng[flip]]
+    return best[1:]
 
 
 def rank_program(g, core, T, topo):
     if T.rank_of(core) is None:
         return
     ops = plan(T, topo, core)
-    seq, eng, deps, raw, st, fin = order(ops, [plan(T, topo, core, p) for p in PARS[1:]])
+    seq, eng, deps, raw, fin = order(ops, [plan(T, topo, core, p) for p in PARS[1:]])
     queue = {"v": g.vector, "s": g.scalar, "p": g.tensor, "g": g, "y": g.sync, "a": g.scalar}
     same = {"v": "v", "s": "s", "p": "p", "g": "g", "y": "y", "a": "s"}
     csem = {"v": "cv", "s": "cs", "p": "cp", "g": "cg"}

import math
import numpy as np
from concourse.bass import DstId, RemoteDMATransfer
from concourse.mybir import AluOpType as A, ActivationFunctionType as F

V, H, K, M, KV, L = 768, 128, 4, 1024, 3072, 192
E = 3
LX = L + 16
TINY = 2.0 ** -30
NWX = 6
XS = [2, 2, 2]
X5 = [2, 2, 2]
XK = [(), (3,), (2, 3), (1, 2, 3), (0, 1, 2, 3)]
SP = "s"
NA = [1, 1, 4]
MMS = 2
WM = ["l", "l", "l"]
GF = [1, 1, 1]
CUT = [True, True, True]
ALT = ["s", "s", "s"]
VP = True
MCUT = [True, True, True]
GCUT = [True, True, True]
WCUT = [True, True, True]
FM = [False, False, False]
M1 = False
DEF = True
CD = True
TP = 1
VF = (0, 9)
TL = True
FD = True
PM = [0, 0, 0]
PCAP = [False, False, False]
WA = [False, False, True]
SP2 = ["sv", "sv", "sv"]
SW = ["sv", "sv", "sv"]
GB = [-1, -1, 0]
RET = "ccc"
X0 = False
VS = ()
f32, bf, i32, u16 = "float32", "bfloat16", "int32", "uint16"

SCRATCH = {
    "wq": ("sbuf", [128, KV], bf),
    "wx": ("sbuf", [128, NWX * KV], bf),
    "mlp": ("sbuf", [128, 256 + 4 * KV + 264], f32),
    "hg": ("sbuf", [128, KV + 8], f32),
    "z": ("sbuf", [128, 2 * V], f32),
    "inv": ("sbuf", [128, 96], f32),
    "acc": ("sbuf", [128, KV], f32),
    "log": ("sbuf", [128, 15 * M], bf),
    "dpt": ("sbuf", [128, L], f32),
    "fa": ("sbuf", [128, NWX * V], bf),
    "f0": ("sbuf", [128, V], bf),
    "xw": ("sbuf", [128, 4 * M], f32),
    "pint": ("sbuf", [128, 5 * L], i32),
    "hl": ("sbuf", [128, KV], f32),
    "zz": ("sbuf", [128, V], f32),
    "hz0": ("sbuf", [128, V], bf),
    "cap": ("sbuf", [128, V], f32),
    "dm": ("sbuf", [128, V], bf),
    "ls": ("sbuf", [128, V], bf),
    "ones": ("sbuf", [128, V], bf),
    "cn": ("sbuf", [128, V], bf),
    "ret": ("sbuf", [128, 2 * 264], f32),
    "inu": ("sbuf", [128, 48], u16),
    "sf": ("sbuf", [128, 384], bf),
    "sb": ("sbuf", [128, 256], f32),
    "id2": ("sbuf", [128, 256], bf),
    "id2f": ("sbuf", [128, 528], f32),
    "zw": ("sbuf", [128, V], f32),
    "wpw": ("sbuf", [128, V], bf),
    "lt": ("sbuf", [128, 96], f32),
    "lw": ("sbuf", [128, 288], u16),
    "pw": ("sbuf", [128, 13 * 128], bf),
    "xm": ("sbuf", [128, 4 * 128], f32),
    "fm": ("sbuf", [128, 144], bf),
    "bg": ("sbuf", [128, 16], bf),
    "sndi": ("sbuf", [128, 16], i32),
    "sns": ("sbuf", [128, 8], i32),
    "pcol": ("sbuf", [128, 8], i32),
    "pcf": ("sbuf", [128, 4], f32),
    "cf": ("sbuf", [128, L], f32),
    "ixf": ("sbuf", [128, L], f32),
    "val": ("sbuf", [128, 4 * L], f32),
    "tf": ("sbuf", [128, 2 * LX], f32),
    "eag": ("sbuf", [128, L], f32),
    "both": ("sbuf", [128, 2 * L], f32),
    "tmp": ("sbuf", [128, L], f32),
    "ix": ("sbuf", [128, L], u16),
    "rho": ("sbuf", [128, L], u16),
    "linv": ("sbuf", [128, LX], u16),
    "jx": ("sbuf", [128, 5 * LX], u16),
    "snu": ("sbuf", [128, 16], u16),
    "snp": ("sbuf", [128, 16], u16),
    "psN": ("psum", [128, 1024], f32),
    "psW": ("psum", [128, 1024], f32),
    "psP": ("psum", [128, 1024], f32),
    "psL": ("psum", [128, 1024], f32),
}
SEMAPHORES = (["cv", "cs", "cp", "cg"] + ["arr%d" % i for i in range(27)] + ["snt%d" % i for i in range(27)]
              + ["dq%d" % i for i in range(80)])

ALIAS = {"ti": ("pint", 0, 3 * L), "srci": ("pint", 3 * L, L), "dlyi": ("pint", 4 * L, L),
         "dr": ("dm", 0, V), "rr": ("fa", 5 * V, V), "mlog": ("mlp", 256, 4 * KV + 264)}
OFF = 128
CH = [(0, 512 - OFF), (512 - OFF, V)]
PARS = [(1.25, 1.6, 3.8, 4.0, 0.55, 0.04), (1.0, 1.56, 3.8, 3.4, 0.42, 0.05), (1.0, 1.15, 2.5, 3.8, 0.45, 0.05)]
WEIGHTS = [0.3 / 285, 0.35 / 230, 0.35 / 222]


def plan(T, topo, core, par=PARS[0]):
    CY, GA, SC, PE, COMM = 0.83e-3 * par[0], par[1], par[2], 1e-3 * par[4], par[3]
    ops = []
    rank = T.rank_of(core)
    n = len(T.cores)
    nxt, prv = T.cores[(rank + 1) % n], T.cores[(rank - 1) % n]
    en, ep = topo.engines(core, nxt), topo.engines(core, prv)
    en, ep = en[:len(en) // 2], ep[len(ep) // 2:]
    mn, mp = sum(1 << e for e in en), sum(1 << e for e in ep)
    nsig = len(en) + len(ep)
    dn, dp = DstId(rid=topo.addr(nxt)[0], pnc=topo.addr(nxt)[1]), DstId(rid=topo.addr(prv)[0], pnc=topo.addr(prv)[1])
    cnts = {"msg": 0, "dq": 0, "tag": "S", "fn": []}

    def bank(name, a):
        return "ps" + name[2:], (a + OFF) % 1024 if name[1] == "s" else a

    def R(name, a=None, b=None, step=None):
        if name[:2] in ("ps", "pr"):
            name, c = bank(name, a)
            a, b = c, c + b - a
        name, off, w = ALIAS.get(name) or (name, 0, T[name].shape[1])
        t = T[name]
        a = off + (0 if a is None else a)
        b = off + (w if b is None else b)
        ap = t[:, a:b] if step is None else t[:, a:b:step]
        if name.startswith("ps"):
            return ap, [(name, k, k + 1, True) for k in range(a // 512, (b - 1) // 512 + 1)], True, b - a
        return ap, [(name, a, b, False)], False, (b - a if step is None else (b - a + step - 1) // step)

    def rows(name, a, b):
        name, off, w = ALIAS.get(name) or (name, 0, 0)
        return T[name][0:128:16, off + a:off + b]

    def add(engs, cost, reads, writes, emit, kind="c", lat=0.0, sem=None, after=()):
        cost -= par[5] if engs in ("v", "s", "sv") else 0.0
        rd = [r for x in reads for r in x[1]]
        wr = [r for x in writes for r in x[1]]
        ops.append({"ex": [r for r in rd if r[3] and r not in wr], "engs": engs, "cost": cost, "rd": rd, "wr": wr,
                    "emit": emit, "kind": kind, "lat": lat, "sem": sem, "after": list(after), "tag": cnts["tag"], "occ": 0.0})
        return len(ops) - 1

    def two(*xs):
        return all(x[0].dtype != T.acc.dtype and x[0].dtype != T.pint.dtype for x in xs)

    def ts(o, i, s1, s2, op0, op1=None, extra=()):
        c = 0.06 + max(64, i[3] * (0.5 if two(o, i) else 1)) * CY
        if op0 == A.mult and op1 in (None, A.add) and not extra and all(x[0].dtype == T.acc.dtype for x in (o, i)):
            return mov(o, i, s1, "sv", s2 or 0.0)
        if op1 is None:
            return add("v", c, [i] + list(extra), [o], lambda g, e: g.vector.tensor_scalar(o[0], i[0], s1, None, op0))
        return add("v", c, [i] + list(extra), [o], lambda g, e: g.vector.tensor_scalar(o[0], i[0], s1, s2, op0, op1))

    def tt(o, a, b, op):
        c = 0.06 + max(64, a[3] * (1 if (a[2] or b[2]) else 2) * (0.5 if two(o, a, b) else 1)) * CY
        return add("v", c, [a, b], [o], lambda g, e: g.vector.tensor_tensor(o[0], a[0], b[0], op))

    def cp(o, i):
        c = 0.06 + max(64, i[3] * (0.5 if two(o, i) else 1)) * CY
        return add("v", c, [i], [o], lambda g, e: g.vector.tensor_copy(o[0], i[0]))

    def act(o, i, func=F.Identity, scale=1.0, bias=0.0):
        return add("s", 0.07 + max(64, i[3]) * CY, [i], [o],
                   lambda g, e: g.scalar.activation(o[0], i[0], func, bias=bias, scale=scale))

    def mov(o, i, scale=1.0, engs="sv", bias=0.0):
        def emit(g, e):
            if e == "s":
                return g.scalar.activation(o[0], i[0], F.Identity, bias=bias, scale=scale)
            return g.vector.tensor_scalar(o[0], i[0], scale, bias, A.mult, A.add)
        return add(engs, 0.07 + max(64, i[3]) * CY, [i], [o], emit)

    def gat(o, win, lst, engs="s", plus=0.0):
        def emit(g, e):
            if e == "s":
                return g.scalar.activation(o[0], win[0].indirect(lst[0]), F.Identity, bias=plus)
            if plus:
                return g.vector.tensor_scalar(o[0], win[0].indirect(lst[0]), plus, None, A.add)
            return g.vector.tensor_copy(o[0], win[0].indirect(lst[0]))
        return add(engs, 0.065 + par[5] + o[3] * GA * CY, [win, lst], [o], emit)

    def gmul(o, win, lst, b, op=A.mult):
        return add("v", 0.05 + par[5] + o[3] * GA * CY, [win, lst, b], [o],
                   lambda g, e: g.vector.tensor_tensor(o[0], win[0].indirect(lst[0]), b[0], op))

    def scat(win, lst, i):
        return add("v", 0.05 + par[5] + i[3] * SC * CY, [lst, i], [win],
                   lambda g, e: g.vector.tensor_copy(win[0].indirect(lst[0]), i[0]))

    def mset(o, c):
        return add("v", 0.06 + max(64, o[3] * (0.5 if two(o) else 1)) * CY, [], [o], lambda g, e: g.vector.memset(o[0], c))

    def mm(ps, o0, n, terms, start=True, stop=True):
        if n > 256 and len(terms) > MMS:
            for j in range(0, len(terms), MMS):
                mm(ps, o0, n, terms[j:j + MMS], start and j == 0, stop and j + MMS >= len(terms))
            return
        ps, o0 = bank(ps, o0)
        a = o0
        while a < o0 + n:
            b = min(o0 + n, (a // 512 + 1) * 512)
            rd, c, rhs = [], 0.03, []
            for t in terms:
                st = t[3] if len(t) > 3 else 1
                lo = t[2] + (a - o0) * st
                r = R(t[1], lo, lo + (b - a - 1) * st + 1, None if st == 1 else st)
                rd += [t[0], r]; rhs.append(r[0])
                c += (max(64, b - a) * (1 if two(t[0]) else 4) + 16) * PE

            def emit(g, e, a=a, b=b, rhs=rhs):
                ins = None
                for j, t in enumerate(terms):
                    ins = g.tensor.matmul(T[ps][:, a:b], t[0][0], rhs[j], start and j == 0, stop and j == len(terms) - 1)
                return ins
            add("p", c, rd, [R("pr" + ps[2:], a, b)], emit)
            a = b

    def dma(q, o, i, reads, writes, nbytes, **kw):
        s = "dq%d" % cnts["dq"]; cnts["dq"] += 1
        def emit(g, e):
            if e == "g":
                return g.dma_start(o, i, **kw)
            return (g.sync if e == "y" else g.scalar).dma_start(o, i)
        f = 2.0 if kw.get("accum_op") is not None else 1.0
        add(q, 1.0 if q == "g" else 0.1, reads, writes, emit, "d", 2.0, s)
        ops[-1]["occ"] = f * nbytes / 4700.0

    def send(to_next, land_next, to_prev, land_prev, guard):
        k = cnts["msg"]; cnts["msg"] += 1
        def emit(g, e):
            g.remote_dma_fused([
                RemoteDMATransfer(dst_ids=[dn], dma_engine_mask=mn, remote_sem=T.sem["arr%d" % k], srcs=[x[0] for x in to_next],
                                  dsts=[land_next[0]], alu_op=int(len(to_next) > 1)),
                RemoteDMATransfer(dst_ids=[dp], dma_engine_mask=mp, remote_sem=T.sem["arr%d" % k], srcs=[to_prev[0]], dsts=[land_prev[0]]),
            ], local_sem=T.sem["snt%d" % k])
            return None
        s = add("g", 0.5, to_next + [to_prev], [], emit, "r", COMM - 2.0 + 0.25 * (len(to_next) - 1), ("snt%d" % k, nsig))
        ops[s]["occ"] = 1.0
        ops[s]["guard"] = [r for x in guard for r in x[1]]
        add("", 0.0, [], [land_next, land_prev], None, "a", 0.5, ("arr%d" % k, nsig), after=[s])

    def gop(cost, reads, writes, emit):
        return add("g", cost, reads, writes, emit)

    ID, IDF = R("id2", 0, 128), R("id2f", 0, 128)
    SHF, SHB, TWOF = R("id2", 112, 240), R("id2f", 16, 144), R("id2f", 144, 272)
    NEGF, HALFF = R("id2f", 272, 400), R("id2f", 400, 528)
    PW = [ID] + [R("pw", j * 128, (j + 1) * 128) for j in range(4)]
    TWO, HALF, NEG, Y0, NEG2, THREE, NMAG, BIG, NBIG = [R("pw", j * 128, (j + 1) * 128) for j in range(4, 13)]
    MAGIC = 1.5 * 2.0 ** 26
    XM = [R("xm", 0, 128), R("xm", 128, 256)]
    DM = [R("xm", 256, 384), R("xm", 384, 512)]
    lg = "log"
    blk = lambda e, t: (5 - t if e % 2 else 9 + t) * M
    place = lambda e, d: d - 1 if e % 2 else 4 - d

    def fland(e, t):
        return R(lg, blk(e, t) + V, blk(e, t) + V + H), R(lg, blk(e, t) + V + H, blk(e, t) + M)

    def rland(k):
        return R("ret", (k % 2) * 264, (k % 2) * 264 + H), R("ret", (k % 2) * 264 + H, (k % 2) * 264 + 2 * H)

    fmsg, bmsg = [0], [0]

    def wires(e, t, ps="psW"):
        o = 0
        if SW[e] == "s":
            gat(R("sf", o, o + 256), R(lg, blk(e, t), blk(e, t) + V), R("snu"), SP)
        else:
            gat(R("sf", 0, H), R(lg, blk(e, t), blk(e, t) + V), R("snu", 0, 8), "s")
            gat(R("sf", H, 256), R(lg, blk(e, t), blk(e, t) + V), R("snu", 8, 16), SW[e])
        mm(ps, V, H, [(SHF, "sf", o)])
        mov(R("sf", o + 256, o + 384), R(ps, V, V + H))
        a, b = fland(e, t)
        ne, nt = (e, t + 1) if t < 4 else (e + 1, 1)
        send([R("sf", o + 256, o + 384)], a, R("sf", o + H, o + 256), b, list(fland(ne, nt)) if ne < E else [])

    dma("y", T.dm[:], T.drive[:], [], [R("dr")], 1536)
    dma("a", T.sndi[:], T.snd[:], [], [R("sndi")], 64)
    if FD:
        for q, (a, b, c) in zip("ya", ((16, 128, 0), (0, 16, 112))):
            dma(q, T.fa[a:b, 4 * V:5 * V], T.drive[c:c + b - a, :], [], [R("fa", 4 * V + a, 4 * V + b)], 1536)
            dma(q, T.sns[a:b, :], T.snd[c:c + b - a, 0:8], [], [R("sns", a // 16, a // 16 + 1)], 32)
    dma("y", R("srci")[0], T.src[:], [], [R("srci")], 768)
    dma("a", R("dlyi")[0], T.dly[:], [], [R("dlyi")], 768)
    dma("y", T.wq[:], T.w[:], [], [R("wq")], 6144)
    dma("y", T.ls[:, 0:V], T.loss[:], [], [R("ls", 0, V)], 1536)
    S0 = R(lg, blk(0, 0), blk(0, 0) + V)
    mset(R("ones"), 1.0)
    gop(0.45, [R("ones")], [ID], lambda g, e: g.affine_select(ID[0], T.ones[:, 0:128], [[-1, 128]], A.is_equal, 0.0, 0, 1))
    cp(R("id2", 128, 256), ID)
    cp(R("snu"), R("sndi"))
    if FD:
        cp(R("snp", 0, 8), R("sns"))
        for x, y, z in ((R("sf", 256, 384), R("fa", 4 * V, 5 * V), R("snp", 0, 8)), (R("sf", H, 256), R("dr"), R("snu", 8, 16))):
            add("v", 0.05 + par[5] + H * GA * CY, [y, z], [x],
                lambda g, e, x=x, y=y, z=z: g.vector.tensor_scalar(x[0], y[0].indirect(z[0]), 1.0, None, A.is_ge))
        send([R("sf", 256, 384)], fland(0, 0)[0], R("sf", H, 256), fland(0, 0)[1], list(fland(0, 1)))
    ts(S0, R("dr"), 1.0, None, A.is_ge)
    if not FD:
        wires(0, 0)
    mset(R(lg, 6 * M, 9 * M), 0.0)
    ts(R("wq", 0, 2 * V), R("wq", 0, 2 * V), TINY, None, A.max)
    act(R("wq", 2 * V, KV), R("wq", 2 * V, KV), F.Identity, 1.0, TINY)
    ts(R("ti", 0, L), R("srci"), 1023, None, A.bitwise_and)
    cp(R("cf"), R("ti", 0, L))
    ts(R("dpt"), R("dlyi"), -1024.0, 4096.0, A.mult, A.add)
    tt(R("ixf"), R("dpt"), R("cf"), A.add)
    cp(R("ix"), R("ixf"))
    act(R("rr"), R("dr"), F.Identity, -1.0, 1.0)
    tt(R("hz0"), R("rr"), S0, A.max)
    act(R("f0"), R("dr"), F.Identity, -2.0, 195.0 - 1.0 / 64)
    act(R("dm"), R("dr"), F.Identity, 1.0, -0.5)
    ts(R("f0"), R("f0"), 192.0, 0.5, A.subtract, A.max)
    act(R("cn"), S0, F.Identity, -8.0, 8.0)
    tt(R("f0"), R("f0"), R("cn"), A.max)
    act(R("f0"), R("f0"), F.Identity, 2.0)
    mov(R("id2f", 0, 144), R("id2", 0, 144))
    for j in range(4):
        mov(PW[j + 1], ID, 16.0 ** (j + 1))
    for x, c in ((TWO, 2.0), (THREE, 3.0), (NEG2, -2.0), (NEG, -1.0), (HALF, 0.5), (Y0, -8.5 * 16 ** 4),
                 (NMAG, -MAGIC)) + (((BIG, 2.0 ** 24), (NBIG, -2.0 ** 24)) if any(PCAP) else ()):
        mov(x, ID, c)
    for j, c in ((1, -8.5 * 16 ** 2), (2, -8.5)):
        mov(R("rr", 0, 128), R("id2", j, 128 + j), c)
        tt(Y0, Y0, R("rr", 0, 128), A.add)
    for e in range(2):
        b = 1 << e
        for r in range(2 * b):
            cp(R("xm", e * 128 + r, (e + 1) * 128, 2 * b), R("id2f", r ^ b, 128, 2 * b))
        tt(DM[e], XM[e], IDF, A.subtract)
    gop(0.2, [R("ones")], [R("bg", 0, 8)], lambda g, e: g.affine_select(T.bg[:, 0:8], T.ones[:, 0:8], [[-16, 8]], A.is_ge, 0.0, 0, 1))
    gop(0.2, [R("bg", 0, 8)], [R("bg", 8, 16)], lambda g, e: g.affine_select(T.bg[:, 8:16], T.bg[:, 0:8], [[16, 8]], A.is_ge, 0.0, 15, -1))
    mset(R("fm"), 0.0)
    cp(R("fm", 16, 144, 16), R("bg", 8, 16))
    mov(R(lg, blk(1, 0), blk(1, 0) + M), R(lg, blk(0, 0), blk(0, 0) + M))
    mset(R("mlog", 4 * KV, 4 * KV + 264), 0.0)
    mset(R("hg", KV, KV + 8), 0.0)
    mov(TWOF, ID, 2.0)
    if VS:
        mov(NEGF, ID, -1.0)
    if any(PM):
        mov(HALFF, ID, 0.5)
    cnts["tag"] = "I"
    ts(R("ti", 0, L), R("srci"), 10, None, A.arith_shift_right)
    ts(R("tmp"), R("cf"), 768.0, None, A.is_ge)
    ts(R("eag"), R("ti", 0, L), -512.0, -1536.0, A.mult, A.add)
    tt(R("tmp"), R("tmp"), R("eag"), A.mult)
    ts(R("eag"), R("ti", 0, L), 768.0, 768.0, A.mult, A.add)
    tt(R("tmp"), R("tmp"), R("eag"), A.add)
    tt(R("srci"), R("tmp"), R("cf"), A.add)
    ts(R("ti", 0, L), R("srci"), 8, None, A.arith_shift_right)
    ts(R("tmp"), R("ti", 0, L), -3071.0, None, A.mult)
    ts(R("eag"), R("srci"), 12.0, None, A.mult)
    tt(R("tmp"), R("tmp"), R("eag"), A.add)
    cp(R("rho"), R("tmp"))
    gop(0.13 + 2 * V * CY, [], [R("mlog", KV, KV + V)],
        lambda g, e: g.iota(R("mlog", KV, KV + V)[0], [[1, 48], [L, 16]], 0, 0, allow_small_or_imprecise_dtypes=True))
    for j in range(1, K):
        act(R("mlog", KV + j * V, KV + (j + 1) * V), R("mlog", KV, KV + V), F.Identity, 1.0, 48.0 * j)
    for j in range(12):
        scat(R("mlog", 0, KV), R("rho", j * 16, j * 16 + 16), R("mlog", KV + j * 256, KV + j * 256 + 256))
    ts(R("ti", L, L + 16), R("sndi"), 8, None, A.arith_shift_right)
    ts(R("lt", 0, 16), R("ti", L, L + 16), -3071.0, 9.0, A.mult, A.add)
    ts(R("lt", 16, 32), R("sndi"), 12.0, None, A.mult)
    tt(R("lt", 0, 16), R("lt", 0, 16), R("lt", 16, 32), A.add)
    cp(R("lw", 0, 16), R("lt", 0, 16))
    gat(R("zz", 0, 256), R("mlog", 0, KV), R("lw", 0, 16))
    dma("y", T.tf[:, 0:L], rows("mlog", 0, KV), [R("mlog", 0, KV)], [R("tf", 0, L)], 6000)
    dma("a", T.tf[:, L:LX], rows("zz", 0, 256), [R("zz", 0, 256)], [R("tf", L, LX)], 600)
    cp(R("linv"), R("tf", 0, LX))
    gop(0.2, [], [R("pcol", 0, 1)], lambda g, e: g.iota(T.pcol[:, 0:1], [[1, 1]], 0, 1))
    ts(R("pcol", 4, 5), R("pcol", 0, 1), 15, None, A.bitwise_and)
    cp(R("pcf", 0, 1), R("pcol", 4, 5))
    gop(0.55, [], [R("val", L, 2 * L)],
        lambda g, e: g.iota(T.val[:, L:2 * L], [[16, L]], -KV, 0, allow_small_or_imprecise_dtypes=True))
    ts(R("tmp"), R("dlyi"), float(KV), T.pcf[:, 0:1], A.mult, A.add, extra=[R("pcf", 0, 1)])
    tt(R("val", 0, L), R("tmp"), R("val", L, 2 * L), A.add)

    def tables(s, e):
        cnts["tag"] = "T%d" % e
        a, b, c = (("mlog", "mlog", KV), ("hl", "mlog", 2 * KV) if TL else ("hl", "xw", 0), ("hl", "xw", 0))[e]
        dma("y", rows(a, 0, KV), s[0], [s], [R(a, 0, KV)], 6000)
        for j in range(4):
            gat(R(b, c + j * V, c + (j + 1) * V), R(a, 0, KV), R("linv", j * 48, j * 48 + 48))
        gat(R("zz", 0, 256), R(a, 0, KV), R("linv", L, LX))
        j = e % 2 * LX
        dma("y", T.tf[:, j:j + L], rows(b, c, c + KV), [R(b, c, c + KV)], [R("tf", j, j + L)], 6000)
        dma("a", T.tf[:, j + L:j + LX], rows("zz", 0, 256), [R("zz", 0, 256)], [R("tf", j + L, j + LX)], 600)
    tables(R("val", 0, L), 0)
    cnts["tag"] = "J"
    ts(R("ti", 0, 16), R("sndi"), 15, None, A.bitwise_and)
    ts(R("ti", 16, 32), R("sndi"), 4, None, A.arith_shift_right)
    ts(R("tmp", 0, 16), R("ti", 0, 16), 48.0, None, A.mult)
    tt(R("tmp", 0, 16), R("tmp", 0, 16), R("ti", 16, 32), A.add)
    cp(R("snp"), R("tmp", 0, 16))
    gop(0.7, [], [R("z", 0, 256)],
        lambda g, e: g.iota(T.z[:, 0:256], [[1, 256]], 0, 0, allow_small_or_imprecise_dtypes=True))
    mset(R("cap"), 256.0)
    scat(R("cap"), R("snp"), R("z", 0, 256))
    dma("y", T.inv[:, 0:48], T.cap[0:128:16, :], [R("cap")], [R("inv", 0, 48)], 1500)
    ts(R("inv", 48, 96), R("inv", 0, 48), 256.0, None, A.is_ge)
    if "g" in RET:
        cp(R("inu"), R("inv", 0, 48))
        mset(R("ret", 256, 264), 0.0); mset(R("ret", 520, 528), 0.0)

    free = list(range(NWX))
    slot = {}

    def xpart(e, d):
        C, o, s = 2.0 ** -21, place(e, d) * M, blk(e, 5 - d)
        if d == 4:
            act(R("xw", o, o + M), R(lg, blk(e, 0), blk(e, 0) + M), F.Identity, 1.0 / 16, C)
        elif d:
            for a, b in ([(0, V), (V, M)] if d == 1 else [(0, M)]):
                act(R("xw", o + a, o + b), R("xw", place(e, d + 1) * M + a, place(e, d + 1) * M + b), F.Identity, 1.0 / 16, C * 15 / 16)
        else:
            o, s = place(e, 1) * M, blk(e, 4)
            x, y = R("xw", o + V, o + M), R(lg, s + V, s + M)
            return dma("g", x[0], y[0], [x, y], [x], 1024, accum_op=A.add) if X0 else tt(x, x, y, A.add)
        for a, b in ([(0, M)] if d > 2 else [(0, V), (V, M)][:d]):
            x, y = R("xw", o + a, o + b), R(lg, s + a, s + b)
            dma("g", x[0], y[0], [x, y], [x], 4 * (b - a), accum_op=A.add)

    def spike(o, i, SP):
        def emit(g, e):
            if e == "s":
                return g.scalar.activation(o[0], i[0], F.Sigmoid, bias=256.0, scale=-2.0 ** 20)
            return g.vector.tensor_scalar(o[0], i[0], 2.0 ** -12, None, A.is_le)
        return add(SP, 0.07 + i[3] * CY, [i], [o], emit)

    def fstep(e, t):
        s = free.pop(0); slot[e, t] = s
        cnts["tag"] = "F%d%d" % (e, t)
        if e < E - 1 and t == 5:
            xpart(e, 0)
        a = min(blk(e, t - 4), blk(e, t - 1))
        win = R(lg, a, a + 4 * M)
        zp = t < 5 or e == E - 1
        pw, pn = ("psN", "psW") if t % 2 and zp else ("psW", "psN")
        ps, sg = (pw, NEG2) if zp else (pn, TWO)
        if zp:
            if t > 1:
                mm(pw, 0, V, [(ID, "dm", 0)], True, False)
                act(R(pw, 0, V), R(pn, 0, V), F.Relu, 0.5, 0.0)
            mm(pw, 0, V, [(ID, "hz0", 0) if t == 1 else (ID, lg, blk(e, t - 1)), (NEG2, "dm", 0)], t == 1, False)
        else:
            mm("psN", 0, V, [(TWO, "dm", 0)], True, False)
        xk = XK[XS[e] if t < 5 else X5[e]]
        for k in range(K):
            for a, b in ([(0, V)] if k < K - 1 else CH):
                o = k * V
                wx, ix = R("wx", s * KV + o + a, s * KV + o + b), R("ix", (o + a) // 16, (o + b) // 16)
                if k in xk:
                    gat(wx, win, ix)
                    tt(wx, wx, R("wq", o + a, o + b), A.mult)
                elif FM[e] and k < 2 and 1 not in xk:
                    if k == 0:
                        gmul(R("wx", s * KV, s * KV + 2 * V), win, R("ix", 0, 96), R("wq", 0, 2 * V))
                else:
                    gmul(wx, win, ix, R("wq", o + a, o + b))
                mm(ps, a, b - a, [(sg, "wx", s * KV + o + a)], False, k == K - 1)
        for a, b in CH:
            S, hz = R(lg, blk(e, t) + a, blk(e, t) + b), R("hz0" if t == 1 else "zz", a, b)
            if not zp:
                tt(S, hz, R("psN", a, b), A.is_le)
                continue
            cnts["fn"] = cnts["fn"][-1:] + [spike(S, R(pw, a, b), SP2[e] if a else "s")]
        if t < 5:
            wires(e, t, pw)
        if zp:
            mm(pn, 0, V, [(TWO, "dm", 0)] + [(TWO, "wx", s * KV + k * V) for k in range(K)])
        if t == 4 and e < E - 1:
            S = R(lg, blk(e, t), blk(e, t) + V)
            act(R("zz"), R(pw, 0, V), F.Relu, 0.5, 0.0)
            dma("g", T.zz[:], S[0], [S, R("zz")], [R("zz")], 3072, accum_op=A.add)
        fa = R("fa", s * V, (s + 1) * V)
        act(fa, R(pn, 0, V), F.Identity, -1.0, 194.0 - 1.0 / 64)
        ts(fa, fa, 192.0, 0.5, A.subtract, A.max)
        if e < E - 1 and 2 <= t < 5:
            xpart(e, 6 - t)
            if t == 4:
                xpart(e, 1)

    def count(e):
        if e == 0 and CD:
            for u in range(1, 6):
                x, y = R("cn"), R(lg, blk(e, u), blk(e, u) + V)
                if u == 1:
                    dma("y", x[0], y[0], [y], [x], 1536)
                else:
                    dma("g", x[0], y[0], [x, y], [x], 1536, accum_op=A.add)
        elif e == 0:
            mm("psN", 0, V, [(ID, lg, blk(e, u)) for u in range(1, 6)])
            mov(R("cn"), R("psN", 0, V))
        elif e == E - 1:
            mm("psN", 0, V, [(ID, lg, blk(1, u)) for u in range(1, 6)] + [(THREE, lg, blk(e, 0))], True, False)
            mm("psN", 0, V, [(ID, lg, blk(e, u)) for u in range(1, 6)] + [(ID, "cn", 0)], False, True)
            mov(R("zz"), R("psN", 0, V), 1.0, "s")
            dma("y", T.cnt[:], T.zz[:], [R("zz")], [], 3072)

    def swap(o, a, both, e):
        mm("prW", 512, L, [(DM[e], a[0], a[1])])
        tt(R("tmp"), R("prW", 512, 512 + L), both, A.mult)
        tt(R(o[0], o[1], o[1] + L), R(a[0], a[1], a[1] + L), R("tmp"), A.add)

    def votes(e):
        s = free[0]
        cnts["tag"] = "V%d" % e
        ts(R("dpt"), R("dpt"), -1.0, 3072.0, A.mult, A.add)
        tt(R("ixf"), R("dpt"), R("cf"), A.add)
        mm("psW", 0, V, [(Y0, "ones", 0)] + [(PW[5 - u], lg, blk(e, u)) for u in range(1, 5)], True, False)
        mm("psW", 0, V, [(PW[0], lg, blk(e, 5))], False, True)
        for k in range(K):
            gat(R("hl", k * V, (k + 1) * V), R("xw"), R("ix", k * 48, k * 48 + 48))
        for k in range(K):
            p = R("hl", k * V, (k + 1) * V)
            tt(p, R("psW", 0, V), p, A.mult)
        for j in range(6):
            a = j % 2 * 512
            p, q, vote = R("hl", j * 512, (j + 1) * 512), R("prN", a, a + 512), R("wx", s * KV + j * 512, s * KV + (j + 1) * 512)
            if VP:
                mm("prN", a, 512, [(NMAG, "ones", 0)], True, False)
            act(q, p, F.Identity, 1.0, MAGIC)
            if j in VS:
                mm("prN", a, 512, [(NMAG, "ones", 0), (NEGF, "hl", j * 512)], False, True)
                act(vote, q, F.Sigmoid, -2.0 ** 20)
            else:
                if VP:
                    mm("prN", a, 512, [(NMAG, "ones", 0)], False, True)
                else:
                    act(q, q, F.Identity, 1.0, -MAGIC)
                cnts["vote"] = [tt(vote, q, p, A.is_lt)]
            if j in (2, 5):
                c0 = (j - 2) * 32
                mm("prW", V + c0, 96, [(R("fm", 16 - i, 144 - i), "wx", s * KV + c0 * 16 + i, 16) for i in range(16)])
            if j == 2:
                mm("prW", 0, L, [(DM[e], "cf", 0)])
        x, y = R("eag"), R("prW", V, V + L)
        add("sv", 0.07 + L * CY, [y], [x], lambda g, q: g.vector.tensor_scalar(x[0], y[0], 9.0, None, A.is_ge) if q == "v"
            else g.scalar.activation(x[0], y[0], F.Sigmoid, bias=-8704.0, scale=1024.0))
        mm("prW", 512, L, [(XM[e], "eag", 0)])
        tt(R("tmp"), R("prW", 0, L), R("eag"), A.mult)
        tt(R("tmp"), R("prW", 512, 512 + L), R("tmp"), A.mult)
        tt(R("ixf"), R("ixf"), R("tmp"), A.add)
        cnts["vote"].append(cp(R("ix"), R("ixf")))
        both = R("both", e * L, (e + 1) * L)
        tt(both, R("prW", 512, 512 + L), R("eag"), A.mult)
        if e == 0:
            tt(R("cf"), R("cf"), R("tmp"), A.add)
            swap(("val", L), ("val", 0), both, 0)
        else:
            swap(("val", 2 * L), ("val", 0), both, 1)
            swap(("val", 3 * L), ("val", 2 * L), R("both", 0, L), 0)

    def lists(e):
        j = e % 2 * LX
        c = 48 if WM[e] == "l" else 0

        def wired(x):
            if RET[e] == "g":
                return
            tt(x, x, R("inv", 48, 96), A.mult)
            tt(x, x, R("inv", 0, 48), A.add)
        if e == E - 1:
            y = R("tf", LX - j, 2 * LX - j)
            ts(y, R("tf", j, j + LX), float(KV), float(4 * KV), A.is_lt, A.mult)
            tt(y, y, R("tf", j, j + LX), A.add)
            ts(y, y, -float(KV), None, A.add)
            wired(R("tf", LX - j + 144, LX - j + L))
            cp(R("jx", 0, LX), y)
        wired(R("tf", j + 144, j + L))
        for tau in range(4, 0, -1):
            ts(R("jx", tau * LX + c, (tau + 1) * LX), R("tf", j + c, j + LX), float((5 - tau) * KV + 256), None, A.min)
        if not c:
            return
        x, q, a, b = R("tf", j, j + 48), R("ti", 0, 48), R("lt", 0, 48), R("lt", 48, 96)
        ts(q, x, 1.0 / KV, -0.4998, A.mult, A.add)
        ts(a, q, -float(KV), None, A.mult)
        ts(b, q, float(V), None, A.mult)
        tt(a, a, x, A.add)
        cp(R("lw", 240, 288), a)
        x, y, z = R("wpw"), R("wq"), R("lw", 240, 288)
        add("s", 0.065 + par[5] + V * GA * CY, [y, z], [x], lambda g, q: g.scalar.activation(x[0], y[0].indirect(z[0]), F.Identity, scale=0.5))
        ts(q, a, 1.0 / V, -0.4993, A.mult, A.add)
        tt(a, a, b, A.add)
        ts(b, q, -float(V), None, A.mult)
        tt(a, a, b, A.add)
        for tau in range(4, -1 if e == E - 1 else 0, -1):
            ts(R("lw", tau * 48, tau * 48 + 48), a, float((5 - tau) * V), None, A.min)

    nacc = [0]
    REC = [R("hl", j * V, (j + 1) * V) for j in range(K)]

    def bstep(e, t):
        head = [(HALF, "ls", 0)] + ([] if t in (0, 5) else [(NEG, lg, blk(e, t))])
        alt, one = ALT[e], TWOF
        hl = lambda t, a, b: R("xw", (t - 1) * V + a, (t - 1) * V + b) if e == E - 1 else R("hg", (t - 2) * V + a, (t - 2) * V + b)
        m0 = ((t - 2) % 4 if e == E - 1 else abs(t - 2)) * KV
        cnts["tag"] = "B%d%d" % (e, t)
        if t == 5:
            mm("psP", 0, V, head)
        else:
            if t and PCAP[e]:
                mm("psL", 0, V, [(ID, lg, blk(e, t))], True, False)
                act(R("psL", 0, V), hl(t + 1, 0, V), F.Identity, 0.5)
                mm("psL", 0, V, [(x, lg, blk(e, t)) for x in (BIG, NBIG, ID)], False, True)
            elif t:
                tt(R("cap"), R("psL", 0, V), R(lg, blk(e, t), blk(e, t) + V), A.max)
            else:
                act(R("hz0"), R(lg, blk(e, 0), blk(e, 0) + V), F.Identity, 2.0)
                act(R("psP", 0, V), hl(1, 0, V))
                tt(R("cap"), R("psP", 0, V), R("hz0"), A.max)
            k = bmsg[0]; bmsg[0] += 1
            w0 = max(t - 1, 0) * KV
            win = R("mlog", w0, 4 * KV + 264)
            jw = lambda a, n: R("jx", t * LX + a * 16, t * LX + (a + n) * 16)
            if WM[e] == "v":
                zw = R("zw", 0, 256)
                gat(zw, win, jw(0, 1), alt)
                gmul(zw, win, jw(1, 1), zw, A.add)
                gmul(zw, win, jw(2, 1), zw, A.add)
                mm("psP", V, H, [(SHB, "zw", 0)])
                mov(R("sb", 0, H), R("psP", V, V + H))
                out = R("zw", H, 256)
            else:
                if WM[e] == "p":
                    gat(R("zw"), win, jw(0, 3), alt)
                for a in range(3):
                    o = a * 256
                    c = 1 if WCUT[e] else 3
                    if WM[e] == "l" and a % c == 0:
                        gmul(R("zw", o, o + 256 * c), hl(t + 1, 0, (5 - t) * V + 8),
                             R("lw", t * 48 + a * 16, t * 48 + (a + c) * 16), R("wpw", o, o + 256 * c))
                    mm("psP", V, H, [(SHB, "zw", o)], a == 0, (WA[e] or OFF > 0) and a == 2)
                    if not WA[e]:
                        mm("psP", V + H, H, [(IDF, "zw", o + H)], OFF > 0 and a == 0, a == 2)
                    elif a:
                        tt(R("sb", H, 256), R("zw", o + H, o + 256), R("zw" if a == 1 else "sb", H, 256), A.add)
                c = H if WA[e] or OFF else 256
                mov(R("sb", 0, c), R("psP", V, V + c))
                if OFF and not WA[e]:
                    mov(R("sb", H, 256), R("psP", V + H, V + 256))
                out = R("sb", H, 256)
            a0, a1 = rland(k)
            send([out], a1, R("sb", 0, H), a0, list(rland(k + 1)))
            mm("psP", 0, V, head, True, False)
            for a in range(3):
                if a == 2 and RET[e] == "c":
                    gmul(R("mlog", w0 - 256, w0), win, jw(12, 1), R("ret", k % 2 * 264, k % 2 * 264 + 256), A.add)
                    win = R("mlog", w0 - 256, 4 * KV + 264)
                for x, y in (CH[::-1] if GCUT[e] else [(0, V)]):
                    gf = GF[e] + (GB[e] if x else 0)
                    zb, o = ("zw", 0) if a == 2 and gf == 0 else ("z", min(a, 2 - gf) * V)
                    zo, jo = R(zb, o + x, o + y), R("jx", t * LX + 48 + a * 48 + x // 16, t * LX + 48 + a * 48 + y // 16)
                    if a > 2 - gf:
                        gmul(zo, win, jo, zo, A.add)
                    else:
                        gat(zo, win, jo, alt, 0.5 if t and a == 0 else 0.0)
                    if a == 2 or a < 2 - gf:
                        mm("psP", x, y - x, [(one, zb, o + x)], False, a == 2 and RET[e] == "c")
            for x, y in (CH[::-1] if RET[e] == "g" else []):
                gat(R("hg", x, y), R("ret", k % 2 * 264, k % 2 * 264 + 264), R("inu", x // 16, y // 16), "sv")
                mm("psP", x, y - x, [(one, "hg", x)], False, True)
        fn, fo = ("f0", 0) if t == 0 else ("fa", slot[e, t] * V)
        for a, b in (CH[::-1] if CUT[e] else [(0, V)]):
            pc = 0 < t < 5 and PCAP[e]
            tt(R("cap" if pc else "psP", a, b), R("psP", a, b), R(fn, fo + a, fo + b), A.mult)
            h = hl(t, a, b) if t > 1 or t and e == E - 1 else hl(3, a, b) if t else R("cap", a, b)
            tt(h, R("psL" if pc else "psP", a, b), R(lg, blk(e, t) + a, blk(e, t) + b) if t == 5 else R("cap", a, b), A.min)
            if t == 0:
                dma("y", T.lam[:, a:b], T.cap[:, a:b], [R("cap", a, b)], [], 4 * (b - a))
                continue
            pl = "psW" if DEF and (e, t) == (E - 2, 1) else "psL"
            if PM[e] and (a or PM[e] > 1):
                i = mm(pl, a, b - a, [(HALFF, h[1][0][0], h[1][0][1])])
            else:
                i = mov(R(pl, a, b), h, 0.5, "s")
            if e == E - 1 and t == 5:
                cnts["fn"] = cnts["fn"] + [i]
            if not MCUT[e] or t == 1 and not M1:
                if a:
                    continue
                b = V
            for k in range(K):
                o = k * V
                i = tt(R("mlog", m0 + o + a, m0 + o + b), R(pl, a, b),
                       R("wx", slot[e, t] * KV + o + a, slot[e, t] * KV + o + b), A.mult)
                if t == 5 and e < E - 1 and k >= VF[1]:
                    ops[i]["after"].append(cnts["vote"][VF[0]])
        if t == 0:
            return
        s = slot[e, t]
        free.append(s)
        if e == E - 1 and t == 1:
            for j in (3, 2, 1, 0):
                p, ac = R(("psN", "psW")[j % 2], 0, V), R("acc", j * V, (j + 1) * V)
                mj = R("mlog", m0 + j * V, m0 + (j + 1) * V)
                if j < TP:
                    mm("psL", 0, V, [(IDF, "acc", j * V), (IDF, "mlog", m0 + j * V)])
                    tt(ac, R("psL", 0, V), REC[j], A.mult)
                else:
                    dma("g", ac[0], mj[0], [mj, ac], [ac], 3072, accum_op=A.add)
                    if j < 2:
                        mov(p, REC[j], 1.0, "s")
                    tt(ac, p, ac, A.mult)
                dma("y", T.gam[:, j * V:(j + 1) * V], ac[0], [ac], [], 3072)
        else:
            cnts["tag"] = "A%d%d" % (e, t)
            na = NA[e + (DEF and (e, t) == (E - 2, 1))]
            for a in range(0, KV, KV // na):
                x, y = R("acc", a, a + KV // na), R("mlog", m0 + a, m0 + a + KV // na)
                if nacc[0] == 0:
                    dma("y", x[0], y[0], [y], [x], 12288 // na)
                else:
                    dma("g", x[0], y[0], [x, y], [x], 12288 // na, accum_op=A.add, max_dma_last_dim=6144)
        nacc[0] += 1

    def inverse():
        cnts["tag"] = "R2"
        for fn in (F.Ln, F.Exp):
            last = cnts["fn"]
            for j in range(K):
                x, w, p = REC[j], R("wq", j * V, (j + 1) * V), R(("psN", "psW")[j % 2], 0, V)
                i = act(x, w, fn) if fn == F.Ln else act(p, x, fn, -1.0, math.log(4.0))
                ops[i]["after"] += last
                ops[i]["cost"] += 0.0 if j else 1.6
                cnts["fn"] = cnts["fn"] + [i]
                last = [i] + last
                if fn == F.Exp:
                    tt(x, p, w, A.mult)
                    act(x, x, F.Identity, -0.25, 2.0)
                    tt(x if j < 2 else p, p, x, A.mult)

    for t in range(1, 6):
        fstep(0, t)
    for e in range(E):
        if e < E - 1:
            votes(e)
        cnts["tag"] = "C%d" % e
        count(e)
        if e == E - 1:
            mset(R("xw", 5 * V, 5 * V + 8), 0.0)
        cnts["tag"] = "L%d" % e
        lists(e)
        if e < E - 1 and (e or not TL):
            tables(R("val", (2 * e + 1) * L, (2 * e + 2) * L), e + 1)
        for t in range(5, 0, -1):
            if e < E - 1:
                fstep(e + 1, 6 - t)
            bstep(e, t)
            if TL and (e, t) == (0, 1):
                tables(R("val", L, 2 * L), 1)
            if e == E - 1 and t == 5:
                inverse()
    bstep(E - 1, 0)
    return ops


KEPT = {}
AHEAD = 0.0
SEED, ROUNDS, MOVES, HEAT, HOP = 5, 300, 48000, 2e-4, 0.1


def order(ops, others=()):
    n = len(ops)
    deps = [set(o["after"]) for o in ops]
    raw = [set(o["after"]) for o in ops]
    hist = {}
    for i, o in enumerate(ops):
        for nm, a, b, x in o["rd"]:
            for j, c, d, w in hist.get(nm, ()):
                if w and c < b and a < d:
                    deps[i].add(j); raw[i].add(j)
        for nm, a, b, x in o["wr"] + o.get("guard", []):
            for j, c, d, w in hist.get(nm, ()):
                if c < b and a < d:
                    deps[i].add(j); raw[i].add(j)
        for nm, a, b, x in o["ex"]:
            for j, c, d, w in hist.get(nm, ()):
                if c < b and a < d:
                    deps[i].add(j)
        for nm, a, b, x in o["ex"]:
            hist[nm] = [h for h in hist.get(nm, []) if not (a <= h[1] and h[2] <= b)] + [(i, a, b, False)]
        for nm, a, b, x in o["wr"]:
            hist[nm] = [h for h in hist.get(nm, []) if not (a <= h[1] and h[2] <= b)] + [(i, a, b, True)]
        for nm, a, b, x in o["rd"]:
            if not x:
                hist.setdefault(nm, []).append((i, a, b, False))
        deps[i].discard(i); raw[i].discard(i)
    succ = [[] for _ in ops]
    for i in range(n):
        for j in deps[i]:
            succ[j].append(i)
    prio = [0.0] * n
    for i in range(n - 1, -1, -1):
        prio[i] = ops[i]["cost"] + ops[i]["lat"] + ops[i]["occ"] + HOP + max([prio[j] for j in succ[i]], default=0.0)
    qof = {"v": "v", "s": "s", "p": "p", "g": "g", "y": "y", "a": "s"}

    hop = lambda i, j: HOP if i in raw[j] and not ops[i]["engs"] == ops[j]["engs"] == "p" else 0.0
    fw = [[(j, hop(i, j)) for j in succ[i]] for i in range(n)]
    bw = [[(j, hop(j, i)) for j in sorted(deps[i])] for i in range(n)]

    engs, cost, lat, zero = [o["engs"] for o in ops], [o["cost"] for o in ops], [o["lat"] for o in ops], [0.0] * n
    occ = [o["occ"] for o in ops]
    both = [a + b for a, b in zip(lat, occ)]

    def place(key, back=False, look=0.5, margin=2.0, bias=0.3):
        nxt, pre, post = (bw, both, zero) if back else (fw, zero, lat)
        dma = 0.0
        left = [len(d) for d in (fw if back else bw)]
        at = [0.0] * n
        cand, free = {q: [] for q in "vspgy"}, {q: 0.0 for q in "vspgy"}
        eng, st, fin = [None] * n, [0.0] * n, [0.0] * n
        done = []

        def ready(j):
            at[j] += pre[j]
            for q in engs[j]:
                cand[qof[q]].append(j)
            if not engs[j]:
                eng[j], st[j], fin[j] = "-", at[j], at[j] + post[j]
                done.append(j)
        for i in range(n):
            if left[i] == 0:
                ready(i)
        while True:
            while done:
                i = done.pop()
                for j, h in nxt[i]:
                    left[j] -= 1
                    if at[j] < fin[i] + h:
                        at[j] = fin[i] + h
                    if left[j] == 0:
                        ready(j)
            bq, bt = None, 1e18
            for q, c in cand.items():
                if c:
                    t = max(min([at[i] for i in c]), free[q])
                    if t < bt:
                        bq, bt = q, t
            if bq is None:
                return eng, st, fin
            now = [i for i in cand[bq] if at[i] <= bt + 1e-9]
            i = max(now, key=lambda x: key[x])
            c = cost[i] + occ[i]
            soon = [j for j in cand[bq] if bt + 1e-9 < at[j] < bt + min(c, look * c + 0.15) and key[j] > key[i] + margin]
            if soon:
                j = max(soon, key=lambda x: key[x])
                fit = [x for x in now if bt + cost[x] <= at[j] + 0.05]
                i = max(fit, key=lambda x: key[x]) if fit else j
            if len(engs[i]) > 1 and bq == "v" and free["s"] <= max(bt, at[i]) + bias:
                if max([x for x in cand["s"] if at[x] <= max(free["s"], at[i]) + 1e-9], key=lambda x: key[x]) == i:
                    bq = "s"
            t0 = max(free[bq], at[i])
            for q in engs[i]:
                cand[qof[q]].remove(i)
            eng[i], st[i], fin[i] = (bq if bq in engs[i] else engs[i]), t0, t0 + cost[i] + post[i]
            free[bq] = t0 + cost[i]
            if occ[i] and not back:
                dma = max(dma, free[bq]) + occ[i]
                fin[i] = dma + lat[i]
            done.append(i)

    if "best" not in KEPT:
        rng = np.random.RandomState(SEED)
        tags = sorted(set(o["tag"] for o in ops))
        alts = [([o["cost"] for o in a], [o["lat"] for o in a]) for a in others]

        def score(c):
            tot = max(c[2]) * WEIGHTS[0]
            sq = sorted(range(n), key=lambda i: (c[1][i], i))
            for (cost, lat), w in zip(alts, WEIGHTS[1:]):
                busy, end = {}, [0.0] * n
                for i in sq:
                    t = 0.0
                    for j, h in bw[i]:
                        if end[j] + h > t:
                            t = end[j] + h
                    q = qof.get(c[0][i])
                    if q:
                        t = max(t, busy.get(q, 0.0)); busy[q] = t + cost[i]
                    end[i] = t + cost[i] + lat[i]
                    if occ[i]:
                        busy["d"] = max(busy.get("d", 0.0), t + cost[i]) + occ[i]
                        end[i] = busy["d"] + lat[i]
                tot += max(end) * w
            return tot
        best = cur = place([prio[i] + (AHEAD if ops[i]["tag"][0] in "FV" else 0.0) for i in range(n)])
        top = now = score(best)
        for it in range(ROUNDS):
            shift = {t: 0.0 for t in tags}
            for t in rng.randint(0, len(tags), 3):
                shift[tags[t]] = float(rng.normal(0, 3.0))
            noise = rng.normal(0, 0.3, n) * (it % 2)
            how = (0.0, 0.5, 1.0)[rng.randint(3)], (0.5, 2.0)[rng.randint(2)], (0.0, 0.3, 1.0)[rng.randint(3)]
            r = place([cur[2][i] + shift[ops[i]["tag"]] + float(noise[i]) for i in range(n)], True, *how)
            c = place(r[2], False, *how)
            if max(c[2]) <= max(cur[2]) * 1.02:
                v = score(c)
                if v <= now + 0.01 * (1 - it / ROUNDS):
                    cur, now = c, v
                if v <= top:
                    best, top = c, v
        seq = sorted(range(n), key=lambda i: (best[1][i], i))
        KEPT["best"] = polish([ops] + list(others), deps, raw, seq, best[0])
    seq, eng, fin = KEPT["best"]
    return seq, eng, deps, raw, fin


def polish(plans, deps, raw, seq, eng):
    ops = plans[0]
    n, m = len(ops), len(plans)
    num = {"v": 0, "s": 1, "p": 2, "g": 3, "y": 4, "a": 1, "-": -1}
    anc, pre = [0] * n, []
    for i in range(n):
        a, keep = 0, []
        for j in sorted(deps[i], reverse=True):
            if not a >> j & 1:
                keep.append(j)
            a |= anc[j]
        for j in deps[i]:
            a |= 1 << j
        anc[i] = a
        pre.append([(j, HOP if j in raw[i] and not ops[i]["engs"] == ops[j]["engs"] == "p" else 0.0) for j in keep])
    occ = [o["occ"] for o in ops]
    costs, lats = [[o["cost"] for o in a] for a in plans], [[o["lat"] for o in a] for a in plans]
    eng = list(eng)
    q = [num[e] for e in eng]

    def run(seq, p0, old, k0=0, room=1e9):
        tot, out = 0.0, [None] * m
        for k in [k0] + [k for k in range(m) if k != k0]:
            end, rel, dm, cs, lt = old[k][0][:], old[k][1][:], old[k][2][:], costs[k], lats[k]
            busy, seen, d, p = [0.0] * 5, 0, 0.0, p0 - 1
            while p >= 0 and seen != 63:
                i = seq[p]
                x = q[i]
                if x >= 0 and not seen >> x & 1:
                    busy[x] = rel[i]; seen |= 1 << x
                if occ[i] and not seen & 32:
                    d = dm[i]; seen |= 32
                p -= 1
            for i in seq[p0:]:
                t = 0.0
                for j, h in pre[i]:
                    u = end[j] + h
                    if u > t:
                        t = u
                x = q[i]
                if x >= 0:
                    if busy[x] > t:
                        t = busy[x]
                    t += cs[i]; busy[x] = t; rel[i] = t
                    if occ[i]:
                        d = (d if d > t else t) + occ[i]; t = d; dm[i] = d
                end[i] = t + lt[i]
            t = max(end)
            if k == k0 and (t - old[k][3]) * WEIGHTS[k] > room:
                return 1e9, None
            tot += t * WEIGHTS[k]
            out[k] = (end, rel, dm, t)
        return tot, out

    def chain(seq, end, rel, dm):
        prev, last, dprev, dl = [None] * n, [None] * 5, [None] * n, None
        for i in seq:
            if q[i] >= 0:
                prev[i] = last[q[i]]; last[q[i]] = i
                if occ[i]:
                    dprev[i] = dl; dl = i
        i, arcs, either, queued = end.index(max(end)), [], [], False
        while i is not None:
            if len(ops[i]["engs"]) > 1:
                either.append(i)
            if occ[i] and not queued and dprev[i] is not None and dm[dprev[i]] > rel[i] + 1e-9:
                arcs.append((dprev[i], i)); i = dprev[i]
                continue
            b, t = None, 0.0
            for j, h in pre[i]:
                if end[j] + h > t:
                    b, t = j, end[j] + h
            queued = prev[i] is not None and rel[prev[i]] > t - 1e-9
            if queued:
                arcs.append((prev[i], i)); b = prev[i]
            i = b
        return arcs, either, prev

    rng = np.random.RandomState(SEED)
    now, state = run(seq, 0, [([0.0] * n,) * 3 + (0.0,)] * m)
    best, arcs = (now, seq, eng[:], state[0][0]), None
    for it in range(MOVES):
        if arcs is None:
            k0 = rng.randint(m)
            arcs, either, prev = chain(seq, *state[k0][:3])
            pos = [0] * n
            for p, i in enumerate(seq):
                pos[i] = p
        r, flip = rng.rand(), None
        if r < 0.08 and either:
            flip = either[rng.randint(len(either))]
            eng[flip] = "s" if eng[flip] == "v" else "v"
            q[flip] = num[eng[flip]]
            new, p0 = seq, pos[flip]
        else:
            a = rng.randint(len(arcs))
            i, j = arcs[a]
            for _ in range(rng.geometric((0.7, 0.2)[it % 2]) - 1):
                if r < 0.55 and prev[i] is not None and not anc[j] >> prev[i] & 1:
                    i = prev[i]
                if r >= 0.55 and a > 0 and arcs[a - 1][0] == j and not anc[arcs[a - 1][1]] >> i & 1:
                    a -= 1; j = arcs[a][1]
            if anc[j] >> i & 1:
                continue
            p0, p1 = pos[i], pos[j]
            if r < 0.55:
                mid, b = seq[p0:p1], anc[j]
                new = seq[:p0] + [x for x in mid if b >> x & 1] + [j] + [x for x in mid if not b >> x & 1] + seq[p1 + 1:]
            else:
                mid = seq[p0 + 1:p1 + 1]
                new = seq[:p0] + [x for x in mid if not anc[x] >> i & 1] + [i] + [x for x in mid if anc[x] >> i & 1] + seq[p1 + 1:]
        room = -math.log(1e-12 + rng.rand()) * (HEAT * (1 - it / MOVES) ** 2 + 1e-7)
        v, st = run(new, p0, state, k0, room)
        if v <= now + room:
            now, state, seq, arcs = v, st, new, None
            if v < best[0]:
                best = (v, seq, eng[:], st[0][0])
        elif flip is not None:
            eng[flip] = "s" if eng[flip] == "v" else "v"
            q[flip] = num[eng[flip]]
    return best[1:]


def rank_program(g, core, T, topo):
    if T.rank_of(core) is None:
        return
    ops = plan(T, topo, core)
    seq, eng, deps, raw, fin = order(ops, [plan(T, topo, core, p) for p in PARS[1:]])
    queue = {"v": g.vector, "s": g.scalar, "p": g.tensor, "g": g, "y": g.sync, "a": g.scalar}
    same = {"v": "v", "s": "s", "p": "p", "g": "g", "y": "y", "a": "s"}
    csem = {"v": "cv", "s": "cs", "p": "cp", "g": "cg"}
    known = {q: {} for q in "vspgy"}
    count = {q: 0 for q in csem}
    token, clock, total = {}, {}, {}
    for i in seq:
        o, q = ops[i], eng[i]
        if o["kind"] == "a":
            token[i] = o["sem"]; clock[i] = {}; total[o["sem"][0]] = o["sem"][1]
            continue
        kn = known[same[q]]
        need = {}
        for j in deps[i]:
            if ops[j]["kind"] == "c" and eng[j] == q and o["kind"] == "c" and (q == "p" or j not in raw[i]):
                continue
            s, v = token[j]
            if v > need.get(s, (0, None))[0]:
                need[s] = (v, j)
        for s, (v, j) in sorted(need.items(), key=lambda x: -fin[x[1][1]]):
            if kn.get(s, 0) < v:
                queue[q].wait_ge(T.sem[s], v)
                kn[s] = v
                for s2, v2 in clock[j].items():
                    if kn.get(s2, 0) < v2:
                        kn[s2] = v2
        clock[i] = dict(kn)
        ins = o["emit"](g, q)
        if o["kind"] == "c":
            count[q] += 1
            ins.then_inc(T.sem[csem[q]], 1)
            token[i] = (csem[q], count[q])
        elif o["kind"] == "d":
            ins.then_inc(T.sem[o["sem"]], 16)
            token[i] = (o["sem"], 16)
        else:
            token[i] = o["sem"]
        total[token[i][0]] = token[i][1]
    for s, v in total.items():
        if known["g"].get(s, 0) < v:
            g.wait_ge(T.sem[s], v)
